import numpy as np, ml_dtypes
CORES = [1,5,17,21,33,37,49,53]
N = 8
BF = ml_dtypes.bfloat16
def gentries(a):
    return np.ascontiguousarray(a.reshape(8, 16, -1).transpose(0, 2, 1)).reshape(8, -1)
def gtable(e):
    e = np.asarray(e); return np.ascontiguousarray(e.reshape(8, -1, 16).transpose(0, 2, 1)).reshape(128, -1).astype(np.int32)
P, BS, T, CAP, G = 4352, 768, 3, 256, 96
S, SB, NEED, KILL = 4, 2, 10, 1
W = P + (N - 1) * G
def clans(rng, kk):
    sc = rng.choice(np.array([191.0, 120.0, 60.0], np.float32), (8, 1, 1)); cen = (sc * rng.random((8, 16, 4))).astype(np.float32); cen[:, :, 0] *= np.float32(0.1)
    t = np.maximum(1, (sc * (0.06 + 0.08 * rng.random((N, 8, 16, 1)))).astype(np.int32)); off = rng.integers(0, 4, (8, 1))
    def near():
        who = ((rng.random((N, 8, P)) * kk[:, None]).astype(np.int64) + off) & 3
        w = sc * (np.float32(0.05) + np.float32(0.15) * rng.random((N, 8, 1, P), dtype=np.float32))
        v = np.take_along_axis(np.broadcast_to(cen, (N, 8, 16, 4)), who[:, :, None, :], 3) + w * (2 * rng.random((N, 8, 16, P), dtype=np.float32) - 1)
        return np.clip(np.rint(v), 0, 191).astype(np.int32)
    x = near(); share = KILL * kk[:, None, None] * rng.choice(np.array([0.03, 0.06, 0.09]), (N, 8, 1, 1))
    y = np.where(rng.random((N, 8, 1, P)) < 0.1, 255, rng.integers(0, 192, (N, 8, 16, P), dtype=np.int32))
    return x, np.where(rng.random((N, 8, 1, P)) < share, near(), y), t
def chosen(key):
    return np.ascontiguousarray(np.argsort(key, axis=-1)[..., :16 * BS])
def deal(pts, num):
    a = np.empty((16, BS), np.int64); a[:, pts] = num.reshape(BS, 16).T
    return a.reshape(-1)
def parts(rng):
    x, y, t = clans(rng, rng.permutation(np.array([1, 1, 2, 2, 2, 3, 3, 4])))
    sd = rng.random((N, 8, BS)) < rng.choice(np.array([0.2, 0.4, 0.6, 0.9]), (N, 8, 1))
    c = chosen(rng.random((N, 8, T, S * W), dtype=np.float32))
    b = np.argsort(rng.random((N, 8, P)) * np.where(np.arange(P) < T * BS, 0.6, 1.0), axis=-1)[..., :(N - 1) * G]
    return x, y, t, sd, c, np.ascontiguousarray(b)
def pack(x, y, t, sd, c, b):
    c = c.reshape(N, 8, T, 16, BS).transpose(0, 1, 3, 2, 4).reshape(N, 128, T * BS)
    return {"x": x.reshape(N, 128, P).astype(np.float32).astype(BF), "y0": y.reshape(N, 128, P).astype(np.float32).astype(BF),
            "tl": t.reshape(N, 128, 1).astype(np.float32).astype(BF), "sd": sd.astype(np.float32).astype(BF),
            "cd": np.ascontiguousarray(c).astype(np.int32), "snd": np.stack([gtable(a) for a in b])}
def setup_inputs(rng):
    return pack(*parts(rng))
def setup_inputs_room(rng):
    x, y, t, sd, c, b = parts(rng)
    o = np.argsort(np.argsort(rng.random((N, 8, BS)), axis=-1), axis=-1); n = rng.choice(np.array([0, 1, CAP - 1, CAP, CAP + 1, BS]), (N, 8))
    n[0] = (CAP, CAP + 1, BS, CAP - 1, 1, 0, CAP, BS); n[1] = (BS, CAP, CAP + 1, CAP, CAP - 1, CAP, 0, 1)
    return pack(x, y, t, o < n[..., None], c, b)
def setup_inputs_ties(rng):
    x, y, t, sd, c, b = parts(rng)
    t = np.tile(rng.integers(0, 21, (1, 8, 16, 1)), (N, 1, 1, 1)); base = rng.integers(10, 121, (8, 16, 1))
    def step():
        return base + t * rng.integers(0, 3, (N, 8, 16, P), dtype=np.int32) + (rng.random((N, 8, 16, P), dtype=np.float32) < 0.3)
    x = step(); y = np.where(rng.random((N, 8, 1, P)) < 0.1 * KILL, step(), 255)
    t[:, 0] = 63; x[:, 0] = rng.choice(np.array([127, 128, 191]), (N, 16, P)); y[:, 0] = rng.choice(np.array([255, 255, 255, 191, 128, 64]), (N, 16, P))
    return pack(x, y, t, sd, c, b)
def setup_inputs_ends(rng):
    x, y, t, sd, c, b = parts(rng); a = np.arange(S * W); n = np.arange(BS); k = np.arange((N - 1) * G)
    key = rng.random((N, 8, T, S * W), dtype=np.float32)
    key[:, 1::2, :, S * P:] -= 1; key[:, 1::2, :, :S] -= 1; key[:, 1::2, :, S * (P - 1):S * P] -= 1
    key[:, 2] += (a >= 16 * BS).astype(np.float32); key[:, 4] += (a < S * W - 16 * BS).astype(np.float32)
    c = rng.permuted(chosen(key), axis=-1); c[:, 6] = np.arange(16 * BS)
    b[:, 1] = k; b[:, 3] = P - 1 - k; b[:, 7] = T * BS - (N - 1) * G + k
    sd[:, ::2] = n >= BS - CAP; sd[:, 1::2] = (n & 1) == 0; sd[:, 5] = (n == 0) | (n == BS - 1)
    return pack(x, y, t, sd, c, b)
def setup_inputs_dark(rng):
    x, y, t, sd, c, b = parts(rng); q = rng.permutation(N); g = rng.permutation(8)
    y[:, g[1]] = 255; t[:, g[2]] = 0
    for j in g[3:7]:
        x[:, j] = x[:, j] & 31; t[:, j] = 63
    y[:, g[3]] = y[:, g[3]] & 31; y[:, g[4]] = 128 + (y[:, g[4]] & 63)
    for r in range(N):
        m = np.isin(np.arange(BS) & 15, rng.permutation(16)[:16 * CAP // BS]); sd[r, g[4]] = m
        num = np.concatenate([rng.permutation(np.arange(S * P, S * W)), np.arange(16 * BS - S * (W - P))])
        c[r, g[4], 0] = deal(np.argsort(rng.random(BS) - m), num)
        m = rng.permutation(BS) < CAP; sd[r, g[5]] = m; o = rng.permutation(16)
        pl = np.argsort(o[np.arange(W) & 15] + rng.random(W))[:16 * CAP]; num = rng.permutation(S * pl + rng.integers(0, S, 16 * CAP))
        num = np.concatenate([num, rng.permutation(np.setdiff1d(np.arange(S * W), num))])[:16 * BS]
        c[r, g[5], 0] = deal(np.argsort(rng.random(BS) - m), num)
    c[:, g[4], 1:] = rng.permuted(np.tile(np.arange(16 * BS), (N, T - 1, 1)), axis=-1)
    key = rng.random((N, S * W)); key[:, S * BS:2 * S * BS] += 1; c[:, g[6], 0] = chosen(key)
    b[:, g[6]] = np.argsort(rng.random((N, P)) + (np.arange(P) // BS == 1), axis=-1)[:, :(N - 1) * G]
    sd[:, g[0]] = False; sd[q[0]] = False; sd[q[1], g[3]] = True
    return pack(x, y, t, sd, c, b)
def setup_inputs_spread(rng):
    x, y, t, sd, c, b = parts(rng)
    x = np.minimum((np.exp2(7.59 * rng.random((N, 8, 1, P))) * rng.random((N, 8, 16, P))).astype(np.int32), 191)
    y = np.minimum((np.exp2(7.59 * rng.random((N, 8, 1, P))) * rng.random((N, 8, 16, P))).astype(np.int32), 191)
    y = np.where(rng.random((N, 8, 1, P)) < rng.choice(np.array([0.1, 0.5, 0.9]), (N, 8, 1, 1)), 255, y)
    low = np.arange(16)[:, None] == rng.integers(0, 16, (N, 8, 1, P))
    y = np.where(rng.random((N, 8, 1, P)) < 0.15, np.where(low, y >> 3, 255), y)
    t = np.rint(np.exp2(6 * rng.random((N, 8, 16, 1)))).astype(np.int32) - 1
    return pack(x, y, np.minimum(t, 63), rng.random((N, 8, BS)) < rng.random((N, 8, 1)), c, b)
def check_inputs(d):
    bad = []
    for k, hi in (("x", 191), ("y0", 191), ("tl", 63), ("sd", 1)):
        v = np.asarray(d[k]).astype(np.float32); ok = (v >= 0) & (v <= hi) & (v == np.floor(v))
        if k == "y0": ok = ok | (v == 255)
        if not np.all(ok): bad.append("range of " + k)
    for k, hi in (("cd", S * W - 1), ("snd", P - 1)):
        if np.min(d[k]) < 0 or np.max(d[k]) > hi: bad.append("range of " + k)
    c = np.sort(np.asarray(d["cd"]).reshape(N, 8, 16, T, BS).transpose(0, 1, 3, 2, 4).reshape(N, 8, T, 16 * BS), axis=-1)
    if np.any(c[..., 1:] == c[..., :-1]): bad.append("equal numbers in a brood of cd")
    s = np.sort(np.stack([gentries(a) for a in d["snd"]]), axis=-1)
    if np.any(s[..., 1:] == s[..., :-1]): bad.append("equal numbers in snd")
    return bad
def windows(a, sl):
    res = []
    for r in range(N):
        w = [a[r]]
        for d in range(1, N):
            q = (r - d) % N; w.append(np.take_along_axis(a[q], sl[q, :, d - 1][:, None, :], 2))
        res.append(np.concatenate(w, axis=2))
    return np.stack(res)
def matches(come, xn, t):
    return np.add.reduce((np.abs(come - xn[:, None, :]) <= t[:, :, None]).astype(np.int64), axis=0) >= NEED
def reference(x, y0, tl, sd, cd, snd):
    X = x.astype(np.float32).astype(np.int32).reshape(N, 8, 16, P); Y = y0.astype(np.float32).astype(np.int32).reshape(N, 8, 16, P)
    t = tl.astype(np.float32).astype(np.int32).reshape(N, 8, 16, 1)
    C = (cd.astype(np.int64) >> SB).reshape(N, 8, 16, T * BS); sl = np.stack([gentries(a) for a in snd]).astype(np.int64).reshape(N, 8, N - 1, G)
    flag = np.zeros((N, 8, P), bool); flag[:, :, :BS] = sd.astype(np.float32) > 0.5; member = np.zeros((N, 8, P), bool)
    xw = windows(X, sl)
    for s in range(T):
        fl = flag[:, :, s * BS:(s + 1) * BS]
        member[:, :, s * BS:(s + 1) * BS] = fl & (np.add.accumulate(fl.astype(np.int64), axis=2) <= CAP)
        new = np.zeros((N, 8, W), bool)
        for r in range(N):
            for g in range(8):
                n = np.flatnonzero(member[r, g, s * BS:(s + 1) * BS]) + s * BS; c = C[r, g][:, n]
                come = xw[r, g][:, c.reshape(-1)].reshape(16, 16, len(n))
                new[r, g][c[matches(come, X[r, g][:, n], t[r, g])]] = True
        for r in range(N):
            flag[r] |= new[r, :, :P]
            for d in range(1, N):
                q = (r - d) % N
                for g in range(8): flag[q, g, sl[q, g, d - 1][new[r, g, P + (d - 1) * G:P + d * G]]] = True
    for s in range(T - 1, -1, -1):
        yw = windows(Y, sl); Z = Y.copy()
        for r in range(N):
            for g in range(8):
                n = np.flatnonzero(member[r, g, s * BS:(s + 1) * BS]) + s * BS; c = C[r, g][:, n]; xn = X[r, g][:, n]
                come = yw[r, g][:, c.reshape(-1)].reshape(16, 16, len(n))
                dead = np.add.reduce(matches(come, xn, t[r, g]).astype(np.int64), axis=0) >= KILL
                Z[r, g][:, n] = np.where(dead, 255, (xn + np.minimum(191, np.minimum.reduce(come, axis=1))) >> 1)
        Y = Z
    return {"yv": np.ascontiguousarray(Y[:, :, :, :T * BS]).reshape(N, 128, T * BS).astype(np.float32).astype(BF), "yf": np.where(member, 2, flag.astype(np.int64)).astype(np.float32).astype(BF)}

@@ -1,0 +1,516 @@
+from concourse.bass import DstId, RemoteDMATransfer
+from concourse.mybir import AluOpType, ActivationFunctionType
+
+P, BS, GB, NR = 4352, 768, 96, 8
+NB = 7 * GB
+W = P + NB
+WX = W + 128
+VW = 4 * W + 512
+C = 512
+NC = 8
+
+
+def _sb(n, d):
+    return ("sbuf", [128, n], d)
+
+
+_BF = {"xw": WX, "yA": WX, "yB": WX, "wA": VW, "wB": VW, "E": 2048, "L": 2048, "I": 128, "BO": 128, "NU": 128, "ga": 4096, "mn": 4096,
+       "sm": C, "sx": C, "row": P, "tlb": 1, "g2": 1024, "cwin": 1024, "sf0": NB, "sf1": NB, "sb": NB, "gb": BS, "rbq": 272, "sdq": 272,
+       "mq": 272, "yfo": 272, "yft": 272, "F2a": 48, "z48": 48, "F": 48, "cs": 48, "dd": 128}
+_F32 = {"L32": 2048, "inv": P, "NF": 48, "A": 48, "q1": 48, "q2": 48, "q3": 48, "N769": 48, "N257": 48, "N256": 48, "pf15": 8, "pf15k": 8}
+_I32 = {"pk": 3 * BS, "pkw": 1544, "dum": 256, "ta": 256, "tb": 256, "sndi": 42, "pi": 8, "pj": 8, "s32": 128, "h32": 128}
+_U16 = {"invT": 96, "sndu": 48, "P16": 48}
+for _s in range(3):
+    _BF.update({"zc%d" % _s: 1024, "xm%d" % _s: 256, "nx%d" % _s: 256, "tq%d" % _s: 1088, "fr%d" % _s: 688, "ab%d" % _s: C, "id%d" % _s: C, "mt%d" % _s: C})
+    _F32.update({"P32_%d" % _s: 48})
+    _U16.update({"vu%d" % _s: 256, "cu%d" % _s: 256, "yp%d" % _s: 48})
+SCRATCH = {}
+for _t, _d in ((_BF, "bfloat16"), (_F32, "float32"), (_I32, "int32"), (_U16, "uint16")):
+    SCRATCH.update({_n: _sb(_c, _d) for _n, _c in _t.items()})
+PSUMS = ["ps0", "ps1", "ps2", "pc0", "pc1", "pr0", "pr1", "pf"]
+for _n in PSUMS:
+    SCRATCH[_n] = ("psum", [128, 512], "float32")
+NDMA = 30
+EXCH = ["x", "f0", "f1", "f2", "y0", "y1", "y2"]
+SEMAPHORES = ["sv", "sa", "st", "sg"] + ["d%d" % k for k in range(NDMA)] + ["r_" + e for e in EXCH] + ["l_" + e for e in EXCH]
+EG_OUT = "ssvsssss"
+EG_OUT2 = "ssssssss"
+EG_BACK2 = "sssssvss"
+EG_BACK = "vsssssss"
+SPLIT = 4
+ZB, ZV, ZS = 8000, 9000, 6000
+
+
+def exchange_plan(topo, cores, r, sg):
+    src = cores[r]
+    dst = [None] + [cores[(r + sg * d) % NR] for d in range(1, NR)]
+    off = [d for d in range(1, NR) if topo.chip(dst[d]) != topo.chip(src)]
+    on = [d for d in range(1, NR) if d not in off]
+    eng = topo.engines(src, dst[off[0]])
+    n = len(eng)
+    first, second = off[:4], off[4:]
+    calls = [[(d, eng[i * n // 4:(i + 1) * n // 4]) for i, d in enumerate(first)],
+             [(d, eng[i * n // 2:(i + 1) * n // 2]) for i, d in enumerate(second)]]
+    for d in on:
+        free = [e for e in topo.engines(src, dst[d]) if e not in eng]
+        calls[0 if d < second[0] else 1].append((d, free[:8]))
+    return calls
+
+
+def rank_program(g, core, T, topo):
+    rank = T.rank_of(core)
+    if rank is None:
+        return
+    OP, AF = AluOpType, ActivationFunctionType
+    cores = list(T.cores)
+    eng = {"g": g, "vector": g.vector, "scalar": g.scalar, "tensor": g.tensor, "sync": g.sync}
+    csem = {"vector": "sv", "scalar": "sa", "tensor": "st", "g": "sg"}
+    count, totals, recs, ndma, seq = {}, {}, {}, [0], [0]
+    known = {q: {} for q in eng}
+
+    def B(name, lo=None, hi=None, st=1, parts=None):
+        lo = 0 if lo is None else lo
+        hi = SCRATCH[name][1][1] if hi is None else hi
+        ap = T[name][:, lo:hi:st] if parts is None else T[name][parts, lo:hi:st]
+        return {"ap": ap, "r": [(name, lo, hi)], "x": []}
+
+    def IND(win, off):
+        return {"ap": win["ap"].indirect(off["ap"]), "r": win["r"], "x": off["r"]}
+
+    def HB(ap):
+        return {"ap": ap, "r": [], "x": []}
+
+    def need_of(q, reads, writes):
+        need = []
+        for acc, w in [(a, False) for a in reads] + [(a, True) for a in writes]:
+            name, lo, hi = acc
+            psum = name in PSUMS
+            for rec in recs.get(name, []):
+                if (rec["hi"] <= lo or rec["lo"] >= hi) and not psum:
+                    continue
+                if rec["q"] == q and q == "tensor":
+                    continue
+                if w or rec["w"] or (psum and rec["q"] != q):
+                    need.append(rec["tok"])
+        return need
+
+    def do_waits(q, need):
+        K = known[q]
+        best = {}
+        for tok in need:
+            s = tok["sem"]
+            if K.get(s, 0) < tok["val"] and (s not in best or best[s]["val"] < tok["val"]):
+                best[s] = tok
+        for s in sorted(best):
+            if any(o != s and best[o]["clk"].get(s, 0) >= best[s]["val"] for o in best):
+                del best[s]
+        for s in sorted(best):
+            eng[q].wait_ge(T.sem[s], best[s]["val"])
+            for a, b in best[s]["clk"].items():
+                K[a] = max(K.get(a, 0), b)
+
+    def record(q, tok, reads, writes):
+        for name, lo, hi in writes:
+            keep = [x for x in recs.get(name, []) if not (name in PSUMS or (x["lo"] >= lo and x["hi"] <= hi))]
+            recs[name] = keep + [{"lo": lo, "hi": hi, "w": True, "tok": tok, "q": q}]
+        for name, lo, hi in reads:
+            recs.setdefault(name, []).append({"lo": lo, "hi": hi, "w": False, "tok": tok, "q": q})
+
+    def op(q, fn, outs, ins):
+        reads = [a for o in ins for a in o["r"] + o["x"]] + [a for o in outs for a in o["x"]]
+        writes = [a for o in outs for a in o["r"]]
+        do_waits(q, need_of(q, reads, writes))
+        s = csem[q]
+        count[s] = count.get(s, 0) + 1
+        fn(eng[q]).then_inc(T.sem[s], 1)
+        clk = dict(known[q])
+        clk[s] = count[s]
+        record(q, {"sem": s, "val": count[s], "clk": clk}, reads, writes)
+
+    def dma(q, out, in_, after=()):
+        do_waits(q, need_of("dma", in_["r"], out["r"]) + list(after))
+        s = "d%d" % ndma[0]
+        ndma[0] += 1
+        eng[q].dma_start(out["ap"], in_["ap"]).then_inc(T.sem[s], 16)
+        clk = dict(known[q])
+        clk[s] = totals[s] = 16
+        record("dma", {"sem": s, "val": 16, "clk": clk}, in_["r"], out["r"])
+
+    def send(name, src, land, at, sg=1):
+        ls, rs = "l_" + name, "r_" + name
+        done, pend, clk = 0, [], {}
+        for call in exchange_plan(topo, cores, rank, sg):
+            tr, reads = [], []
+            for d, es in call:
+                to = cores[(rank + sg * d) % NR]
+                rid, pid = topo.addr(to)[:2]
+                lo = (d - 1) * GB
+                reads.append((src, lo, lo + GB))
+                tr.append(RemoteDMATransfer(dst_ids=[DstId(rid=rid, pnc=pid)], dma_engine_mask=sum(1 << e for e in es), remote_sem=T.sem[rs],
+                                            src=T[src][:, lo:lo + GB], dst=T[land][:, at + lo:at + lo + GB]))
+                done += len(es)
+            do_waits("g", need_of("g", reads, []))
+            g.remote_dma_fused(tr, local_sem=T.sem[ls])
+            pend += reads
+            clk = dict(known["g"])
+        clk[ls] = totals[ls] = done
+        record("g", {"sem": ls, "val": done, "clk": clk}, pend, [])
+        n = sum(len(es) for q in range(NR) if q != rank for call in exchange_plan(topo, cores, q, sg) for d, es in call if (q + sg * d) % NR == rank)
+        totals[rs] = n
+        rt = {"sem": rs, "val": n, "clk": {rs: n}}
+        recs[land] = [x for x in recs.get(land, []) if not (x["lo"] >= at and x["hi"] <= at + NB)] + [{"lo": at, "hi": at + NB, "w": True, "tok": rt, "q": "ext"}]
+        return rt
+
+    def copy(out, in_): op("vector", lambda e: e.tensor_copy(out["ap"], in_["ap"]), [out], [in_])
+    def tt(out, a, b, o): op("vector", lambda e: e.tensor_tensor(out["ap"], a["ap"], b["ap"], o), [out], [a, b])
+    def fill(out, v): op("vector", lambda e: e.memset(out["ap"], v), [out], [])
+
+    def ts(out, a, s1, o1, s2=None, o2=None):
+        col = isinstance(s1, dict)
+        v1 = s1["ap"] if col else s1
+        ins = [a, s1] if col else [a]
+        if o2 is None:
+            op("vector", lambda e: e.tensor_scalar(out["ap"], a["ap"], v1, None, o1), [out], ins)
+        else:
+            op("vector", lambda e: e.tensor_scalar(out["ap"], a["ap"], v1, s2, o1, o2), [out], ins)
+
+    def scan(out, d0, d1, o0, o1):
+        op("vector", lambda e: e.tensor_tensor_scan(out["ap"], d0["ap"], d1["ap"], 0.0, o0, o1), [out], [d0, d1])
+
+    def act(out, in_, f, **kw): op("scalar", lambda e: e.activation(out["ap"], in_["ap"], f, **kw), [out], [in_])
+
+    def take(q, out, win, off):
+        if q == "v":
+            copy(out, IND(win, off))
+        else:
+            act(out, IND(win, off), AF.Copy)
+
+    def pe(mms):
+        def run_all(e):
+            for o, l, r, a, b in mms:
+                k = e.matmul(o["ap"], l["ap"], r["ap"], a, b)
+            return k
+        outs, ins = {}, {}
+        for o, l, r, a, b in mms:
+            outs[o["r"][0]] = o
+            ins[l["r"][0]] = l
+            ins[r["r"][0]] = r
+        op("tensor", run_all, list(outs.values()), list(ins.values()))
+
+    def chain(out, pairs, first=True, last=True):
+        n = len(pairs)
+        return [(out, l, r, first and i == 0, last and i == n - 1) for i, (l, r) in enumerate(pairs)]
+
+    def Lm(a, nm="L"):
+        return B(nm, 128 * a, 128 * a + 128)
+
+    def gsel(o, pat, cmp, base, cm, i=None):
+        i = o if i is None else i
+        op("g", lambda e: e.affine_select(o["ap"], i["ap"], pat, cmp, 0.0, base, cm), [o], [i])
+
+    def giota(o, pat, base, cm):
+        op("g", lambda e: e.iota(o["ap"], pat, base, cm, allow_small_or_imprecise_dtypes=True), [o], [])
+
+    def zero(win, lo, nv, ns, ng):
+        for q, n in (("v", nv), ("s", ns), ("g", ng)):
+            end = lo + n
+            while lo < end:
+                m = end - lo if q == "v" else min(2048, end - lo)
+                o = B(win, lo, lo + m)
+                if q == "v":
+                    fill(o, 0.0)
+                elif q == "s":
+                    act(o, B("E", 0, m), AF.Copy, scale=0.0)
+                else:
+                    giota(o, [[0, m]], 0, 0)
+                lo += m
+
+    def pack(s):
+        o = B("pk", s * BS, s * BS + BS)
+        ts(o, o, 256.0, OP.mult)
+        tt(o, o, B("xw", s * BS, s * BS + BS), OP.add)
+
+    def members(s):
+        pf = B("pf", 0, 48)
+        ts(B("F"), pf, 0.5, OP.is_gt)
+        scan(B("cs"), B("z48"), B("F"), OP.add, OP.add)
+        ts(B("NF"), pf, 0.5, OP.is_le)
+        pe(chain(B("pc0", 0, 48), [(B("BO"), B("cs")), (B("NU"), B("F"))]))
+        tt(B("A"), B("NF"), B("N769"), OP.mult)
+        tt(B("P32_%d" % s), B("pc0", 0, 48), B("A"), OP.max)
+        copy(B("P16"), B("P32_%d" % s))
+        copy(IND(B("pkw"), B("P16")), B("pk", s * BS, s * BS + BS))
+        half_list(s, 0)
+        ts(B("tb"), B("pkw", 1, 257), 255, OP.bitwise_and)
+        copy(B("xm%d" % s), B("tb"))
+        pe([(B("pr0", 128 * h, 128 * h + 128), B("xm%d" % s, 128 * h, 128 * h + 128), B("I"), True, True) for h in range(2)])
+
+    def half_list(s, lo):
+        ts(B("ta", lo, lo + 128), B("pkw", 1 + lo, 129 + lo), 10, OP.arith_shift_right)
+        copy(B("cu%d" % s, lo, lo + 128), B("ta", lo, lo + 128))
+
+    def members2(s):
+        ts(B("nx%d" % s), B("pr0", 0, 256), -1.0, OP.mult)
+        half_list(s, 128)
+
+    def numbers(s):
+        ts(B("ta"), B("pkw", 1, 257), 8, OP.arith_shift_right)
+        copy(B("vu%d" % s), B("ta"))
+        if s < 2:
+            copy(B("pkw", 1, 257), B("dum"))
+
+    def places(s):
+        p = B("P32_%d" % s)
+        ts(B("q1"), p, 256.5, OP.is_lt)
+        tt(B("q2"), p, B("N257"), OP.subtract)
+        tt(B("q3"), B("q2"), B("q1"), OP.mult)
+        tt(B("q2"), B("q3"), B("N256"), OP.add)
+        copy(B("yp%d" % s), B("q2"))
+
+    def chunks(kind, s, win, ks, eg):
+        res = []
+        for k in ks:
+            i = seq[0]
+            seq[0] += 1
+            ga = B("g2", C * (i % 2), C * (i % 2) + C) if kind == "o" and s == 2 else B("ga", C * k, C * k + C)
+            res.append({"kind": kind, "s": s, "k": k, "i": i, "win": win, "q": eg[k], "ga": ga})
+        return res
+
+    def gat(c):
+        take(c["q"], c["ga"], B("xw" if c["kind"] == "o" else c["win"]), B("cu%d" % c["s"], 32 * c["k"], 32 * c["k"] + 32))
+
+    def dif(c):
+        h, e = 128 * (c["k"] // 4), C * (c["k"] % 4)
+        pe(chain(B("ps%d" % (c["i"] % 3)), [(B("nx%d" % c["s"], h, h + 128), B("E", e, e + C)), (B("I"), c["ga"])]))
+
+    def near(c):
+        r = c["i"] % 3
+        act(B("ab%d" % r), B("ps%d" % r), AF.Abs)
+        ts(B("id%d" % r), B("ab%d" % r), B("tlb"), OP.is_le)
+        pe(chain(B("pc%d" % (c["i"] % 2)), [(B("BO"), B("id%d" % r))]))
+        if c["kind"] == "b":
+            scan(B("mn", C * c["k"], C * c["k"] + C), B("sm"), c["ga"], OP.max, OP.min)
+
+    def fin(c):
+        s, k, pc = c["s"], c["k"], B("pc%d" % (c["i"] % 2))
+        if c["kind"] == "o":
+            mt = B("mt%d" % (c["i"] % 3))
+            act(mt, pc, AF.Relu, bias=-9.0)
+            copy(IND(B(c["win"]), B("vu%d" % s, 32 * k, 32 * k + 32)), mt)
+            return
+        scan(c["ga"], B("sx"), pc, OP.min, OP.max)
+        if k % 4 == 3:
+            m, c0 = 128 * (k // 4), 2048 * (k // 4)
+            tt(B("s32"), B("mn", c0 + 15, c0 + 2048, 16), B("xm%d" % s, m, m + 128), OP.add)
+            ts(B("dd"), B("ga", c0 + 15, c0 + 2048, 16), 9.5, OP.is_ge, 255.0, OP.mult)
+            ts(B("h32"), B("s32"), 1, OP.arith_shift_right)
+            tt(B("zc%d" % s, m, m + 128), B("h32"), B("dd"), OP.max)
+
+    def run(cs, at={}, after=None):
+        n = len(cs)
+        for t in range(-2, n + 1):
+            early = after and t == NC
+            if early:
+                fin(cs[t - 1])
+                after()
+            if t < 0 and t in at:
+                at[t]()
+            if 0 <= t + 1 < n:
+                dif(cs[t + 1])
+            if 0 <= t < n:
+                near(cs[t])
+            if t >= 1 and not early:
+                fin(cs[t - 1])
+            if t + 2 < n:
+                gat(cs[t + 2])
+            if t >= 0 and t in at:
+                at[t]()
+
+    def border_flags(s, win):
+        now, old = "sf%d" % (s % 2), "sf%d" % ((s + 1) % 2)
+        cut = (0, 288, 480) if s < 2 else (0, 336, NB)
+        for h in range(2):
+            a, b = cut[h], cut[h + 1]
+            prs = [] if s == 0 else [(B("I"), B(old, a, b))]
+            prs += [(B("I"), B(win, 4 * P + 4 * a + k, 4 * P + 4 * b, 4)) for k in range(4)]
+            pe(chain(B("pr%d" % h, 0, b - a), prs))
+            act(B(now, a, b), B("pr%d" % h, 0, b - a), AF.Copy)
+        if s < 2:
+            st = [B(win, 4 * P + 4 * 480 + k, 4 * W, 4) for k in range(4)]
+            m0, m1, o = B("mt0", 0, 192), B("mt1", 0, 192), B(now, 480, NB)
+            tt(m0, st[0], st[1], OP.add)
+            tt(m1, st[2], st[3], OP.add)
+            if s:
+                tt(m0, m0, B(old, 480, NB), OP.add)
+            tt(o, m0, m1, OP.add)
+        send("f%d" % s, now, "fr%d" % s, 0, -1)
+
+    def brood_table(t, win):
+        o = 4 * BS * t
+        return [(Lm(a), B(win, o + 4 * a + k, o + 4 * BS, 64)) for a in range(16) for k in range(4)]
+
+    def flags_in(s):
+        win = B("fr%d" % s)
+        o = 48 * s
+        take("s", B("gb", 0, 384), win, B("invT", o, o + 24))
+        take("v", B("gb", 384, BS), win, B("invT", o + 24, o + 48))
+        pe(chain(B("pf", 0, 48), [(Lm(a), B("gb", a, BS, 16)) for a in range(16)], first=False))
+
+    def stand(s, nxt):
+        take("s", B(nxt, BS * s, BS * s + 384), B("zc%d" % s), B("yp%d" % s, 0, 24))
+        take("v", B(nxt, BS * s + 384, BS * s + BS), B("zc%d" % s), B("yp%d" % s, 24, 48))
+
+    def border_take(win):
+        take("s", B("sb", 0, 384), B(win, 0, P), B("sndu", 0, 24))
+        take("v", B("sb", 384, NB), B(win, 0, P), B("sndu", 24, 42))
+
+    fill(B("BO"), 1.0)
+    fill(B("gb"), 0.0)
+    fill(B("L"), 0.0)
+    fill(B("I"), 1.0)
+    dma("sync", B("sndi"), HB(T.snd[:, :]))
+    dma("scalar", B("pk", 0, BS), HB(T.cd[:, 0:BS]))
+    dma("sync", B("xw", 0, BS), HB(T.x[:, 0:BS]))
+    dma("sync", B("gb", parts=slice(0, 128, 16)), HB(T.sd[:, :]))
+    dma("sync", B("xw", BS, P), HB(T.x[:, BS:P]))
+    dma("sync", B("tlb"), HB(T.tl[:, :]))
+    fill(B("E"), 1.0)
+    gsel(B("BO"), [[-16, 8], [0, 16]], OP.is_ge, 0, 1)
+    gsel(B("BO"), [[16, 8], [0, 16]], OP.is_ge, 15, -1)
+    gsel(B("NU"), [[-1, 128]], OP.is_gt, 0, 1, B("BO"))
+    giota(B("pi"), [[0, 8]], 0, 1)
+    giota(B("N256"), [[16, 48]], 256, 0)
+    giota(B("dum"), [[0, 8], [4096, 32]], 4 * W * 256, 0)
+    gsel(B("I"), [[-1, 128]], OP.is_equal, 0, 1)
+    er = B("pk", 2 * BS, 2 * BS + NB)
+    giota(er, [[1, NB]], 0, 0)
+    gsel(B("E"), [[-1, 128], [0, 16]], OP.is_equal, 0, 1)
+    for lo in range(0, P, 2048):
+        hi = min(P, lo + 2048)
+        act(B("inv", lo, hi), B("L", 0, hi - lo), AF.Copy, scale=0.0, bias=float(NB))
+    for a in range(16):
+        act(B("L", 128 * a + a, 128 * a + 128, 16), B("BO", a, 128, 16), AF.Copy)
+    act(B("L32"), B("L"), AF.Copy)
+    fill(B("z48"), 0.0)
+    ts(B("NU"), B("NU"), -1.0, OP.mult)
+    ts(B("pj"), B("pi"), 15, OP.bitwise_and)
+    copy(B("pf15"), B("pj"))
+    ts(B("pf15k"), B("pf15"), 256.0, OP.mult)
+    ts(B("N256"), B("N256"), B("pf15", 0, 1), OP.add)
+    ts(B("N769"), B("N256"), 513.0, OP.add)
+    ts(B("dum"), B("dum"), B("pf15k", 0, 1), OP.add)
+    copy(B("pkw", 1, 257), B("dum"))
+    copy(B("sndu", 0, 42), B("sndi"))
+    copy(IND(B("inv"), B("sndu", 0, 42)), er)
+    pack(0)
+    pe(chain(B("pf", 0, 48), [(Lm(a), B("gb", a, BS, 16)) for a in range(16)]))
+    members(0)
+    take("s", B("sb"), B("xw", 0, P), B("sndu", 0, 42))
+    rx = send("x", "sb", "xw", P)
+    dma("sync", B("yA", 0, P), HB(T.y0[:, :]), after=[rx])
+    dma("sync", B("pk", BS, 2 * BS), HB(T.cd[:, BS:2 * BS]))
+    for s in (2, 1, 0):
+        dma("sync", B("zc%d" % s, 256, 1024), HB(T.y0[:, s * BS:s * BS + BS]))
+    dma("sync", B("yB", 0, P), HB(T.y0[:, :]))
+    dma("sync", B("pk", 2 * BS, 3 * BS), HB(T.cd[:, 2 * BS:3 * BS]))
+    members2(0)
+    numbers(0)
+    fill(B("xw", W, WX), 0.0)
+    zero("wA", 0, ZV, ZS, 20096 - ZV - ZS)
+    for n, v in (("sm", 191.0), ("sx", 200.0)):
+        fill(B(n), v)
+    for s in range(3):
+        fill(B("fr%d" % s, 672, 688), 0.0)
+    fill(B("yA", W, WX), 0.0)
+    fill(B("yB", W, WX), 0.0)
+    ts(B("N257"), B("N256"), 1.0, OP.add)
+    tabi = chain(B("pf", 0, 96), [(Lm(a, "L32"), B("inv", BS + a, 3 * BS, 16)) for a in range(16)])
+    run(chunks("o", 0, "wA", range(NC), EG_OUT), {t: (lambda t=t: pe(tabi[4 * t - 16:4 * t - 12])) for t in range(4, 8)})
+    gsel(B("sm"), [[0, 32], [1, 16]], OP.is_equal, 0, 0)
+    gsel(B("sx"), [[0, 32], [1, 16]], OP.not_equal, 0, 0)
+    zero("wB", 0, 0, 0, ZB)
+    ts(B("invT"), B("pf", 0, 96), 0.0625, OP.mult)
+    border_flags(0, "wA")
+    pe(chain(B("pf", 0, 48), brood_table(1, "wA"), last=False))
+    border_take("yA")
+    send("y0", "sb", "yA", P)
+    pack(1)
+    places(0)
+    zero("wB", ZB, 3500, 4096, 20096 - 3500 - 4096 - ZB)
+    dma("sync", B("tq0"), B("wA", 0, 4 * P, parts=slice(0, 128, 16)))
+    giota(B("cwin", 0, 256), [[0, 256]], 1, 0)
+    giota(B("cwin", 256, 1024), [[0, 768]], 0, 0)
+    zero("row", 0, 0, 0, P)
+    zero("sdq", 0, 0, 0, 272)
+    flags_in(0)
+    members(1)
+    tab2 = chain(B("pf", 0, 48), brood_table(2, "wA"))
+    at = {t: (lambda t=t: pe(tab2[16 * t - 48:16 * t - 32])) for t in range(3, 7)}
+
+    def mid1():
+        members2(1)
+        numbers(1)
+    at[-1] = mid1
+    run(chunks("o", 1, "wB", range(NC), EG_OUT), at)
+    border_flags(1, "wB")
+    copy(B("F2a"), B("pf", 0, 48))
+    pe(chain(B("pf", 0, 48), brood_table(2, "wB") + [(B("I"), B("F2a"))], last=False))
+    pack(2)
+    places(1)
+    zero("wA", 0, 4500, 2048, 20096 - 2048 - 4500)
+    for s in (0, 1):
+        take("s", B("row", s * BS, s * BS + BS), B("cwin"), B("yp%d" % s))
+    dma("sync", B("tq1"), B("wB", 0, 4 * P, parts=slice(0, 128, 16)))
+    for q in range(3):
+        n = 272 if q < 2 else 224
+        dma("sync", B("sdq", 0, n, parts=slice(q, 128, 16)), HB(T.sd[:, 272 * q:272 * q + n]))
+    flags_in(1)
+    members(2)
+
+    def mid2():
+        numbers(2)
+        places(2)
+
+    def after2():
+        stand(2, "yB")
+        border_take("yB")
+        send("y1", "sb", "yB", P)
+        dma("sync", B("yA", 2 * BS, 3 * BS), B("yB", 2 * BS, 3 * BS))
+        dma("sync", HB(T.yv[:, 2 * BS:3 * BS]), B("yB", 2 * BS, 3 * BS))
+    run(chunks("b", 2, "yA", range(NC), EG_BACK2) + chunks("o", 2, "wA", range(SPLIT), EG_OUT2), {-1: lambda: members2(2), 3: mid2}, after2)
+    take("s", B("row", 2 * BS, 3 * BS), B("cwin"), B("yp2"))
+    dma("sync", B("mq"), B("row", parts=slice(0, 128, 16)))
+    zero("row", 0, 0, 0, 3 * BS)
+
+    def after1():
+        stand(1, "yA")
+        border_take("yA")
+        send("y2", "sb", "yA", P)
+        dma("sync", HB(T.yv[:, BS:2 * BS]), B("yA", BS, 2 * BS))
+    run(chunks("b", 1, "yB", range(NC), EG_BACK) + chunks("o", 2, "wA", range(SPLIT, NC), EG_OUT2), {}, after1)
+    acc = B("pf", 0, 272)
+
+    def flags_out():
+        border_flags(2, "wA")
+        dma("sync", B("tq2"), B("wA", 0, 4 * P, parts=slice(0, 128, 16)))
+
+    def flags_own():
+        pe(chain(acc, [(B("I"), B("tq%d" % s, k, 1088, 4)) for s in range(3) for k in range(4)] + [(B("I"), B("sdq"))], last=False))
+
+    def flags_all():
+        copy(IND(B("row"), B("sndu", 0, 42)), B("fr2", 0, NB))
+        dma("sync", B("rbq"), B("row", parts=slice(0, 128, 16)))
+
+    def flags_end():
+        pe(chain(acc, [(B("I"), B("rbq"))], first=False))
+        ts(B("yft"), acc, 0.5, OP.is_gt)
+        tt(B("yfo"), B("yft"), B("mq"), OP.add)
+        dma("sync", HB(T.yf[:, :]), B("yfo"))
+    run(chunks("b", 0, "yA", range(NC), EG_BACK), {1: flags_out, 5: flags_own, 6: flags_all, 8: flags_end})
+    stand(0, "yB")
+    dma("scalar", HB(T.yv[:, 0:384]), B("yB", 0, 384))
+    dma("sync", HB(T.yv[:, 384:BS]), B("yB", 384, BS))
+    totals.update(count)
+    for s in sorted(totals):
+        if known["g"].get(s, 0) < totals[s]:
+            g.wait_ge(T.sem[s], totals[s])

@@ -4,56 +4,83 @@ from concourse.mybir import AluOpType, ActivationFunctionType
 P, BS, GB, NR = 4352, 768, 96, 8
 NB = 7 * GB
 W = P + NB
-WX = W + 128
-VW = 4 * W + 512
-C = 512
-NC = 8
+U = 512
+DUM = 1024
+FW = DUM + 4 * W
+S0 = 1024
+MAGIC = 12582912.0
+FR = NB + 16
+Z0 = 2 * U
+INV, ER = 2048, 4352
+CUT = 4 * GB
 
 
 def _sb(n, d):
     return ("sbuf", [128, n], d)
 
 
-_BF = {"xw": WX, "yA": WX, "yB": WX, "wA": VW, "wB": VW, "E": 2048, "L": 2048, "I": 128, "BO": 128, "NU": 128, "ga": 4096, "mn": 4096,
-       "sm": C, "sx": C, "row": P, "tlb": 1, "g2": 1024, "cwin": 1024, "sf0": NB, "sf1": NB, "sb": NB, "gb": BS, "rbq": 272, "sdq": 272,
-       "mq": 272, "yfo": 272, "yft": 272, "F2a": 48, "z48": 48, "F": 48, "cs": 48, "dd": 128}
-_F32 = {"L32": 2048, "inv": P, "NF": 48, "A": 48, "q1": 48, "q2": 48, "q3": 48, "N769": 48, "N257": 48, "N256": 48, "pf15": 8, "pf15k": 8}
-_I32 = {"pk": 3 * BS, "pkw": 1544, "dum": 256, "ta": 256, "tb": 256, "sndi": 42, "pi": 8, "pj": 8, "s32": 128, "h32": 128}
-_U16 = {"invT": 96, "sndu": 48, "P16": 48}
+_BF = {"xw": W, "Y": P + 3 * NB, "wV": FW, "L": 2048, "LT": 2048, "I": 128, "H": 128, "Qm": 128, "Ds": 128, "BO": 128, "NU": 128, "ga": 6 * U, "mn": 4 * U,
+       "id": 6 * U, "ab": 2 * U, "sm": U, "oz": Z0 + BS, "tlb": 1, "fr": 3 * FR, "sf": NB, "sb": NB, "gb": BS, "sdq": 272,
+       "mq": 272, "yfo": 272, "yft": 272, "F": 48, "cs": 48, "dd": 128, "be": 48, "bb": 48}
+_F16 = {"E": 2048}
+_F32 = {"wS": S0 + FW, "four": U, "zf": 314, "I32": 128, "tse": 168, "tsb": 192, "NF": 48, "A": 48, "q1": 48, "q2": 48, "q3": 48, "N769": 48,
+        "N257": 48, "N256": 48, "pf15": 8, "tf": 8, "sc": 8, "dk": 256, "vv": 256, "t1": 256, "t2": 256, "zt": 128}
+_I32 = {"pk": 2 * BS, "pkw": 1544, "dum": 256, "ta": 256, "tb": 256, "sndi": 42, "pi": 8, "pj": 8}
+_U16 = {"invT": 96, "sndu": 48, "P16": 48, "ou": 256, "invo": 48}
 for _s in range(3):
-    _BF.update({"zc%d" % _s: 1024, "xm%d" % _s: 256, "nx%d" % _s: 256, "tq%d" % _s: 1088, "fr%d" % _s: 688, "ab%d" % _s: C, "id%d" % _s: C, "mt%d" % _s: C})
+    _BF.update({"zc%d" % (_s % 2): 1088, "xm%d" % _s: 256})
+    _F16.update({"nx%d" % _s: 256})
     _F32.update({"P32_%d" % _s: 48})
-    _U16.update({"vu%d" % _s: 256, "cu%d" % _s: 256, "yp%d" % _s: 48})
+    _U16.update({"cu%d" % _s: 256, "yp%d" % _s: 48})
+_U16.update({"cb0": 256, "cb1": 256})
 SCRATCH = {}
-for _t, _d in ((_BF, "bfloat16"), (_F32, "float32"), (_I32, "int32"), (_U16, "uint16")):
+for _t, _d in ((_BF, "bfloat16"), (_F16, "float16"), (_F32, "float32"), (_I32, "int32"), (_U16, "uint16")):
     SCRATCH.update({_n: _sb(_c, _d) for _n, _c in _t.items()})
+SCRATCH["rowd"] = ("dram", [8, P], "bfloat16")
 PSUMS = ["ps0", "ps1", "ps2", "pc0", "pc1", "pr0", "pr1", "pf"]
 for _n in PSUMS:
     SCRATCH[_n] = ("psum", [128, 512], "float32")
-NDMA = 30
+NDMA = 44
 EXCH = ["x", "f0", "f1", "f2", "y0", "y1", "y2"]
 SEMAPHORES = ["sv", "sa", "st", "sg"] + ["d%d" % k for k in range(NDMA)] + ["r_" + e for e in EXCH] + ["l_" + e for e in EXCH]
-EG_OUT = "ssvsssss"
-EG_OUT2 = "ssssssss"
-EG_BACK2 = "sssssvss"
-EG_BACK = "vsssssss"
-SPLIT = 4
-ZB, ZV, ZS = 8000, 9000, 6000
+
+OUT = {"v": "LB LA LC VV n0 LD n1 n2 o01 n3 s1 o23 n4 n5 s3 o45 n6 n7 s5 o67 s6 s7",
+       "s": "g0 g1 g2 g3 g4 g5 s0 g6 g7 s2 s4 SDMA X2",
+       "t": "d0 LM d1 d2 c01 d3 d4 c23 d5 c45 d6 d7 c67 X1 X3"}
+BACK = {"v": "g1 n0 m0 n1 m1 n2 y01 m2 n3 m3 z01 n4 y23 m4 n5 m5 z23 n6 y45 n7 m6 m7 z45 y67 z67",
+        "s": "g0 g2 g3 g4 g5 g6 g7",
+        "t": "d0 d1 d2 c01 d3 e01 d4 c23 d5 e23 d6 c45 d7 e45 c67 e67"}
+BACK2 = {"v": "LB LA LC m0 n0 LD n1 m1 n2 y01 m2 PLACES n3 m3 z01 n4 y23 m4 n5 m5 z23 n6 y45 n7 m6 m7 z45 y67 z67",
+         "s": "g0 g1 g2 g3 g4 g5 g6 g7", "t": BACK["t"].replace("d0", "d0 LM")}
+OUT2A = {"v": "VV n0 n1 n2 o01 n3 n4 o23 n5 s2 o45",
+         "s": "g4 g5 ROW s0 s1 s3",
+         "t": "d0 d1 d2 c01 d3 d4 c23 d5 c45"}
+OUT2B = {"v": "n6 n7 s5 o67 s6 s7 TQ",
+         "s": "X2",
+         "t": "d6 d7 c67 X1 X3 B1"}
+BACK0 = {"v": "B3 n0 m0 n1 m1 n2 y01 m2 n3 m3 z01 END n4 y23 m4 n5 m5 z23 n6 y45 n7 m6 m7 z45 NEW y67 z67",
+         "s": "g0 B2 g1 g2 g3 g4 g5 g6 g7 RG",
+         "t": "d0 d1 d2 c01 OWN d3 W e01 d4 c23 d5 e23 d6 c45 d7 e45 c67 e67"}
 
 
 def exchange_plan(topo, cores, r, sg):
     src = cores[r]
     dst = [None] + [cores[(r + sg * d) % NR] for d in range(1, NR)]
     off = [d for d in range(1, NR) if topo.chip(dst[d]) != topo.chip(src)]
-    on = [d for d in range(1, NR) if d not in off]
     eng = topo.engines(src, dst[off[0]])
-    n = len(eng)
-    first, second = off[:4], off[4:]
-    calls = [[(d, eng[i * n // 4:(i + 1) * n // 4]) for i, d in enumerate(first)],
-             [(d, eng[i * n // 2:(i + 1) * n // 2]) for i, d in enumerate(second)]]
-    for d in on:
-        free = [e for e in topo.engines(src, dst[d]) if e not in eng]
-        calls[0 if d < second[0] else 1].append((d, free[:8]))
+    q = len(eng) // 4
+    calls = []
+    for k, ds in enumerate((range(1, 5), range(5, NR))):
+        mine = [d for d in ds if d in off]
+        sizes = {4: [q, q, q, q], 2: [2 * q, 2 * q], 3: [q, q, 2 * q] if k == 0 else [2 * q, q, q]}[len(mine)]
+        call, at = [], 0
+        for d, n in zip(mine, sizes):
+            call.append((d, eng[at:at + n]))
+            at += n
+        for d in ds:
+            if d not in off:
+                call.append((d, [e for e in topo.engines(src, dst[d]) if e not in eng][:8]))
+        calls.append(call)
     return calls
 
 
@@ -65,8 +92,9 @@ def rank_program(g, core, T, topo):
     cores = list(T.cores)
     eng = {"g": g, "vector": g.vector, "scalar": g.scalar, "tensor": g.tensor, "sync": g.sync}
     csem = {"vector": "sv", "scalar": "sa", "tensor": "st", "g": "sg"}
-    count, totals, recs, ndma, seq = {}, {}, {}, [0], [0]
+    count, totals, recs, ndma = {}, {}, {}, [0]
     known = {q: {} for q in eng}
+    ROWS = slice(0, 128, 16)
 
     def B(name, lo=None, hi=None, st=1, parts=None):
         lo = 0 if lo is None else lo
@@ -179,13 +207,20 @@ def rank_program(g, core, T, topo):
 
     def act(out, in_, f, **kw): op("scalar", lambda e: e.activation(out["ap"], in_["ap"], f, **kw), [out], [in_])
 
-    def take(q, out, win, off):
+    def move(q, out, in_):
         if q == "v":
-            copy(out, IND(win, off))
+            copy(out, in_)
         else:
-            act(out, IND(win, off), AF.Copy)
+            act(out, in_, AF.Copy)
 
-    def pe(mms):
+    def take(q, out, win, off):
+        move(q, out, IND(win, off))
+
+    def pe(mms, behind=False):
+        if behind and known["tensor"].get("st", 0) < count["st"]:
+            g.tensor.wait_ge(T.sem["st"], count["st"])
+            known["tensor"]["st"] = count["st"]
+
         def run_all(e):
             for o, l, r, a, b in mms:
                 k = e.matmul(o["ap"], l["ap"], r["ap"], a, b)
@@ -204,6 +239,9 @@ def rank_program(g, core, T, topo):
     def Lm(a, nm="L"):
         return B(nm, 128 * a, 128 * a + 128)
 
+    def table(src, lo, n, nm="L"):
+        return [(Lm(a, nm), B(src, lo + a, lo + n, 16)) for a in range(16)]
+
     def gsel(o, pat, cmp, base, cm, i=None):
         i = o if i is None else i
         op("g", lambda e: e.affine_select(o["ap"], i["ap"], pat, cmp, 0.0, base, cm), [o], [i])
@@ -211,53 +249,52 @@ def rank_program(g, core, T, topo):
     def giota(o, pat, base, cm):
         op("g", lambda e: e.iota(o["ap"], pat, base, cm, allow_small_or_imprecise_dtypes=True), [o], [])
 
-    def zero(win, lo, nv, ns, ng):
-        for q, n in (("v", nv), ("s", ns), ("g", ng)):
-            end = lo + n
-            while lo < end:
-                m = end - lo if q == "v" else min(2048, end - lo)
-                o = B(win, lo, lo + m)
-                if q == "v":
-                    fill(o, 0.0)
-                elif q == "s":
-                    act(o, B("E", 0, m), AF.Copy, scale=0.0)
-                else:
-                    giota(o, [[0, m]], 0, 0)
-                lo += m
+    def sfill(o, v, src):
+        act(o, src, AF.Copy, scale=0.0, bias=v)
 
     def pack(s):
-        o = B("pk", s * BS, s * BS + BS)
+        o = B("pk", s % 2 * BS, s % 2 * BS + BS)
         ts(o, o, 256.0, OP.mult)
         tt(o, o, B("xw", s * BS, s * BS + BS), OP.add)
+
+    def places_of(s, lo, hi):
+        ts(B("ta", lo, hi), B("pkw", 1 + lo, 1 + hi), 10, OP.arith_shift_right)
+        copy(B("cu%d" % s, lo, hi), B("ta", lo, hi))
+
+    def marks_of(s, h):
+        lo, hi = 128 * h, 128 * h + 128
+        ts(B("tb", lo, hi), B("pkw", 1 + lo, 1 + hi), 255, OP.bitwise_and)
+        copy(B("xm%d" % s, lo, hi), B("tb", lo, hi))
+
+    def turned(s, h):
+        pe([(B("pr%d" % h, 0, 128), B("xm%d" % s, 128 * h, 128 * h + 128), B("Ds"), True, True)])
+
+    def scaled(s, h):
+        ts(B("nx%d" % s, 128 * h, 128 * h + 128), B("pr%d" % h, 0, 128), -1.0, OP.mult)
 
     def members(s):
         pf = B("pf", 0, 48)
         ts(B("F"), pf, 0.5, OP.is_gt)
-        scan(B("cs"), B("z48"), B("F"), OP.add, OP.add)
+        scan(B("cs"), B("oz", Z0, Z0 + 48), B("F"), OP.add, OP.add)
         ts(B("NF"), pf, 0.5, OP.is_le)
         pe(chain(B("pc0", 0, 48), [(B("BO"), B("cs")), (B("NU"), B("F"))]))
         tt(B("A"), B("NF"), B("N769"), OP.mult)
         tt(B("P32_%d" % s), B("pc0", 0, 48), B("A"), OP.max)
         copy(B("P16"), B("P32_%d" % s))
-        copy(IND(B("pkw"), B("P16")), B("pk", s * BS, s * BS + BS))
-        half_list(s, 0)
-        ts(B("tb"), B("pkw", 1, 257), 255, OP.bitwise_and)
-        copy(B("xm%d" % s), B("tb"))
-        pe([(B("pr0", 128 * h, 128 * h + 128), B("xm%d" % s, 128 * h, 128 * h + 128), B("I"), True, True) for h in range(2)])
+        copy(IND(B("pkw"), B("P16")), B("pk", s % 2 * BS, s % 2 * BS + BS))
+        places_of(s, 0, 64)
+        marks_of(s, 0)
+        turned(s, 0)
 
-    def half_list(s, lo):
-        ts(B("ta", lo, lo + 128), B("pkw", 1 + lo, 129 + lo), 10, OP.arith_shift_right)
-        copy(B("cu%d" % s, lo, lo + 128), B("ta", lo, lo + 128))
+    def numbers(lo, hi):
+        ts(B("tb", lo, hi), B("pkw", 1 + lo, 1 + hi), 8, OP.arith_shift_right)
+        ts(B("vv", lo, hi), B("tb", lo, hi), 1.0 / 32768, OP.mult, 9.0 + DUM / 32768, OP.add)
 
-    def members2(s):
-        ts(B("nx%d" % s), B("pr0", 0, 256), -1.0, OP.mult)
-        half_list(s, 128)
-
-    def numbers(s):
-        ts(B("ta"), B("pkw", 1, 257), 8, OP.arith_shift_right)
-        copy(B("vu%d" % s), B("ta"))
-        if s < 2:
-            copy(B("pkw", 1, 257), B("dum"))
+    def back_list(s):
+        ts(B("t1"), B("ta"), P - 0.5, OP.is_ge, float(NB * (2 - s)), OP.mult)
+        tt(B("t2"), B("t1"), B("ta"), OP.add)
+        copy(B("cb%d" % s), B("t2"))
+        copy(B("pkw", 1, 257), B("dum"))
 
     def places(s):
         p = B("P32_%d" % s)
@@ -267,249 +304,343 @@ def rank_program(g, core, T, topo):
         tt(B("q2"), B("q3"), B("N256"), OP.add)
         copy(B("yp%d" % s), B("q2"))
 
-    def chunks(kind, s, win, ks, eg):
-        res = []
-        for k in ks:
-            i = seq[0]
-            seq[0] += 1
-            ga = B("g2", C * (i % 2), C * (i % 2) + C) if kind == "o" and s == 2 else B("ga", C * k, C * k + C)
-            res.append({"kind": kind, "s": s, "k": k, "i": i, "win": win, "q": eg[k], "ga": ga})
-        return res
+    RING = {"ga": 6, "ps": 3, "ab": 2, "id": 3, "pc": 2, "mn": 2, "pz": 2}
+    turn, holder, slot, made, group = {r: 0 for r in RING}, {}, {}, set(), {}
 
-    def gat(c):
-        take(c["q"], c["ga"], B("xw" if c["kind"] == "o" else c["win"]), B("cu%d" % c["s"], 32 * c["k"], 32 * c["k"] + 32))
+    def ready(st, c, us, sized):
+        pair = lambda u: group[(st, u)]
+        u = us[0] if us else None
+        back = st[0] == "b"
+        if c == "g":
+            return [("g", (u - 1,))] * (u > 0), ("ga", u, [("d", us)] + ([("m", us)] if back else []))
+        if c == "d":
+            return [("g", us)], ("ps", u, [("a" if u in sized else "n", us)])
+        if c == "a":
+            return [("d", us)], ("ab", u, [("n", us)])
+        if c == "n":
+            return [("a" if u in sized else "d", us)], ("id", pair(u), [("c", pair(u))])
+        if c == "m":
+            return [("g", us)], ("mn", pair(u), [("e", pair(u))])
+        if c == "c":
+            return [("n", (k,)) for k in us], ("pc", us, [("y" if back else "o", us)])
+        if c in "oy":
+            return [("c", us)], None
+        if c == "s":
+            return [("o", pair(k)) for k in us], None
+        if c == "e":
+            return [("y", us)] + [("m", (k,)) for k in us], ("pz", us, [("z", us)])
+        if c == "z":
+            return [("e", us)], None
 
-    def dif(c):
-        h, e = 128 * (c["k"] // 4), C * (c["k"] % 4)
-        pe(chain(B("ps%d" % (c["i"] % 3)), [(B("nx%d" % c["s"], h, h + 128), B("E", e, e + C)), (B("I"), c["ga"])]))
+    def issue(st, q, c, us, sized):
+        s, back, u, n = int(st[1]), st[0] == "b", us[0], len(us)
+        at = lambda ring, key: slot[(ring, st, key)]
+        m0, m1 = 32 * u, 32 * (u + n)
+        ga = lambda: B("ga", U * at("ga", u), U * at("ga", u) + U)
+        def part(ring):
+            pr = group[(st, u)]
+            o = 2 * U * at(ring, pr) + U * pr.index(u)
+            return B(ring, o, o + U)
+        if c == "g":
+            win = B("Y", 0, P + NB * (3 - s)) if back else B("xw")
+            take(q, ga(), win, B(("cb%d" if back and s < 2 else "cu%d") % s, m0, m1))
+        elif c == "d":
+            h, e = 128 * (u // 4), U * (u % 4)
+            pe(chain(B("ps%d" % at("ps", u)), [(B("nx%d" % s, h, h + 128), B("E", e, e + U)), (B("Ds"), ga())]))
+        elif c == "a":
+            act(B("ab", U * at("ab", u), U * at("ab", u) + U), B("ps%d" % at("ps", u)), AF.Abs)
+        elif c == "n" and u in sized:
+            ts(part("id"), B("ab", U * at("ab", u), U * at("ab", u) + U), 0.5, OP.is_lt)
+        elif c == "n":
+            ts(part("id"), B("ps%d" % at("ps", u)), MAGIC, OP.add, MAGIC, OP.is_equal)
+        elif c == "m":
+            scan(part("mn"), B("sm"), ga(), OP.max, OP.min)
+        elif c == "c":
+            pe(chain(B("pc%d" % at("pc", us), 0, 32 * n), table("id", 2 * U * at("id", us), U * n)))
+        elif c == "o":
+            tt(B("t1", m0, m1), B("pc%d" % at("pc", us), 0, 32 * n), B("vv", m0, m1), OP.min)
+            tt(B("t2", m0, m1), B("t1", m0, m1), B("dk", m0, m1), OP.max)
+            ts(B("ou", m0, m1), B("t2", m0, m1), -9.0, OP.add, 32768.0, OP.mult)
+        elif c == "s" and q == "v":
+            copy(IND(B("wV"), B("ou", m0, m1)), B("oz", 0, U * n))
+        elif c == "s":
+            act(IND(B("wS", S0), B("ou", m0, m1)), B("four", 0, U * n), AF.Silu)
+        elif c == "y":
+            o = 64 * at("pc", us)
+            ts(B("dd", o, o + 32 * n), B("pc%d" % at("pc", us), 0, 32 * n), 9.5, OP.is_ge, 255.0, OP.mult)
+        elif c == "e":
+            o, d = 2 * U * at("mn", us), 64 * at("pc", us)
+            pe(chain(B("pr%d" % at("pz", us), 0, 32 * n), [(B("H"), B("xm%d" % s, m0, m1)), (B("Qm"), B("oz", 0, 32 * n)), (B("H"), B("mn", o + 15, o + U * n, 16)),
+                                                           (B("BO"), B("dd", d, d + 32 * n))]))
+        elif c == "z":
+            z = B("zt", 64 * at("pz", us), 64 * at("pz", us) + 32 * n)
+            ts(z, B("pr%d" % at("pz", us), 0, 32 * n), 255.0, OP.min, MAGIC, OP.add)
+            ts(B("zc%d" % (s % 2), m0, m1), z, MAGIC, OP.subtract)
 
-    def near(c):
-        r = c["i"] % 3
-        act(B("ab%d" % r), B("ps%d" % r), AF.Abs)
-        ts(B("id%d" % r), B("ab%d" % r), B("tlb"), OP.is_le)
-        pe(chain(B("pc%d" % (c["i"] % 2)), [(B("BO"), B("id%d" % r))]))
-        if c["kind"] == "b":
-            scan(B("mn", C * c["k"], C * c["k"] + C), B("sm"), c["ga"], OP.max, OP.min)
+    def run(parts, own):
+        todo = {q: [] for q in "vst"}
+        sized = {}
+        for st, ls in parts:
+            for q in ls:
+                for w in ls[q].split():
+                    us = () if w[0].isupper() else tuple(int(k) for k in w[1:])
+                    todo[q].append((st, w if not us else w[0], us))
+                    if w[0] == "c":
+                        group.update({(st, k): us for k in us})
+                    if w[0] == "a":
+                        sized.setdefault(st, []).append(us[0])
+        while any(todo.values()):
+            moved = False
+            for q in "svt":
+                while todo[q]:
+                    st, c, us = todo[q][0]
+                    if not us:
+                        if not all(any((x, b, ()) in made for x in (st, "o2", "b0")) for b in own[c][1]):
+                            break
+                        if c == "X1" and any(x[:2] == (st, "o") for x in todo["v"]):
+                            break
+                        own[c][0]()
+                    else:
+                        before, ring = ready(st, c, us, sized.get(st, []))
+                        w = {"d": "LA" if us[0] < 4 else "LD", "g": "LB" if us[0] > 1 else ""}.get(c)
+                        if (st, w, ()) in todo["v"]:
+                            break
+                        if not all((st, b, k) in made for b, k in before):
+                            break
+                        if ring and (ring[0], st, ring[1]) not in slot:
+                            k = turn[ring[0]]
+                            if not all(x in made for x in holder.get((ring[0], k), [])):
+                                break
+                            slot[(ring[0], st, ring[1])] = k
+                            holder[(ring[0], k)] = [(st, b, j) for b, j in ring[2]]
+                            turn[ring[0]] = (k + 1) % RING[ring[0]]
+                        issue(st, q, c, us, sized.get(st, []))
+                    made.add(todo[q].pop(0))
+                    moved = True
+            assert moved, todo
 
-    def fin(c):
-        s, k, pc = c["s"], c["k"], B("pc%d" % (c["i"] % 2))
-        if c["kind"] == "o":
-            mt = B("mt%d" % (c["i"] % 3))
-            act(mt, pc, AF.Relu, bias=-9.0)
-            copy(IND(B(c["win"]), B("vu%d" % s, 32 * k, 32 * k + 32)), mt)
-            return
-        scan(c["ga"], B("sx"), pc, OP.min, OP.max)
-        if k % 4 == 3:
-            m, c0 = 128 * (k // 4), 2048 * (k // 4)
-            tt(B("s32"), B("mn", c0 + 15, c0 + 2048, 16), B("xm%d" % s, m, m + 128), OP.add)
-            ts(B("dd"), B("ga", c0 + 15, c0 + 2048, 16), 9.5, OP.is_ge, 255.0, OP.mult)
-            ts(B("h32"), B("s32"), 1, OP.arith_shift_right)
-            tt(B("zc%d" % s, m, m + 128), B("h32"), B("dd"), OP.max)
-
-    def run(cs, at={}, after=None):
-        n = len(cs)
-        for t in range(-2, n + 1):
-            early = after and t == NC
-            if early:
-                fin(cs[t - 1])
-                after()
-            if t < 0 and t in at:
-                at[t]()
-            if 0 <= t + 1 < n:
-                dif(cs[t + 1])
-            if 0 <= t < n:
-                near(cs[t])
-            if t >= 1 and not early:
-                fin(cs[t - 1])
-            if t + 2 < n:
-                gat(cs[t + 2])
-            if t >= 0 and t in at:
-                at[t]()
-
-    def border_flags(s, win):
-        now, old = "sf%d" % (s % 2), "sf%d" % ((s + 1) % 2)
-        cut = (0, 288, 480) if s < 2 else (0, 336, NB)
-        for h in range(2):
-            a, b = cut[h], cut[h + 1]
-            prs = [] if s == 0 else [(B("I"), B(old, a, b))]
-            prs += [(B("I"), B(win, 4 * P + 4 * a + k, 4 * P + 4 * b, 4)) for k in range(4)]
-            pe(chain(B("pr%d" % h, 0, b - a), prs))
-            act(B(now, a, b), B("pr%d" % h, 0, b - a), AF.Copy)
+    def s_rows(s):
+        dma("sync", B("tse"), B("wS", S0 + DUM + 4 * P, S0 + FW, parts=ROWS))
         if s < 2:
-            st = [B(win, 4 * P + 4 * 480 + k, 4 * W, 4) for k in range(4)]
-            m0, m1, o = B("mt0", 0, 192), B("mt1", 0, 192), B(now, 480, NB)
-            tt(m0, st[0], st[1], OP.add)
-            tt(m1, st[2], st[3], OP.add)
-            if s:
-                tt(m0, m0, B(old, 480, NB), OP.add)
-            tt(o, m0, m1, OP.add)
-        send("f%d" % s, now, "fr%d" % s, 0, -1)
+            o = S0 + DUM + 4 * BS * (s + 1)
+            dma("sync", B("tsb"), B("wS", o, o + 4 * BS, parts=ROWS))
 
-    def brood_table(t, win):
-        o = 4 * BS * t
-        return [(Lm(a), B(win, o + 4 * a + k, o + 4 * BS, 64)) for a in range(16) for k in range(4)]
+    def stubs(out, src, n):
+        pe(chain(out, [(B("I32"), B(src, k, 4 * n, 4)) for k in range(4)]))
+
+    def runs(src, n, banks, cut, first, last):
+        mm = []
+        for a in range(16):
+            for lo, hi in ((n * a, min(n * a + n, cut)), (max(n * a, cut), n * a + n)):
+                if lo < hi:
+                    o = cut if lo >= cut else 0
+                    mm.append((B(banks[lo >= cut], lo - o, hi - o), Lm(a, "LT"), B(src, lo - n * a, hi - n * a), first, last))
+        return mm
+
+    def out_calls(s):
+        def x3():
+            pe([(B("pr0", 0, CUT), B("I"), B("oz", Z0, Z0 + CUT), True, False), (B("pr1", 0, NB - CUT), B("I"), B("oz", Z0, Z0 + NB - CUT), True, False)])
+            pe(runs("be", 42, ("pr0", "pr1"), CUT, False, False), True)
+        return {"LA": (lambda: scaled(s, 0), []), "LB": (lambda: places_of(s, 64, 256), []), "LC": (lambda: marks_of(s, 1), []),
+                "LM": (lambda: turned(s, 1), ["LC"]), "LD": (lambda: scaled(s, 1), ["LM"]), "VV": (lambda: numbers(0, 256), []), "SDMA": (lambda: s_rows(s), []),
+                "X1": (lambda: stubs(B("pc0", 0, 42), "tse", 42), ["SDMA"]), "X2": (lambda: move("s", B("be", 0, 42), B("pc0", 0, 42)), ["X1"]),
+                "X3": (x3, ["X2"]), "PLACES": (lambda: places(s), [])}
+
+    def border_sum(h):
+        o, (a, b) = DUM + 4 * P, ((0, CUT), (CUT, NB))[h]
+        pe(chain(B("pr%d" % h, 0, b - a), [(B("I"), B("wV", o + 4 * a + k, o + 4 * b, 4)) for k in range(4)], first=False), h == 0)
+
+    def border_sign(h):
+        if h == 0:
+            act(B("sf", 0, CUT), B("pr0", 0, CUT), AF.Sign, scale=-1.0)
+        else:
+            ts(B("sf", CUT, NB), B("pr1", 0, NB - CUT), 0.5, OP.is_gt, -1.0, OP.mult)
+
+    def border_flags(s):
+        for h in range(2):
+            border_sum(h)
+            border_sign(h)
+        send("f%d" % s, "sf", "fr", FR * s, -1)
+
+    def own_flags(t):
+        o = DUM + 4 * BS * t
+        stubs(B("pc1", 0, 48), "tsb", 48)
+        move("s", B("bb"), B("pc1", 0, 48))
+        pe(chain(B("pf", 0, 48), [(Lm(a), B("wV", o + 4 * a + k, o + 4 * BS, 64)) for a in range(16) for k in range(4)], last=False))
+        pe(runs("bb", 48, ("ps0", "ps1"), 384, True, True))
+        for h in range(2):
+            move("s", B("mn", 384 * h, 384 * h + 384), B("ps%d" % h, 0, 384))
+        pe(chain(B("pf", 0, 48), table("mn", 0, BS), first=False, last=False))
 
     def flags_in(s):
-        win = B("fr%d" % s)
+        win = B("fr", FR * s, FR * s + FR)
         o = 48 * s
-        take("s", B("gb", 0, 384), win, B("invT", o, o + 24))
-        take("v", B("gb", 384, BS), win, B("invT", o + 24, o + 48))
-        pe(chain(B("pf", 0, 48), [(Lm(a), B("gb", a, BS, 16)) for a in range(16)], first=False))
+        act(B("gb", 0, 384), IND(win, B("invT", o, o + 24)), AF.Copy, scale=-1.0)
+        ts(B("gb", 384, BS), IND(win, B("invT", o + 24, o + 48)), -1.0, OP.mult)
+        pe(chain(B("pf", 0, 48), table("gb", 0, BS), first=False))
 
-    def stand(s, nxt):
-        take("s", B(nxt, BS * s, BS * s + 384), B("zc%d" % s), B("yp%d" % s, 0, 24))
-        take("v", B(nxt, BS * s + 384, BS * s + BS), B("zc%d" % s), B("yp%d" % s, 24, 48))
+    def stand(s):
+        take("s", B("Y", BS * s, BS * s + 384), B("zc%d" % (s % 2), 0, 1024), B("yp%d" % s, 0, 24))
+        take("v", B("Y", BS * s + 384, BS * s + BS), B("zc%d" % (s % 2), 0, 1024), B("yp%d" % s, 24, 48))
+
+    def old(s):
+        dma("sync", B("zc%d" % (s % 2), 256, 1024), HB(T.y0[:, s * BS:s * BS + BS]))
+
+    def member_row(s, buf, lo):
+        take("s", B(buf, lo, lo + BS), B("oz", Z0 - 256, Z0 + BS), B("yp%d" % s))
+        dma("sync", B("rowd", s * BS, s * BS + BS), B(buf, lo, lo + BS, parts=ROWS))
 
     def border_take(win):
-        take("s", B("sb", 0, 384), B(win, 0, P), B("sndu", 0, 24))
-        take("v", B("sb", 384, NB), B(win, 0, P), B("sndu", 24, 42))
+        take("s", B("sb", 0, 352), B(win, 0, P), B("sndu", 0, 22))
+        take("v", B("sb", 352, NB), B(win, 0, P), B("sndu", 22, 42))
 
-    fill(B("BO"), 1.0)
     fill(B("gb"), 0.0)
-    fill(B("L"), 0.0)
+    fill(B("BO"), 1.0)
     fill(B("I"), 1.0)
     dma("sync", B("sndi"), HB(T.snd[:, :]))
-    dma("scalar", B("pk", 0, BS), HB(T.cd[:, 0:BS]))
     dma("sync", B("xw", 0, BS), HB(T.x[:, 0:BS]))
-    dma("sync", B("gb", parts=slice(0, 128, 16)), HB(T.sd[:, :]))
+    dma("sync", B("gb", parts=ROWS), HB(T.sd[:, :]))
     dma("sync", B("xw", BS, P), HB(T.x[:, BS:P]))
     dma("sync", B("tlb"), HB(T.tl[:, :]))
-    fill(B("E"), 1.0)
+    dma("sync", B("pk", 0, BS), HB(T.cd[:, 0:BS]))
+    fill(B("L"), 0.0)
+    fill(B("oz", Z0), 0.0)
+    dma("sync", B("wV", DUM, DUM + 4 * BS, parts=ROWS), B("oz", Z0, Z0 + 192))
+    dma("sync", B("wV", DUM + 12 * BS, DUM + 4 * P, parts=ROWS), B("oz", Z0, Z0 + 512))
     gsel(B("BO"), [[-16, 8], [0, 16]], OP.is_ge, 0, 1)
     gsel(B("BO"), [[16, 8], [0, 16]], OP.is_ge, 15, -1)
-    gsel(B("NU"), [[-1, 128]], OP.is_gt, 0, 1, B("BO"))
     giota(B("pi"), [[0, 8]], 0, 1)
+    gsel(B("NU"), [[-1, 128]], OP.is_gt, 0, 1, B("BO"))
     giota(B("N256"), [[16, 48]], 256, 0)
-    giota(B("dum"), [[0, 8], [4096, 32]], 4 * W * 256, 0)
     gsel(B("I"), [[-1, 128]], OP.is_equal, 0, 1)
-    er = B("pk", 2 * BS, 2 * BS + NB)
-    giota(er, [[1, NB]], 0, 0)
-    gsel(B("E"), [[-1, 128], [0, 16]], OP.is_equal, 0, 1)
-    for lo in range(0, P, 2048):
-        hi = min(P, lo + 2048)
-        act(B("inv", lo, hi), B("L", 0, hi - lo), AF.Copy, scale=0.0, bias=float(NB))
+    giota(B("dk"), [[0, 4], [16, 64]], 0, 0)
+    giota(B("wS", ER, ER + NB), [[1, NB]], 64, 0)
     for a in range(16):
         act(B("L", 128 * a + a, 128 * a + 128, 16), B("BO", a, 128, 16), AF.Copy)
-    act(B("L32"), B("L"), AF.Copy)
-    fill(B("z48"), 0.0)
-    ts(B("NU"), B("NU"), -1.0, OP.mult)
     ts(B("pj"), B("pi"), 15, OP.bitwise_and)
     copy(B("pf15"), B("pj"))
-    ts(B("pf15k"), B("pf15"), 256.0, OP.mult)
+    ts(B("NU"), B("NU"), -1.0, OP.mult)
     ts(B("N256"), B("N256"), B("pf15", 0, 1), OP.add)
-    ts(B("N769"), B("N256"), 513.0, OP.add)
-    ts(B("dum"), B("dum"), B("pf15k", 0, 1), OP.add)
-    copy(B("pkw", 1, 257), B("dum"))
     copy(B("sndu", 0, 42), B("sndi"))
-    copy(IND(B("inv"), B("sndu", 0, 42)), er)
-    pack(0)
-    pe(chain(B("pf", 0, 48), [(Lm(a), B("gb", a, BS, 16)) for a in range(16)]))
-    members(0)
-    take("s", B("sb"), B("xw", 0, P), B("sndu", 0, 42))
+    fill(B("wV", DUM + 4 * BS, DUM + 8 * BS), 0.0)
+    ts(B("N769"), B("N256"), 513.0, OP.add)
+    act(B("wS", 0, 2048), B("L"), AF.Copy)
+    pe(chain(B("pf", 0, 48), table("gb", 0, BS)))
+    ts(B("q1", 0, 42), B("sndi"), BS - 0.5, OP.is_ge)
+    ts(B("q2", 0, 42), B("sndi"), 3 * BS - 0.5, OP.is_lt)
+    ts(B("q3", 0, 42), B("N256", 0, 42), float(3 * BS - 256), OP.add)
+    tt(B("q1", 0, 42), B("q1", 0, 42), B("q2", 0, 42), OP.mult)
+    tt(B("q2", 0, 42), B("sndi"), B("q3", 0, 42), OP.subtract)
+    tt(B("q1", 0, 42), B("q1", 0, 42), B("q2", 0, 42), OP.mult)
+    tt(B("q2", 0, 42), B("q1", 0, 42), B("q3", 0, 42), OP.add)
+    ts(B("invo", 0, 42), B("q2", 0, 42), float(-BS), OP.add)
+    ts(B("dk"), B("dk"), B("pf15", 0, 1), OP.add)
+    ts(B("dum"), B("dk"), float(-DUM), OP.add, 256.0, OP.mult)
+    copy(B("pkw", 1, 257), B("dum"))
+    border_take("xw")
     rx = send("x", "sb", "xw", P)
-    dma("sync", B("yA", 0, P), HB(T.y0[:, :]), after=[rx])
+    ts(B("tf", 0, 1), B("tlb"), 2.0, OP.mult, 1.0, OP.add)
+    op("vector", lambda e: e.reciprocal(T.sc[:, 0:1], T.tf[:, 0:1]), [B("sc", 0, 1)], [B("tf", 0, 1)])
+    ts(B("Ds"), B("I"), B("sc", 0, 1), OP.mult)
+    giota(B("id", 0, 2048), [[-1, 128], [0, 16]], 0, 1)
+    fill(B("zf"), 0.0)
+    pack(0)
+    sfill(B("wS", INV, INV + 2 * BS), 64.0 + NB, B("L", 0, 2 * BS))
+    act(IND(B("wS", INV, INV + 2 * BS + NB), B("invo", 0, 42)), B("wS", ER, ER + NB), AF.Silu)
+    members(0)
+    sfill(B("wV", DUM + 4 * P, DUM + 4 * P + 2048), 0.0, B("L"))
+    sfill(B("wV", DUM + 4 * P + 2048, FW), 0.0, B("L", 0, 4 * NB - 2048))
+    sfill(B("four"), 4.0, B("L", 0, U))
+    run([("o0", {"v": "LB LA LC VV LD", "t": "LM"})], out_calls(0))
+    pe(chain(B("pf", 0, 96), [(B("wS", 128 * a, 128 * a + 128), B("wS", INV + a, INV + 2 * BS, 16)) for a in range(16)]))
+    ts(B("E"), B("id", 0, 2048), 0.0, OP.is_equal)
+    fill(B("oz", 0, Z0), 1.0)
+    ts(B("dk"), B("dk"), 1.0 / 32768, OP.mult, 9.0, OP.add)
+    for k in (3, 2, 1, 0):
+        dma("sync", B("wS", S0 + DUM + W * k, S0 + DUM + W * k + W, parts=ROWS), B("zf"), after=[rx])
     dma("sync", B("pk", BS, 2 * BS), HB(T.cd[:, BS:2 * BS]))
-    for s in (2, 1, 0):
-        dma("sync", B("zc%d" % s, 256, 1024), HB(T.y0[:, s * BS:s * BS + BS]))
-    dma("sync", B("yB", 0, P), HB(T.y0[:, :]))
-    dma("sync", B("pk", 2 * BS, 3 * BS), HB(T.cd[:, 2 * BS:3 * BS]))
-    members2(0)
-    numbers(0)
-    fill(B("xw", W, WX), 0.0)
-    zero("wA", 0, ZV, ZS, 20096 - ZV - ZS)
-    for n, v in (("sm", 191.0), ("sx", 200.0)):
-        fill(B(n), v)
-    for s in range(3):
-        fill(B("fr%d" % s, 672, 688), 0.0)
-    fill(B("yA", W, WX), 0.0)
-    fill(B("yB", W, WX), 0.0)
-    ts(B("N257"), B("N256"), 1.0, OP.add)
-    tabi = chain(B("pf", 0, 96), [(Lm(a, "L32"), B("inv", BS + a, 3 * BS, 16)) for a in range(16)])
-    run(chunks("o", 0, "wA", range(NC), EG_OUT), {t: (lambda t=t: pe(tabi[4 * t - 16:4 * t - 12])) for t in range(4, 8)})
+    dma("sync", B("Y", 0, P), HB(T.y0[:, :]))
+    fill(B("wV", DUM + 8 * BS, DUM + 12 * BS), 0.0)
+    gsel(B("I32"), [[-1, 128]], OP.is_equal, 0, 1, B("four", 0, 128))
+    for h in range(2):
+        gsel(B("LT", 1024 * h, 1024 * h + 1024), [[-1, 8], [-16, 8], [0, 16]], OP.is_equal, -8 * h, 1, B("oz", 0, 1024))
+    giota(B("sm"), [[0, U]], 191, 0)
     gsel(B("sm"), [[0, 32], [1, 16]], OP.is_equal, 0, 0)
-    gsel(B("sx"), [[0, 32], [1, 16]], OP.not_equal, 0, 0)
-    zero("wB", 0, 0, 0, ZB)
-    ts(B("invT"), B("pf", 0, 96), 0.0625, OP.mult)
-    border_flags(0, "wA")
-    pe(chain(B("pf", 0, 48), brood_table(1, "wA"), last=False))
-    border_take("yA")
-    send("y0", "sb", "yA", P)
+    for s in range(2):
+        giota(B("fr", FR * s + NB, FR * s + FR), [[0, 16]], 0, 0)
+    giota(B("sdq"), [[0, 272]], 0, 0)
+    dma("sync", B("rowd", 3 * BS, P), B("oz", Z0, Z0 + 128))
+    run([("o0", dict(OUT, v=" ".join(w for w in OUT["v"].split() if w[0] not in "LV"), t=OUT["t"].replace("LM ", "")))], out_calls(0))
+    ts(B("invT"), B("pf", 0, 96), 0.0625, OP.mult, -63.75, OP.add)
+    border_flags(0)
+    own_flags(1)
+    border_take("Y")
+    send("y0", "sb", "Y", P)
     pack(1)
+    dma("sync", B("pk", 0, BS), HB(T.cd[:, 2 * BS:3 * BS]))
+    ts(B("N257"), B("N256"), 1.0, OP.add)
+    back_list(0)
     places(0)
-    zero("wB", ZB, 3500, 4096, 20096 - 3500 - 4096 - ZB)
-    dma("sync", B("tq0"), B("wA", 0, 4 * P, parts=slice(0, 128, 16)))
-    giota(B("cwin", 0, 256), [[0, 256]], 1, 0)
-    giota(B("cwin", 256, 1024), [[0, 768]], 0, 0)
-    zero("row", 0, 0, 0, P)
-    zero("sdq", 0, 0, 0, 272)
+    ts(B("H"), B("I"), 0.5, OP.mult)
+    ts(B("Qm"), B("I"), -0.25, OP.mult)
     flags_in(0)
     members(1)
-    tab2 = chain(B("pf", 0, 48), brood_table(2, "wA"))
-    at = {t: (lambda t=t: pe(tab2[16 * t - 48:16 * t - 32])) for t in range(3, 7)}
-
-    def mid1():
-        members2(1)
-        numbers(1)
-    at[-1] = mid1
-    run(chunks("o", 1, "wB", range(NC), EG_OUT), at)
-    border_flags(1, "wB")
-    copy(B("F2a"), B("pf", 0, 48))
-    pe(chain(B("pf", 0, 48), brood_table(2, "wB") + [(B("I"), B("F2a"))], last=False))
-    pack(2)
-    places(1)
-    zero("wA", 0, 4500, 2048, 20096 - 2048 - 4500)
-    for s in (0, 1):
-        take("s", B("row", s * BS, s * BS + BS), B("cwin"), B("yp%d" % s))
-    dma("sync", B("tq1"), B("wB", 0, 4 * P, parts=slice(0, 128, 16)))
+    for s in (2, 1):
+        old(s)
     for q in range(3):
         n = 272 if q < 2 else 224
         dma("sync", B("sdq", 0, n, parts=slice(q, 128, 16)), HB(T.sd[:, 272 * q:272 * q + n]))
+    run([("o1", OUT)], out_calls(1))
+    border_flags(1)
+    own_flags(2)
+    pack(2)
+    back_list(1)
+    places(1)
+    for s in (0, 1):
+        member_row(s, "id", BS * s)
     flags_in(1)
     members(2)
 
-    def mid2():
-        numbers(2)
-        places(2)
-
-    def after2():
-        stand(2, "yB")
-        border_take("yB")
-        send("y1", "sb", "yB", P)
-        dma("sync", B("yA", 2 * BS, 3 * BS), B("yB", 2 * BS, 3 * BS))
-        dma("sync", HB(T.yv[:, 2 * BS:3 * BS]), B("yB", 2 * BS, 3 * BS))
-    run(chunks("b", 2, "yA", range(NC), EG_BACK2) + chunks("o", 2, "wA", range(SPLIT), EG_OUT2), {-1: lambda: members2(2), 3: mid2}, after2)
-    take("s", B("row", 2 * BS, 3 * BS), B("cwin"), B("yp2"))
-    dma("sync", B("mq"), B("row", parts=slice(0, 128, 16)))
-    zero("row", 0, 0, 0, 3 * BS)
-
-    def after1():
-        stand(1, "yA")
-        border_take("yA")
-        send("y2", "sb", "yA", P)
-        dma("sync", HB(T.yv[:, BS:2 * BS]), B("yA", BS, 2 * BS))
-    run(chunks("b", 1, "yB", range(NC), EG_BACK) + chunks("o", 2, "wA", range(SPLIT, NC), EG_OUT2), {}, after1)
+    run([("b2", BACK2), ("o2", {"s": "g0 g1 g2 g3"})], out_calls(2))
+    stand(2)
+    border_take("Y")
+    ry = send("y1", "sb", "Y", P + NB)
+    dma("sync", HB(T.yv[:, 2 * BS:3 * BS]), B("Y", 2 * BS, 3 * BS), after=[ry])
+    old(0)
+    calls = out_calls(2)
+    calls["ROW"] = (lambda: (member_row(2, "gb", 0), dma("sync", B("mq"), B("rowd"))), [])
+    run([("o2", OUT2A), ("b1", BACK), ("o2", {"s": "g6 g7 s4 SDMA"})], calls)
+    stand(1)
+    border_take("Y")
+    ry = send("y2", "sb", "Y", P + 2 * NB)
     acc = B("pf", 0, 272)
 
-    def flags_out():
-        border_flags(2, "wA")
-        dma("sync", B("tq2"), B("wA", 0, 4 * P, parts=slice(0, 128, 16)))
+    def all_rows():
+        dma("g", B("fr", 0, 1088), B("wS", S0 + DUM, S0 + DUM + 4 * P, parts=ROWS))
+        dma("sync", B("zc1", 0, 1088), B("wV", DUM, DUM + 4 * P, parts=ROWS))
+        dma("sync", HB(T.yv[:, BS:2 * BS]), B("Y", BS, 2 * BS), after=[ry])
 
-    def flags_own():
-        pe(chain(acc, [(B("I"), B("tq%d" % s, k, 1088, 4)) for s in range(3) for k in range(4)] + [(B("I"), B("sdq"))], last=False))
+    def own_sum():
+        pe(chain(acc, [(B("I"), B(w, k, 1088, 4)) for w in ("fr", "zc1") for k in range(4)] + [(B("I"), B("sdq")), (B("I"), B("mq"))]))
 
-    def flags_all():
-        copy(IND(B("row"), B("sndu", 0, 42)), B("fr2", 0, NB))
-        dma("sync", B("rbq"), B("row", parts=slice(0, 128, 16)))
-
-    def flags_end():
-        pe(chain(acc, [(B("I"), B("rbq"))], first=False))
+    def own_end():
         ts(B("yft"), acc, 0.5, OP.is_gt)
         tt(B("yfo"), B("yft"), B("mq"), OP.add)
-        dma("sync", HB(T.yf[:, :]), B("yfo"))
-    run(chunks("b", 0, "yA", range(NC), EG_BACK), {1: flags_out, 5: flags_own, 6: flags_all, 8: flags_end})
-    stand(0, "yB")
-    dma("scalar", HB(T.yv[:, 0:384]), B("yB", 0, 384))
-    dma("sync", HB(T.yv[:, 384:BS]), B("yB", 384, BS))
+        dma("sync", B("xw", 0, P, parts=ROWS), B("yfo"))
+
+    def arrived():
+        ts(B("sf"), B("sb"), 0.5, OP.is_lt, -1.0, OP.mult)
+        scan(B("ab", 0, NB), B("fr", 2 * FR, 2 * FR + NB), B("sf"), OP.min, OP.mult)
+    calls.update({"B1": (lambda: (border_sum(0), border_sum(1)), ["TQ"]), "B2": (lambda: border_sign(0), ["B1"]),
+                  "B3": (lambda: (border_sign(1), send("f2", "sf", "fr", 2 * FR, -1)), ["B1", "B2"]), "W": (lambda: None, ["B3"]),
+                  "TQ": (all_rows, []), "OWN": (own_sum, ["TQ"]), "END": (own_end, ["OWN"]),
+                  "RG": (lambda: take("s", B("sb"), B("xw", 0, P), B("sndu", 0, 42)), ["END"]), "NEW": (arrived, ["RG"])})
+    run([("o2", OUT2B), ("b0", BACK0)], calls)
+    for h in range(2):
+        take("s", B("Y", 384 * h, 384 * h + 384), B("zc0", 0, 1024), B("yp0", 24 * h, 24 * h + 24))
+        dma("scalar", HB(T.yv[:, 384 * h:384 * h + 384]), B("Y", 384 * h, 384 * h + 384))
+    tt(IND(B("xw", 0, P), B("sndu", 0, 42)), B("ab", 0, NB), B("sb"), OP.add)
+    dma("sync", HB(T.yf[:, :]), B("xw", 0, P, parts=ROWS))
     totals.update(count)
     for s in sorted(totals):
         if known["g"].get(s, 0) < totals[s]:

@@ -12,19 +12,20 @@ MAGIC = 12582912.0
 FR = NB + 16
 Z0 = 2 * U
 INV, ER = 2048, 4352
-CUT = 4 * GB
+CUT = 3 * GB
+HALVES = ((0, CUT), (CUT, NB))
 
 
 def _sb(n, d):
     return ("sbuf", [128, n], d)
 
 
-_BF = {"xw": W, "Y": P + 3 * NB, "wV": FW, "L": 2048, "LT": 2048, "I": 128, "H": 128, "Qm": 128, "Ds": 128, "BO": 128, "NU": 128, "ga": 6 * U, "mn": 4 * U,
-       "id": 6 * U, "ab": 2 * U, "sm": U, "oz": Z0 + BS, "tlb": 1, "fr": 3 * FR, "sf": NB, "sb": NB, "gb": BS, "sdq": 272,
-       "mq": 272, "yfo": 272, "yft": 272, "F": 48, "cs": 48, "dd": 128, "be": 48, "bb": 48}
+_BF = {"xw": W, "Y": P + 3 * NB, "wV": FW, "L": 2048, "LT": 2048, "I": 128, "H": 128, "Ds": 128, "BO": 128, "NU": 128, "ga": 8 * U, "mn": 8 * U,
+       "id": 8 * U, "sm": U, "sx": U, "oz": Z0 + BS, "tlb": 1, "fr": 3 * FR, "sf": BS, "sb": NB, "gb": BS, "sdq": 272,
+       "mq": 272, "yfo": 272, "F": 48, "cs": 48, "dd": 256, "be": 48}
 _F16 = {"E": 2048}
-_F32 = {"wS": S0 + FW, "four": U, "zf": 314, "I32": 128, "tse": 168, "tsb": 192, "NF": 48, "A": 48, "q1": 48, "q2": 48, "q3": 48, "N769": 48,
-        "N257": 48, "N256": 48, "pf15": 8, "tf": 8, "sc": 8, "dk": 256, "vv": 256, "t1": 256, "t2": 256, "zt": 128}
+_F32 = {"wS": S0 + FW, "I32": 128, "ts": 272, "NF": 48, "A": 48, "q1": 48, "q2": 48, "q3": 48, "N769": 48,
+        "N257": 48, "N256": 48, "pf15": 8, "tf": 8, "sc": 8, "dk": 256, "vv": 256, "t1": 256, "t2": 256}
 _I32 = {"pk": 2 * BS, "pkw": 1544, "dum": 256, "ta": 256, "tb": 256, "sndi": 42, "pi": 8, "pj": 8}
 _U16 = {"invT": 96, "sndu": 48, "P16": 48, "ou": 256, "invo": 48}
 for _s in range(3):
@@ -44,23 +45,24 @@ NDMA = 44
 EXCH = ["x", "f0", "f1", "f2", "y0", "y1", "y2"]
 SEMAPHORES = ["sv", "sa", "st", "sg"] + ["d%d" % k for k in range(NDMA)] + ["r_" + e for e in EXCH] + ["l_" + e for e in EXCH]
 
-OUT = {"v": "LB LA LC VV n0 LD n1 n2 o01 n3 s1 o23 n4 n5 s3 o45 n6 n7 s5 o67 s6 s7",
-       "s": "g0 g1 g2 g3 g4 g5 s0 g6 g7 s2 s4 SDMA X2",
-       "t": "d0 LM d1 d2 c01 d3 d4 c23 d5 c45 d6 d7 c67 X1 X3"}
-BACK = {"v": "g1 n0 m0 n1 m1 n2 y01 m2 n3 m3 z01 n4 y23 m4 n5 m5 z23 n6 y45 n7 m6 m7 z45 y67 z67",
-        "s": "g0 g2 g3 g4 g5 g6 g7",
-        "t": "d0 d1 d2 c01 d3 e01 d4 c23 d5 e23 d6 c45 d7 e45 c67 e67"}
-BACK2 = {"v": "LB LA LC m0 n0 LD n1 m1 n2 y01 m2 PLACES n3 m3 z01 n4 y23 m4 n5 m5 z23 n6 y45 n7 m6 m7 z45 y67 z67",
-         "s": "g0 g1 g2 g3 g4 g5 g6 g7", "t": BACK["t"].replace("d0", "d0 LM")}
-OUT2A = {"v": "VV n0 n1 n2 o01 n3 n4 o23 n5 s2 o45",
-         "s": "g4 g5 ROW s0 s1 s3",
-         "t": "d0 d1 d2 c01 d3 d4 c23 d5 c45"}
-OUT2B = {"v": "n6 n7 s5 o67 s6 s7 TQ",
-         "s": "X2",
-         "t": "d6 d7 c67 X1 X3 B1"}
-BACK0 = {"v": "B3 n0 m0 n1 m1 n2 y01 m2 n3 m3 z01 END n4 y23 m4 n5 m5 z23 n6 y45 n7 m6 m7 z45 NEW y67 z67",
-         "s": "g0 B2 g1 g2 g3 g4 g5 g6 g7 RG",
-         "t": "d0 d1 d2 c01 OWN d3 W e01 d4 c23 d5 e23 d6 c45 d7 e45 c67 e67"}
+OUT = {"v": "LB LA g1 LC n0 LD n1 g6 n2 VV n3 n4 o01 n5 o23 s3 o45 n6 n7 s5 o67 s6 s7",
+       "s": "g0 g2 g3 g4 g5 g7 s0 s1 s2 s4 SDMA K0 K1 K2",
+       "t": "d0 d1 LM d2 d3 c01 d4 d5 c23 c45 d6 d7 c67 J3 J0 J1 J2"}
+OUT0 = {"v": "g1 INV n0 n1 g6 n2 n3 o01 n4 n5 o23 s3 o45 n6 n7 s5 o67 s6 s7", "s": OUT["s"], "t": OUT["t"].replace("LM ", "")}
+BACK = {"v": "g1 g2 n0 n1 n2 m0 n3 n4 m1 n5 m2 m3 n6 m4 n7 m5 m6 m7 y012345 z012345 y67 z67",
+        "s": "g0 g3 g4 g5 g6 g7",
+        "t": "d0 d1 d2 d3 d4 d5 d6 d7 c012345 h67 e012345 c67 e67"}
+BACK2 = {"v": "LB LA g1 LC n0 LD n1 n2 m0 n3 n4 m1 n5 m2 m3 n6 m4 n7 PLACES" + BACK["v"].split("n7")[1],
+         "s": "g0 g2 g3 g4 g5 g6 g7", "t": BACK["t"].replace("d1", "d1 LM")}
+OUT2A = {"v": "n0 n1 n2 VV n3 o01 n4 n5 n6 n7",
+         "s": "g5 g6 g7 s0 s1",
+         "t": "d0 d1 d2 d3 c01 d4 d5 d6 d7 c2345"}
+OUT2B = {"v": "o67 s6 s7 TQ",
+         "s": "s5 SDMA K0 K1 K2",
+         "t": "c67 J3 J0 J1 J2 B1"}
+BACK0 = {"v": "B2 g1 g2 n0 n1 n2 m0 n3 END n4 m1 n5 m2 m3 n6 m4 n7 m5 m6 m7 NEW y012345 z012345 y67 z67 FIN",
+         "s": "g0 B3 g3 g4 g5 g6 g7 RG",
+         "t": BACK["t"].replace("d3", "d3 OWN").replace("e012345", "W e012345")}
 
 
 def exchange_plan(topo, cores, r, sg):
@@ -70,7 +72,7 @@ def exchange_plan(topo, cores, r, sg):
     eng = topo.engines(src, dst[off[0]])
     q = len(eng) // 4
     calls = []
-    for k, ds in enumerate((range(1, 5), range(5, NR))):
+    for k, ds in enumerate((range(1, 4), range(4, NR))):
         mine = [d for d in ds if d in off]
         sizes = {4: [q, q, q, q], 2: [2 * q, 2 * q], 3: [q, q, 2 * q] if k == 0 else [2 * q, q, q]}[len(mine)]
         call, at = [], 0
@@ -216,11 +218,7 @@ def rank_program(g, core, T, topo):
     def take(q, out, win, off):
         move(q, out, IND(win, off))
 
-    def pe(mms, behind=False):
-        if behind and known["tensor"].get("st", 0) < count["st"]:
-            g.tensor.wait_ge(T.sem["st"], count["st"])
-            known["tensor"]["st"] = count["st"]
-
+    def pe(mms):
         def run_all(e):
             for o, l, r, a, b in mms:
                 k = e.matmul(o["ap"], l["ap"], r["ap"], a, b)
@@ -272,7 +270,7 @@ def rank_program(g, core, T, topo):
     def scaled(s, h):
         ts(B("nx%d" % s, 128 * h, 128 * h + 128), B("pr%d" % h, 0, 128), -1.0, OP.mult)
 
-    def members(s):
+    def members(s, beside=lambda: None):
         pf = B("pf", 0, 48)
         ts(B("F"), pf, 0.5, OP.is_gt)
         scan(B("cs"), B("oz", Z0, Z0 + 48), B("F"), OP.add, OP.add)
@@ -284,6 +282,7 @@ def rank_program(g, core, T, topo):
         copy(IND(B("pkw"), B("P16")), B("pk", s % 2 * BS, s % 2 * BS + BS))
         places_of(s, 0, 64)
         marks_of(s, 0)
+        beside()
         turned(s, 0)
 
     def numbers(lo, hi):
@@ -304,157 +303,143 @@ def rank_program(g, core, T, topo):
         tt(B("q2"), B("q3"), B("N256"), OP.add)
         copy(B("yp%d" % s), B("q2"))
 
-    RING = {"ga": 6, "ps": 3, "ab": 2, "id": 3, "pc": 2, "mn": 2, "pz": 2}
-    turn, holder, slot, made, group = {r: 0 for r in RING}, {}, {}, set(), {}
+    RING = {"ga": 8, "ps": 3, "pc": 2, "pz": 2}
+    turn, holder, slot, made, of = {r: 0 for r in RING}, {}, {}, set(), {}
 
-    def ready(st, c, us, sized):
-        pair = lambda u: group[(st, u)]
-        u = us[0] if us else None
-        back = st[0] == "b"
+    def aside(st, u):
+        return st == "o2" and u >= 6
+
+    def ready(st, c, us):
+        u, back = us[0], st[0] == "b"
+        call = lambda k, u: (k, of[(st, k, u)])
+        rows = (st, "r", u) in of
         if c == "g":
-            return [("g", (u - 1,))] * (u > 0), ("ga", u, [("d", us)] + ([("m", us)] if back else []))
+            return [], ("ga", [("d", us)] + ([("m", us)] if back else []))
         if c == "d":
-            return [("g", us)], ("ps", u, [("a" if u in sized else "n", us)])
-        if c == "a":
-            return [("d", us)], ("ab", u, [("n", us)])
+            return [("g", us)], ("ps", [("n", us)])
         if c == "n":
-            return [("a" if u in sized else "d", us)], ("id", pair(u), [("c", pair(u))])
+            return [("d", us)], None if aside(st, u) else ("id", [("y", us) if rows else call("c", u)])
         if c == "m":
-            return [("g", us)], ("mn", pair(u), [("e", pair(u))])
-        if c == "c":
-            return [("n", (k,)) for k in us], ("pc", us, [("y" if back else "o", us)])
-        if c in "oy":
-            return [("c", us)], None
+            return [("g", us)], ("mn", [call("e", u)])
+        if c == "c" and (st, "h", u) in of:
+            return [("h", us)], None
+        if c in "chr":
+            return [("n", (k,)) for k in us], ("pc", [("x" if rows else "y" if back else "o", us)])
+        if c in "oyx":
+            return [("x" if rows and c == "y" else "r" if rows else "c", us)], None
         if c == "s":
-            return [("o", pair(k)) for k in us], None
+            return [call("o", k) for k in us], None
         if c == "e":
-            return [("y", us)] + [("m", (k,)) for k in us], ("pz", us, [("z", us)])
-        if c == "z":
-            return [("e", us)], None
+            return [call("y", k) for k in us] + [("m", (k,)) for k in us], ("pz", [("z", us)])
+        return [("e", us)], None
 
-    def issue(st, q, c, us, sized):
+    def issue(st, q, c, us):
         s, back, u, n = int(st[1]), st[0] == "b", us[0], len(us)
-        at = lambda ring, key: slot[(ring, st, key)]
         m0, m1 = 32 * u, 32 * (u + n)
-        ga = lambda: B("ga", U * at("ga", u), U * at("ga", u) + U)
-        def part(ring):
-            pr = group[(st, u)]
-            o = 2 * U * at(ring, pr) + U * pr.index(u)
-            return B(ring, o, o + U)
+        ga = lambda: B("ga", U * slot[(st, "ga", us)], U * slot[(st, "ga", us)] + U)
+        bank = lambda ring, w: B({"pz": "pr"}.get(ring, ring) + str(slot[(st, ring, us)]), 0, w)
+        unit = lambda buf: B(buf, U * u, U * u + U)
         if c == "g":
             win = B("Y", 0, P + NB * (3 - s)) if back else B("xw")
             take(q, ga(), win, B(("cb%d" if back and s < 2 else "cu%d") % s, m0, m1))
         elif c == "d":
             h, e = 128 * (u // 4), U * (u % 4)
-            pe(chain(B("ps%d" % at("ps", u)), [(B("nx%d" % s, h, h + 128), B("E", e, e + U)), (B("Ds"), ga())]))
-        elif c == "a":
-            act(B("ab", U * at("ab", u), U * at("ab", u) + U), B("ps%d" % at("ps", u)), AF.Abs)
-        elif c == "n" and u in sized:
-            ts(part("id"), B("ab", U * at("ab", u), U * at("ab", u) + U), 0.5, OP.is_lt)
+            pe(chain(bank("ps", U), [(B("nx%d" % s, h, h + 128), B("E", e, e + U)), (B("Ds"), ga())]))
         elif c == "n":
-            ts(part("id"), B("ps%d" % at("ps", u)), MAGIC, OP.add, MAGIC, OP.is_equal)
+            ts(B("LT", U * (u - 6), U * (u - 5)) if aside(st, u) else unit("id"), bank("ps", U), MAGIC, OP.add, MAGIC, OP.is_equal)
         elif c == "m":
-            scan(part("mn"), B("sm"), ga(), OP.max, OP.min)
-        elif c == "c":
-            pe(chain(B("pc%d" % at("pc", us), 0, 32 * n), table("id", 2 * U * at("id", us), U * n)))
+            scan(unit("mn"), B("sm"), ga(), OP.max, OP.min)
+        elif c in "hc":
+            mm = chain(bank("pc", 32 * n), table("LT", 0, U * n) if aside(st, u) else table("id", U * u, U * n))
+            pe(mm[:8] if c == "h" else mm[8:] if (st, "h", u) in of else mm)
+        elif c == "r":
+            pe(chain(bank("pc", U), [(B("BO"), unit("id"))]))
+        elif c == "x":
+            scan(unit("id"), B("sx"), bank("pc", U), OP.mult, OP.max)
         elif c == "o":
-            tt(B("t1", m0, m1), B("pc%d" % at("pc", us), 0, 32 * n), B("vv", m0, m1), OP.min)
+            tt(B("t1", m0, m1), bank("pc", 32 * n), B("vv", m0, m1), OP.min)
             tt(B("t2", m0, m1), B("t1", m0, m1), B("dk", m0, m1), OP.max)
             ts(B("ou", m0, m1), B("t2", m0, m1), -9.0, OP.add, 32768.0, OP.mult)
         elif c == "s" and q == "v":
             copy(IND(B("wV"), B("ou", m0, m1)), B("oz", 0, U * n))
         elif c == "s":
-            act(IND(B("wS", S0), B("ou", m0, m1)), B("four", 0, U * n), AF.Silu)
+            act(IND(B("wS", S0), B("ou", m0, m1)), B("wS", 0, U * n), AF.Silu)
         elif c == "y":
-            o = 64 * at("pc", us)
-            ts(B("dd", o, o + 32 * n), B("pc%d" % at("pc", us), 0, 32 * n), 9.5, OP.is_ge, 255.0, OP.mult)
+            cnt = B("id", U * u + 15, U * u + U, 16) if (st, "r", u) in of else bank("pc", 32 * n)
+            ts(B("dd", m0, m1), cnt, 9.5, OP.is_ge, 255.0, OP.mult)
         elif c == "e":
-            o, d = 2 * U * at("mn", us), 64 * at("pc", us)
-            pe(chain(B("pr%d" % at("pz", us), 0, 32 * n), [(B("H"), B("xm%d" % s, m0, m1)), (B("Qm"), B("oz", 0, 32 * n)), (B("H"), B("mn", o + 15, o + U * n, 16)),
-                                                           (B("BO"), B("dd", d, d + 32 * n))]))
+            pe(chain(bank("pz", 32 * n), [(B("H"), B("xm%d" % s, m0, m1)), (B("H"), B("mn", U * u + 15, U * (u + n), 16)), (B("BO"), B("dd", m0, m1))]))
         elif c == "z":
-            z = B("zt", 64 * at("pz", us), 64 * at("pz", us) + 32 * n)
-            ts(z, B("pr%d" % at("pz", us), 0, 32 * n), 255.0, OP.min, MAGIC, OP.add)
-            ts(B("zc%d" % (s % 2), m0, m1), z, MAGIC, OP.subtract)
+            ts(B("t1", m0, m1), bank("pz", 32 * n), -0.25, OP.add, MAGIC, OP.add)
+            ts(B("zc%d" % (s % 2), m0, m1), B("t1", m0, m1), MAGIC, OP.subtract, 255.0, OP.min)
 
     def run(parts, own):
         todo = {q: [] for q in "vst"}
-        sized = {}
         for st, ls in parts:
             for q in ls:
                 for w in ls[q].split():
                     us = () if w[0].isupper() else tuple(int(k) for k in w[1:])
                     todo[q].append((st, w if not us else w[0], us))
-                    if w[0] == "c":
-                        group.update({(st, k): us for k in us})
-                    if w[0] == "a":
-                        sized.setdefault(st, []).append(us[0])
+                    of.update({(st, w[0], k): us for k in us})
         while any(todo.values()):
             moved = False
             for q in "svt":
                 while todo[q]:
                     st, c, us = todo[q][0]
                     if not us:
-                        if not all(any((x, b, ()) in made for x in (st, "o2", "b0")) for b in own[c][1]):
-                            break
-                        if c == "X1" and any(x[:2] == (st, "o") for x in todo["v"]):
+                        if not all(any((x, b, ()) in made for x in (st, "b2", "o2", "b0")) for b in own[c][1]):
                             break
                         own[c][0]()
                     else:
-                        before, ring = ready(st, c, us, sized.get(st, []))
+                        before, ring = ready(st, c, us)
                         w = {"d": "LA" if us[0] < 4 else "LD", "g": "LB" if us[0] > 1 else ""}.get(c)
-                        if (st, w, ()) in todo["v"]:
+                        if (st, w, ()) in todo["v"] or not all((st, b, k) in made for b, k in before):
                             break
-                        if not all((st, b, k) in made for b, k in before):
-                            break
-                        if ring and (ring[0], st, ring[1]) not in slot:
-                            k = turn[ring[0]]
+                        if ring:
+                            k = turn.get(ring[0], us[0])
                             if not all(x in made for x in holder.get((ring[0], k), [])):
                                 break
-                            slot[(ring[0], st, ring[1])] = k
-                            holder[(ring[0], k)] = [(st, b, j) for b, j in ring[2]]
-                            turn[ring[0]] = (k + 1) % RING[ring[0]]
-                        issue(st, q, c, us, sized.get(st, []))
+                            slot[(st, ring[0], us)] = k
+                            holder[(ring[0], k)] = [(st, b, j) for b, j in ring[1]]
+                            if ring[0] in RING:
+                                turn[ring[0]] = (k + 1) % RING[ring[0]]
+                        issue(st, q, c, us)
                     made.add(todo[q].pop(0))
                     moved = True
             assert moved, todo
 
     def s_rows(s):
-        dma("sync", B("tse"), B("wS", S0 + DUM + 4 * P, S0 + FW, parts=ROWS))
         if s < 2:
             o = S0 + DUM + 4 * BS * (s + 1)
-            dma("sync", B("tsb"), B("wS", o, o + 4 * BS, parts=ROWS))
-
-    def stubs(out, src, n):
-        pe(chain(out, [(B("I32"), B(src, k, 4 * n, 4)) for k in range(4)]))
-
-    def runs(src, n, banks, cut, first, last):
-        mm = []
-        for a in range(16):
-            for lo, hi in ((n * a, min(n * a + n, cut)), (max(n * a, cut), n * a + n)):
-                if lo < hi:
-                    o = cut if lo >= cut else 0
-                    mm.append((B(banks[lo >= cut], lo - o, hi - o), Lm(a, "LT"), B(src, lo - n * a, hi - n * a), first, last))
-        return mm
+            dma("sync", B("ts", 0, 192), B("wS", o, o + 4 * BS, parts=ROWS))
 
     def out_calls(s):
-        def x3():
-            pe([(B("pr0", 0, CUT), B("I"), B("oz", Z0, Z0 + CUT), True, False), (B("pr1", 0, NB - CUT), B("I"), B("oz", Z0, Z0 + NB - CUT), True, False)])
-            pe(runs("be", 42, ("pr0", "pr1"), CUT, False, False), True)
-        return {"LA": (lambda: scaled(s, 0), []), "LB": (lambda: places_of(s, 64, 256), []), "LC": (lambda: marks_of(s, 1), []),
+        o = S0 + DUM + 4 * P
+
+        def narrow(k):
+            move("s", B("mn", 1024 * k, 1024 * k + NB), B("wS", o + k, S0 + FW, 4))
+
+        def add(k):
+            if k == 3:
+                pe([(B("pr%d" % h, 0, b - a), B("I32"), B("wS", o + 4 * a + 3, o + 4 * b, 4), True, False) for h, (a, b) in enumerate(HALVES)])
+            else:
+                pe([(B("pr%d" % h, 0, b - a), B("I"), B("mn", 1024 * k + a, 1024 * k + b), False, False) for h, (a, b) in enumerate(HALVES)])
+        stubs = {"K%d" % k: (lambda k=k: narrow(k), []) for k in range(3)}
+        stubs.update({"J%d" % k: (lambda k=k: add(k), ["K%d" % k, "J3"] if k < 3 else ["SDMA"]) for k in range(4)})
+        return {**stubs, "LA": (lambda: scaled(s, 0), []), "LB": (lambda: places_of(s, 64, 256), []), "LC": (lambda: marks_of(s, 1), []),
                 "LM": (lambda: turned(s, 1), ["LC"]), "LD": (lambda: scaled(s, 1), ["LM"]), "VV": (lambda: numbers(0, 256), []), "SDMA": (lambda: s_rows(s), []),
-                "X1": (lambda: stubs(B("pc0", 0, 42), "tse", 42), ["SDMA"]), "X2": (lambda: move("s", B("be", 0, 42), B("pc0", 0, 42)), ["X1"]),
-                "X3": (x3, ["X2"]), "PLACES": (lambda: places(s), [])}
+                "PLACES": (lambda: places(s), []),
+                "INV": (lambda: ts(B("invT"), B("pf", 0, 96), 0.0625, OP.mult, -63.75, OP.add), [])}
 
     def border_sum(h):
-        o, (a, b) = DUM + 4 * P, ((0, CUT), (CUT, NB))[h]
-        pe(chain(B("pr%d" % h, 0, b - a), [(B("I"), B("wV", o + 4 * a + k, o + 4 * b, 4)) for k in range(4)], first=False), h == 0)
+        o, (a, b) = DUM + 4 * P, HALVES[h]
+        pe(chain(B("pr%d" % h, 0, b - a), [(B("I"), B("wV", o + 4 * a + k, o + 4 * b, 4)) for k in range(4)], first=False))
 
     def border_sign(h):
         if h == 0:
-            act(B("sf", 0, CUT), B("pr0", 0, CUT), AF.Sign, scale=-1.0)
+            ts(B("sf", 0, CUT), B("pr0", 0, CUT), 0.5, OP.is_gt, -1.0, OP.mult)
         else:
-            ts(B("sf", CUT, NB), B("pr1", 0, NB - CUT), 0.5, OP.is_gt, -1.0, OP.mult)
+            act(B("sf", CUT, NB), B("pr1", 0, NB - CUT), AF.Sign, scale=-1.0)
 
     def border_flags(s):
         for h in range(2):
@@ -464,13 +449,16 @@ def rank_program(g, core, T, topo):
 
     def own_flags(t):
         o = DUM + 4 * BS * t
-        stubs(B("pc1", 0, 48), "tsb", 48)
-        move("s", B("bb"), B("pc1", 0, 48))
-        pe(chain(B("pf", 0, 48), [(Lm(a), B("wV", o + 4 * a + k, o + 4 * BS, 64)) for a in range(16) for k in range(4)], last=False))
-        pe(runs("bb", 48, ("ps0", "ps1"), 384, True, True))
+        pe(chain(B("pc0", 0, 48), [(B("I32"), B("ts", k, 192, 4)) for k in range(4)]))
+        move("s", B("be"), B("pc0", 0, 48))
+        for h in range(2):
+            pe(chain(B("ps%d" % h, 0, 384), [(B("I"), B("wV", o + 1536 * h + k, o + 1536 * h + 1536, 4)) for k in range(4)], last=False))
+        pe([(B("ps%d" % (a // 8), 48 * (a % 8), 48 * (a % 8) + 48), Lm(a, "LT"), B("be"), False, a % 8 == 7) for a in range(16)])
+
+    def own_table():
         for h in range(2):
             move("s", B("mn", 384 * h, 384 * h + 384), B("ps%d" % h, 0, 384))
-        pe(chain(B("pf", 0, 48), table("mn", 0, BS), first=False, last=False))
+        pe(chain(B("pf", 0, 48), table("mn", 0, BS), last=False))
 
     def flags_in(s):
         win = B("fr", FR * s, FR * s + FR)
@@ -491,8 +479,8 @@ def rank_program(g, core, T, topo):
         dma("sync", B("rowd", s * BS, s * BS + BS), B(buf, lo, lo + BS, parts=ROWS))
 
     def border_take(win):
-        take("s", B("sb", 0, 352), B(win, 0, P), B("sndu", 0, 22))
-        take("v", B("sb", 352, NB), B(win, 0, P), B("sndu", 22, 42))
+        take("v", B("sb", 0, CUT), B(win, 0, P), B("sndu", 0, 18))
+        take("s", B("sb", CUT, NB), B(win, 0, P), B("sndu", 18, 42))
 
     fill(B("gb"), 0.0)
     fill(B("BO"), 1.0)
@@ -503,8 +491,8 @@ def rank_program(g, core, T, topo):
     dma("sync", B("xw", BS, P), HB(T.x[:, BS:P]))
     dma("sync", B("tlb"), HB(T.tl[:, :]))
     dma("sync", B("pk", 0, BS), HB(T.cd[:, 0:BS]))
-    fill(B("L"), 0.0)
     fill(B("oz", Z0), 0.0)
+    fill(B("L"), 0.0)
     dma("sync", B("wV", DUM, DUM + 4 * BS, parts=ROWS), B("oz", Z0, Z0 + 192))
     dma("sync", B("wV", DUM + 12 * BS, DUM + 4 * P, parts=ROWS), B("oz", Z0, Z0 + 512))
     gsel(B("BO"), [[-16, 8], [0, 16]], OP.is_ge, 0, 1)
@@ -515,6 +503,8 @@ def rank_program(g, core, T, topo):
     gsel(B("I"), [[-1, 128]], OP.is_equal, 0, 1)
     giota(B("dk"), [[0, 4], [16, 64]], 0, 0)
     giota(B("wS", ER, ER + NB), [[1, NB]], 64, 0)
+    sfill(B("wS", INV, INV + BS), 64.0 + NB, B("oz", Z0))
+    sfill(B("wS", INV + BS, INV + 2 * BS), 64.0 + NB, B("oz", Z0))
     for a in range(16):
         act(B("L", 128 * a + a, 128 * a + 128, 16), B("BO", a, 128, 16), AF.Copy)
     ts(B("pj"), B("pi"), 15, OP.bitwise_and)
@@ -543,73 +533,73 @@ def rank_program(g, core, T, topo):
     op("vector", lambda e: e.reciprocal(T.sc[:, 0:1], T.tf[:, 0:1]), [B("sc", 0, 1)], [B("tf", 0, 1)])
     ts(B("Ds"), B("I"), B("sc", 0, 1), OP.mult)
     giota(B("id", 0, 2048), [[-1, 128], [0, 16]], 0, 1)
-    fill(B("zf"), 0.0)
+    giota(B("wS", S0 + DUM + 4 * P), [[0, 4 * NB]], 0, 0)
+    fill(B("ts"), 0.0)
     pack(0)
-    sfill(B("wS", INV, INV + 2 * BS), 64.0 + NB, B("L", 0, 2 * BS))
     act(IND(B("wS", INV, INV + 2 * BS + NB), B("invo", 0, 42)), B("wS", ER, ER + NB), AF.Silu)
-    members(0)
-    sfill(B("wV", DUM + 4 * P, DUM + 4 * P + 2048), 0.0, B("L"))
-    sfill(B("wV", DUM + 4 * P + 2048, FW), 0.0, B("L", 0, 4 * NB - 2048))
-    sfill(B("four"), 4.0, B("L", 0, U))
-    run([("o0", {"v": "LB LA LC VV LD", "t": "LM"})], out_calls(0))
-    pe(chain(B("pf", 0, 96), [(B("wS", 128 * a, 128 * a + 128), B("wS", INV + a, INV + 2 * BS, 16)) for a in range(16)]))
+    members(0, lambda: pe(chain(B("pf", 0, 96), [(B("wS", 128 * a, 128 * a + 128), B("wS", INV + a, INV + 2 * BS, 16)) for a in range(16)])))
+    for lo, hi in ((4 * P, 4 * P + 2048), (4 * P + 2048, 4 * W), (8 * BS, 10 * BS), (10 * BS, 12 * BS)):
+        sfill(B("wV", DUM + lo, DUM + hi), 0.0, B("L", 0, hi - lo))
+    run([("o0", {"v": "LB LC VV LA LD", "t": "LM"})], out_calls(0))
+    giota(B("wS", 0, U), [[0, U]], 4, 0)
     ts(B("E"), B("id", 0, 2048), 0.0, OP.is_equal)
     fill(B("oz", 0, Z0), 1.0)
     ts(B("dk"), B("dk"), 1.0 / 32768, OP.mult, 9.0, OP.add)
     for k in (3, 2, 1, 0):
-        dma("sync", B("wS", S0 + DUM + W * k, S0 + DUM + W * k + W, parts=ROWS), B("zf"), after=[rx])
+        dma("sync", B("wS", S0 + DUM + P * k, S0 + DUM + P * k + P, parts=ROWS), B("ts"), after=[rx])
     dma("sync", B("pk", BS, 2 * BS), HB(T.cd[:, BS:2 * BS]))
     dma("sync", B("Y", 0, P), HB(T.y0[:, :]))
-    fill(B("wV", DUM + 8 * BS, DUM + 12 * BS), 0.0)
-    gsel(B("I32"), [[-1, 128]], OP.is_equal, 0, 1, B("four", 0, 128))
+    dma("sync", B("pk", 0, BS), HB(T.cd[:, 2 * BS:3 * BS]))
+    for s in (2, 1):
+        old(s)
+    gsel(B("I32"), [[-1, 128]], OP.is_equal, 0, 1, B("wS", 0, 128))
     for h in range(2):
         gsel(B("LT", 1024 * h, 1024 * h + 1024), [[-1, 8], [-16, 8], [0, 16]], OP.is_equal, -8 * h, 1, B("oz", 0, 1024))
     giota(B("sm"), [[0, U]], 191, 0)
     gsel(B("sm"), [[0, 32], [1, 16]], OP.is_equal, 0, 0)
+    gsel(B("sx"), [[0, 32], [1, 16]], OP.not_equal, 0, 0, B("oz", 0, U))
     for s in range(2):
         giota(B("fr", FR * s + NB, FR * s + FR), [[0, 16]], 0, 0)
     giota(B("sdq"), [[0, 272]], 0, 0)
     dma("sync", B("rowd", 3 * BS, P), B("oz", Z0, Z0 + 128))
-    run([("o0", dict(OUT, v=" ".join(w for w in OUT["v"].split() if w[0] not in "LV"), t=OUT["t"].replace("LM ", "")))], out_calls(0))
-    ts(B("invT"), B("pf", 0, 96), 0.0625, OP.mult, -63.75, OP.add)
+    run([("o0", OUT0)], out_calls(0))
     border_flags(0)
     own_flags(1)
-    border_take("Y")
-    send("y0", "sb", "Y", P)
+    take("s", B("sb"), B("Y", 0, P), B("sndu", 0, 42))
     pack(1)
-    dma("sync", B("pk", 0, BS), HB(T.cd[:, 2 * BS:3 * BS]))
-    ts(B("N257"), B("N256"), 1.0, OP.add)
     back_list(0)
+    own_table()
+    ts(B("N257"), B("N256"), 1.0, OP.add)
     places(0)
     ts(B("H"), B("I"), 0.5, OP.mult)
-    ts(B("Qm"), B("I"), -0.25, OP.mult)
     flags_in(0)
+    do_waits("g", need_of("g", [("fr", 0, NB)], []))
+    send("y0", "sb", "Y", P)
     members(1)
-    for s in (2, 1):
-        old(s)
     for q in range(3):
         n = 272 if q < 2 else 224
-        dma("sync", B("sdq", 0, n, parts=slice(q, 128, 16)), HB(T.sd[:, 272 * q:272 * q + n]))
+        dma("sync", B("sdq", 0, n, parts=slice(q, 128, 16)), HB(T.sd[:, 272 * q:272 * q + n]), after=need_of("dma", [("P16", 0, 48)], []))
     run([("o1", OUT)], out_calls(1))
     border_flags(1)
     own_flags(2)
+    member_row(0, "id", 0)
     pack(2)
     back_list(1)
+    own_table()
     places(1)
-    for s in (0, 1):
-        member_row(s, "id", BS * s)
     flags_in(1)
+    member_row(1, "sf", 0)
     members(2)
 
-    run([("b2", BACK2), ("o2", {"s": "g0 g1 g2 g3"})], out_calls(2))
+    calls = out_calls(2)
+    calls["ROW"] = (lambda: (member_row(2, "gb", 0), dma("sync", B("mq"), B("rowd"))), ["PLACES"])
+    run([("b2", BACK2), ("o2", {"s": "g0 g1 g2 g3 g4 ROW"})], calls)
     stand(2)
     border_take("Y")
     ry = send("y1", "sb", "Y", P + NB)
     dma("sync", HB(T.yv[:, 2 * BS:3 * BS]), B("Y", 2 * BS, 3 * BS), after=[ry])
     old(0)
-    calls = out_calls(2)
-    calls["ROW"] = (lambda: (member_row(2, "gb", 0), dma("sync", B("mq"), B("rowd"))), [])
-    run([("o2", OUT2A), ("b1", BACK), ("o2", {"s": "g6 g7 s4 SDMA"})], calls)
+    run([("o2", OUT2A), ("b1", {"v": "g1"}), ("o2", {"v": "o2345"}), ("b1", dict(BACK, v=BACK["v"][3:])), ("o2", {"s": "s2 s3 s4"})], calls)
     stand(1)
     border_take("Y")
     ry = send("y2", "sb", "Y", P + 2 * NB)
@@ -623,24 +613,26 @@ def rank_program(g, core, T, topo):
     def own_sum():
         pe(chain(acc, [(B("I"), B(w, k, 1088, 4)) for w in ("fr", "zc1") for k in range(4)] + [(B("I"), B("sdq")), (B("I"), B("mq"))]))
 
+    def last():
+        tt(IND(B("xw", 0, P), B("sndu", 0, 42)), B("gb", 0, NB), B("sb"), OP.add)
+        dma("sync", HB(T.yf[:, :]), B("xw", 0, P, parts=ROWS))
+
     def own_end():
-        ts(B("yft"), acc, 0.5, OP.is_gt)
-        tt(B("yfo"), B("yft"), B("mq"), OP.add)
+        ts(B("yfo"), acc, 0.5, OP.is_gt)
+        tt(B("yfo"), B("yfo"), B("mq"), OP.add)
         dma("sync", B("xw", 0, P, parts=ROWS), B("yfo"))
 
     def arrived():
-        ts(B("sf"), B("sb"), 0.5, OP.is_lt, -1.0, OP.mult)
-        scan(B("ab", 0, NB), B("fr", 2 * FR, 2 * FR + NB), B("sf"), OP.min, OP.mult)
+        ts(B("sf", 0, NB), B("sb"), 0.5, OP.is_lt, -1.0, OP.mult)
+        scan(B("gb", 0, NB), B("fr", 2 * FR, 2 * FR + NB), B("sf", 0, NB), OP.min, OP.mult)
     calls.update({"B1": (lambda: (border_sum(0), border_sum(1)), ["TQ"]), "B2": (lambda: border_sign(0), ["B1"]),
                   "B3": (lambda: (border_sign(1), send("f2", "sf", "fr", 2 * FR, -1)), ["B1", "B2"]), "W": (lambda: None, ["B3"]),
                   "TQ": (all_rows, []), "OWN": (own_sum, ["TQ"]), "END": (own_end, ["OWN"]),
-                  "RG": (lambda: take("s", B("sb"), B("xw", 0, P), B("sndu", 0, 42)), ["END"]), "NEW": (arrived, ["RG"])})
+                  "RG": (lambda: take("s", B("sb"), B("xw", 0, P), B("sndu", 0, 42)), ["END"]), "NEW": (arrived, ["RG"]), "FIN": (last, [])})
     run([("o2", OUT2B), ("b0", BACK0)], calls)
     for h in range(2):
         take("s", B("Y", 384 * h, 384 * h + 384), B("zc0", 0, 1024), B("yp0", 24 * h, 24 * h + 24))
         dma("scalar", HB(T.yv[:, 384 * h:384 * h + 384]), B("Y", 384 * h, 384 * h + 384))
-    tt(IND(B("xw", 0, P), B("sndu", 0, 42)), B("ab", 0, NB), B("sb"), OP.add)
-    dma("sync", HB(T.yf[:, :]), B("xw", 0, P, parts=ROWS))
     totals.update(count)
     for s in sorted(totals):
         if known["g"].get(s, 0) < totals[s]:

@@ -11,7 +11,7 @@ S0 = 1024
 MAGIC = 12582912.0
 FR = NB + 16
 Z0 = 2 * U
-INV, ER = 2048, 4352
+INV, ER = 2048, 6400
 CUT = 3 * GB
 HALVES = ((0, CUT), (CUT, NB))
 
@@ -21,13 +21,13 @@ def _sb(n, d):
 
 
 _BF = {"xw": W, "Y": P + 3 * NB, "wV": FW, "L": 2048, "LT": 2048, "I": 128, "H": 128, "Ds": 128, "BO": 128, "NU": 128, "ga": 8 * U, "mn": 8 * U,
-       "id": 8 * U, "sm": U, "sx": U, "oz": Z0 + BS, "tlb": 1, "fr": 3 * FR, "sf": BS, "sb": NB, "gb": BS, "sdq": 272,
-       "mq": 272, "yfo": 272, "F": 48, "cs": 48, "dd": 256, "be": 48}
+       "id": 8 * U, "sm": 2 * U, "oz": Z0 + BS, "tlb": 1, "fr": 3 * FR, "sf": BS, "sb": NB, "gb": BS, "sdq": 272,
+       "mq": 272, "yfo": 272, "F": 48, "cs": 48, "dd": 256, "be": 48, "Fo": 48, "M": NB, "D": 16}
 _F16 = {"E": 2048}
 _F32 = {"wS": S0 + FW, "I32": 128, "ts": 272, "NF": 48, "A": 48, "q1": 48, "q2": 48, "q3": 48, "N769": 48,
         "N257": 48, "N256": 48, "pf15": 8, "tf": 8, "sc": 8, "dk": 256, "vv": 256, "t1": 256, "t2": 256}
-_I32 = {"pk": 2 * BS, "pkw": 1544, "dum": 256, "ta": 256, "tb": 256, "sndi": 42, "pi": 8, "pj": 8}
-_U16 = {"invT": 96, "sndu": 48, "P16": 48, "ou": 256, "invo": 48}
+_I32 = {"pk": 2 * BS, "pkw": 1544, "tb": 256, "sndi": 42, "pi": 8, "pj": 8, "sn": 42, "ar": 16}
+_U16 = {"invT": 96, "sndu": 48, "P16": 48, "ou": 256, "rs": 48, "rr": 48}
 for _s in range(3):
     _BF.update({"zc%d" % (_s % 2): 1088, "xm%d" % _s: 256})
     _F16.update({"nx%d" % _s: 256})
@@ -38,43 +38,38 @@ SCRATCH = {}
 for _t, _d in ((_BF, "bfloat16"), (_F16, "float16"), (_F32, "float32"), (_I32, "int32"), (_U16, "uint16")):
     SCRATCH.update({_n: _sb(_c, _d) for _n, _c in _t.items()})
 SCRATCH["rowd"] = ("dram", [8, P], "bfloat16")
-PSUMS = ["ps0", "ps1", "ps2", "pc0", "pc1", "pr0", "pr1", "pf"]
+PSUMS = {"ps": 4 * U, "pc0": U, "pc1": U, "pr0": U, "pr1": U}
 for _n in PSUMS:
-    SCRATCH[_n] = ("psum", [128, 512], "float32")
+    SCRATCH[_n] = ("psum", [128, PSUMS[_n]], "float32")
 NDMA = 44
-EXCH = ["x", "f0", "f1", "f2", "y0", "y1", "y2"]
+EXCH = ["n", "x", "f0", "f1", "f2", "y0", "y1", "y2"]
+ONE = []
 SEMAPHORES = ["sv", "sa", "st", "sg"] + ["d%d" % k for k in range(NDMA)] + ["r_" + e for e in EXCH] + ["l_" + e for e in EXCH]
 
-OUT = {"v": "LB LA g1 LC n0 LD n1 g6 n2 VV n3 n4 o01 n5 o23 s3 o45 n6 n7 s5 o67 s6 s7",
-       "s": "g0 g2 g3 g4 g5 g7 s0 s1 s2 s4 SDMA K0 K1 K2",
-       "t": "d0 d1 LM d2 d3 c01 d4 d5 c23 c45 d6 d7 c67 J3 J0 J1 J2"}
-OUT0 = {"v": "g1 INV n0 n1 g6 n2 n3 o01 n4 n5 o23 s3 o45 n6 n7 s5 o67 s6 s7", "s": OUT["s"], "t": OUT["t"].replace("LM ", "")}
-BACK = {"v": "g1 g2 n0 n1 n2 m0 n3 n4 m1 n5 m2 m3 n6 m4 n7 m5 m6 m7 y012345 z012345 y67 z67",
-        "s": "g0 g3 g4 g5 g6 g7",
-        "t": "d0 d1 d2 d3 d4 d5 d6 d7 c012345 h67 e012345 c67 e67"}
-BACK2 = {"v": "LB LA g1 LC n0 LD n1 n2 m0 n3 n4 m1 n5 m2 m3 n6 m4 n7 PLACES" + BACK["v"].split("n7")[1],
-         "s": "g0 g2 g3 g4 g5 g6 g7", "t": BACK["t"].replace("d1", "d1 LM")}
-OUT2A = {"v": "n0 n1 n2 VV n3 o01 n4 n5 n6 n7",
-         "s": "g5 g6 g7 s0 s1",
-         "t": "d0 d1 d2 d3 c01 d4 d5 d6 d7 c2345"}
-OUT2B = {"v": "o67 s6 s7 TQ",
-         "s": "s5 SDMA K0 K1 K2",
-         "t": "c67 J3 J0 J1 J2 B1"}
-BACK0 = {"v": "B2 g1 g2 n0 n1 n2 m0 n3 END n4 m1 n5 m2 m3 n6 m4 n7 m5 m6 m7 NEW y012345 z012345 y67 z67 FIN",
-         "s": "g0 B3 g3 g4 g5 g6 g7 RG",
-         "t": BACK["t"].replace("d3", "d3 OWN").replace("e012345", "W e012345")}
+OUT = {"v": "LB LA LC LD g3 n01 VV n23 n45 o01 n67 o2345 s3 o67 s5 s67",
+       "s": "g0 g1 g2 g4 g5 g6 g7 s0 s1 s2 s4 SDMA K0 K1 K2",
+       "t": "d0 LM d1 d2 d3 d4 d5 c01 d6 d7 c2345 c67 J3 J0 J1 J2"}
+OUT0 = {"v": "g1 g2 INV n01 VV n23 o01 n45 n67 o2345 s3 o67 s5 s67", "s": "g0 g3 g4 g5 g6 g7 MASK s0 s1 s2 s4 SDMA K0 K1 K2",
+        "t": "d0 d1 d2 d3 c01 d4 d5 d6 d7 c2345 c67 J3 J0 J1 J2"}
+BACK = {"v": "b2: LB LA LC g3 LD n01 n23 m01 n45 m23 PLACES m45 m67 y012345 y67 z012345 VV z67 N21 T20 Y2 o2: n01 n23 o01 n45 n67 b1: g1 g2 o2: o2345 "
+             "b1: n01 n23 m23 n45 m01 n67 m45 y012345 m67 y67 z012345 z67 N11 T10 Y1 o2: o67 s5 s67 TQ B2 "
+             "b0: g1 g3 n01 END n23 n45 m01 m23 m45 m67 NEW y012345 FIN y67 z012345 z67 N01",
+        "s": "b2: g0 g1 g2 g4 g5 g6 g7 o2: g0 b2: a67 n67 o2: g1 g2 g3 N20 T21 g4 g5 g6 g7 ROW s0 s1 b1: g0 g3 g4 g5 g6 g7 o2: s2 s3 s4 SDMA N10 T11 K0 K1 K2 "
+             "b0: g0 B3 g2 g4 g5 g6 g7 RG a67 n67 N00",
+        "t": "b2: d0 LM d1 d2 d3 d4 d5 d6 d7 c012345 c67 e012345 e67 o2: d0 d1 d2 d3 c01 d4 d5 d6 d7 c2345 "
+             "b1: d0 d1 d2 d3 d4 d5 d6 d7 c012345 c67 e012345 e67 o2: c67 J3 J0 J1 J2 OWN0 B1 b0: d0 d1 OWN d2 d3 d4 d5 d6 d7 c012345 e012345 c67 e67"}
 
 
-def exchange_plan(topo, cores, r, sg):
+def exchange_plan(topo, cores, r, sg, one=False):
     src = cores[r]
     dst = [None] + [cores[(r + sg * d) % NR] for d in range(1, NR)]
     off = [d for d in range(1, NR) if topo.chip(dst[d]) != topo.chip(src)]
     eng = topo.engines(src, dst[off[0]])
     q = len(eng) // 4
     calls = []
-    for k, ds in enumerate((range(1, 4), range(4, NR))):
+    for k, ds in enumerate((range(1, NR),) if one else (range(1, 4), range(4, NR))):
         mine = [d for d in ds if d in off]
-        sizes = {4: [q, q, q, q], 2: [2 * q, 2 * q], 3: [q, q, 2 * q] if k == 0 else [2 * q, q, q]}[len(mine)]
+        sizes = {6: [q // 2] * 4 + [q, q], 4: [q, q, q, q], 2: [2 * q, 2 * q], 3: [q, q, 2 * q] if k == 0 else [2 * q, q, q]}[len(mine)]
         call, at = [], 0
         for d, n in zip(mine, sizes):
             call.append((d, eng[at:at + n]))
@@ -102,6 +97,8 @@ def rank_program(g, core, T, topo):
         lo = 0 if lo is None else lo
         hi = SCRATCH[name][1][1] if hi is None else hi
         ap = T[name][:, lo:hi:st] if parts is None else T[name][parts, lo:hi:st]
+        if name in PSUMS:
+            lo, hi = lo // U * U, -(-hi // U) * U
         return {"ap": ap, "r": [(name, lo, hi)], "x": []}
 
     def IND(win, off):
@@ -116,7 +113,7 @@ def rank_program(g, core, T, topo):
             name, lo, hi = acc
             psum = name in PSUMS
             for rec in recs.get(name, []):
-                if (rec["hi"] <= lo or rec["lo"] >= hi) and not psum:
+                if rec["hi"] <= lo or rec["lo"] >= hi:
                     continue
                 if rec["q"] == q and q == "tensor":
                     continue
@@ -141,7 +138,7 @@ def rank_program(g, core, T, topo):
 
     def record(q, tok, reads, writes):
         for name, lo, hi in writes:
-            keep = [x for x in recs.get(name, []) if not (name in PSUMS or (x["lo"] >= lo and x["hi"] <= hi))]
+            keep = [x for x in recs.get(name, []) if not (x["lo"] >= lo and x["hi"] <= hi)]
             recs[name] = keep + [{"lo": lo, "hi": hi, "w": True, "tok": tok, "q": q}]
         for name, lo, hi in reads:
             recs.setdefault(name, []).append({"lo": lo, "hi": hi, "w": False, "tok": tok, "q": q})
@@ -166,10 +163,11 @@ def rank_program(g, core, T, topo):
         clk[s] = totals[s] = 16
         record("dma", {"sem": s, "val": 16, "clk": clk}, in_["r"], out["r"])
 
-    def send(name, src, land, at, sg=1):
+    def send(name, src, land, at, sg=1, GB=GB):
+        NB = 7 * GB
         ls, rs = "l_" + name, "r_" + name
         done, pend, clk = 0, [], {}
-        for call in exchange_plan(topo, cores, rank, sg):
+        for call in exchange_plan(topo, cores, rank, sg, name in ONE):
             tr, reads = [], []
             for d, es in call:
                 to = cores[(rank + sg * d) % NR]
@@ -185,7 +183,7 @@ def rank_program(g, core, T, topo):
             clk = dict(known["g"])
         clk[ls] = totals[ls] = done
         record("g", {"sem": ls, "val": done, "clk": clk}, pend, [])
-        n = sum(len(es) for q in range(NR) if q != rank for call in exchange_plan(topo, cores, q, sg) for d, es in call if (q + sg * d) % NR == rank)
+        n = sum(len(es) for q in range(NR) if q != rank for call in exchange_plan(topo, cores, q, sg, name in ONE) for d, es in call if (q + sg * d) % NR == rank)
         totals[rs] = n
         rt = {"sem": rs, "val": n, "clk": {rs: n}}
         recs[land] = [x for x in recs.get(land, []) if not (x["lo"] >= at and x["hi"] <= at + NB)] + [{"lo": at, "hi": at + NB, "w": True, "tok": rt, "q": "ext"}]
@@ -256,8 +254,7 @@ def rank_program(g, core, T, topo):
         tt(o, o, B("xw", s * BS, s * BS + BS), OP.add)
 
     def places_of(s, lo, hi):
-        ts(B("ta", lo, hi), B("pkw", 1 + lo, 1 + hi), 10, OP.arith_shift_right)
-        copy(B("cu%d" % s, lo, hi), B("ta", lo, hi))
+        ts(B("cu%d" % s, lo, hi), B("pkw", 1 + lo, 1 + hi), 1.0 / 1024, OP.mult, -0.499, OP.add)
 
     def marks_of(s, h):
         lo, hi = 128 * h, 128 * h + 128
@@ -270,15 +267,17 @@ def rank_program(g, core, T, topo):
     def scaled(s, h):
         ts(B("nx%d" % s, 128 * h, 128 * h + 128), B("pr%d" % h, 0, 128), -1.0, OP.mult)
 
-    def members(s, beside=lambda: None):
-        pf = B("pf", 0, 48)
-        ts(B("F"), pf, 0.5, OP.is_gt)
-        scan(B("cs"), B("oz", Z0, Z0 + 48), B("F"), OP.add, OP.add)
-        ts(B("NF"), pf, 0.5, OP.is_le)
+    def positions(s):
+        scan(B("cs"), B("oz", Z0, Z0 + 48), B("F"), OP.add, OP.subtract)
         pe(chain(B("pc0", 0, 48), [(B("BO"), B("cs")), (B("NU"), B("F"))]))
+        ts(B("NF"), B("F"), 1.0, OP.add)
         tt(B("A"), B("NF"), B("N769"), OP.mult)
         tt(B("P32_%d" % s), B("pc0", 0, 48), B("A"), OP.max)
         copy(B("P16"), B("P32_%d" % s))
+
+    def members(s, beside=lambda: None):
+        if s:
+            positions(s)
         copy(IND(B("pkw"), B("P16")), B("pk", s % 2 * BS, s % 2 * BS + BS))
         places_of(s, 0, 64)
         marks_of(s, 0)
@@ -290,10 +289,13 @@ def rank_program(g, core, T, topo):
         ts(B("vv", lo, hi), B("tb", lo, hi), 1.0 / 32768, OP.mult, 9.0 + DUM / 32768, OP.add)
 
     def back_list(s):
-        ts(B("t1"), B("ta"), P - 0.5, OP.is_ge, float(NB * (2 - s)), OP.mult)
-        tt(B("t2"), B("t1"), B("ta"), OP.add)
-        copy(B("cb%d" % s), B("t2"))
-        copy(B("pkw", 1, 257), B("dum"))
+        ts(B("t1"), B("pkw", 1, 257), 1024.0 * P, OP.is_ge, 1024.0 * NB * (2 - s), OP.mult)
+        tt(B("t2"), B("t1"), B("pkw", 1, 257), OP.add)
+        ts(B("cb%d" % s), B("t2"), 1.0 / 1024, OP.mult, -0.499, OP.add)
+        absent()
+
+    def absent():
+        giota(B("pkw", 1, 257), [[0, 256]], -256 * DUM, 0)
 
     def places(s):
         p = B("P32_%d" % s)
@@ -303,110 +305,107 @@ def rank_program(g, core, T, topo):
         tt(B("q2"), B("q3"), B("N256"), OP.add)
         copy(B("yp%d" % s), B("q2"))
 
-    RING = {"ga": 8, "ps": 3, "pc": 2, "pz": 2}
-    turn, holder, slot, made, of = {r: 0 for r in RING}, {}, {}, set(), {}
+    turn, holder, slot, made, sized, signed = [0], {}, {}, set(), set(), set()
 
     def aside(st, u):
         return st == "o2" and u >= 6
 
     def ready(st, c, us):
-        u, back = us[0], st[0] == "b"
-        call = lambda k, u: (k, of[(st, k, u)])
-        rows = (st, "r", u) in of
+        back, first = st[0] == "b", "a" if (st, us[0]) in sized else "n"
+        near = lambda: {} if aside(st, us[0]) else {("id", u): ["c"] for u in us}
         if c == "g":
-            return [], ("ga", [("d", us)] + ([("m", us)] if back else []))
+            return "", {("ga", u): ["d", "m"][:1 + back] for u in us}
         if c == "d":
-            return [("g", us)], ("ps", [("n", us)])
-        if c == "n":
-            return [("d", us)], None if aside(st, u) else ("id", [("y", us) if rows else call("c", u)])
+            return "g", {("ps", us[0] % 4): [first]}
+        if c == first:
+            return "d", near()
         if c == "m":
-            return [("g", us)], ("mn", [call("e", u)])
-        if c == "c" and (st, "h", u) in of:
-            return [("h", us)], None
-        if c in "chr":
-            return [("n", (k,)) for k in us], ("pc", [("x" if rows else "y" if back else "o", us)])
-        if c in "oyx":
-            return [("x" if rows and c == "y" else "r" if rows else "c", us)], None
-        if c == "s":
-            return [call("o", k) for k in us], None
-        if c == "e":
-            return [call("y", k) for k in us] + [("m", (k,)) for k in us], ("pz", [("z", us)])
-        return [("e", us)], None
+            return "g", {("mn", u): ["e"] for u in us}
+        if c == "h" or c == "c" and (st, "h", us[0]) not in made:
+            return "n", {("pc", turn[0]): ["y" if back else "o"]}
+        return {"n": "a", "c": "h", "o": "c", "y": "c", "s": "o", "e": "ym", "z": "e"}[c], {}
 
     def issue(st, q, c, us):
         s, back, u, n = int(st[1]), st[0] == "b", us[0], len(us)
         m0, m1 = 32 * u, 32 * (u + n)
-        ga = lambda: B("ga", U * slot[(st, "ga", us)], U * slot[(st, "ga", us)] + U)
-        bank = lambda ring, w: B({"pz": "pr"}.get(ring, ring) + str(slot[(st, ring, us)]), 0, w)
-        unit = lambda buf: B(buf, U * u, U * u + U)
+        units = lambda buf, k=u: B(buf, U * k, U * (k + n))
+        near = units("LT", u - 6) if aside(st, u) else units("id")
+        cnt = lambda: B("pc%d" % slot[(st, u)], 0, 32 * n)
         if c == "g":
             win = B("Y", 0, P + NB * (3 - s)) if back else B("xw")
-            take(q, ga(), win, B(("cb%d" if back and s < 2 else "cu%d") % s, m0, m1))
+            take(q, units("ga"), win, B(("cb%d" if back and s < 2 else "cu%d") % s, m0, m1))
         elif c == "d":
-            h, e = 128 * (u // 4), U * (u % 4)
-            pe(chain(bank("ps", U), [(B("nx%d" % s, h, h + 128), B("E", e, e + U)), (B("Ds"), ga())]))
+            pe(chain(units("ps", u % 4), [(B("nx%d" % s, 128 * (u // 4), 128 * (u // 4) + 128), units("E", u % 4)), (B("Ds"), units("ga"))]))
+        elif c == "a":
+            act(near, units("ps", u % 4), AF.Abs)
+        elif c == "n" and q == "s":
+            act(near, near, AF.Sign, scale=-1.0, bias=0.499)
+        elif c == "n" and (st, u) in sized:
+            ts(near, near, 0.5, OP.is_lt)
         elif c == "n":
-            ts(B("LT", U * (u - 6), U * (u - 5)) if aside(st, u) else unit("id"), bank("ps", U), MAGIC, OP.add, MAGIC, OP.is_equal)
+            ts(near, units("ps", u % 4), MAGIC, OP.add, MAGIC, OP.is_equal)
         elif c == "m":
-            scan(unit("mn"), B("sm"), ga(), OP.max, OP.min)
+            scan(units("mn"), B("sm", 0, U * n), units("ga"), OP.max, OP.min)
         elif c in "hc":
-            mm = chain(bank("pc", 32 * n), table("LT", 0, U * n) if aside(st, u) else table("id", U * u, U * n))
-            pe(mm[:8] if c == "h" else mm[8:] if (st, "h", u) in of else mm)
-        elif c == "r":
-            pe(chain(bank("pc", U), [(B("BO"), unit("id"))]))
-        elif c == "x":
-            scan(unit("id"), B("sx"), bank("pc", U), OP.mult, OP.max)
+            mm = chain(cnt(), table(*near["r"][0][:2], U * n))
+            pe(mm[:8] if c == "h" else mm[8:] if (st, "h", u) in made else mm)
         elif c == "o":
-            tt(B("t1", m0, m1), bank("pc", 32 * n), B("vv", m0, m1), OP.min)
+            tt(B("t1", m0, m1), cnt(), B("vv", m0, m1), OP.min)
             tt(B("t2", m0, m1), B("t1", m0, m1), B("dk", m0, m1), OP.max)
             ts(B("ou", m0, m1), B("t2", m0, m1), -9.0, OP.add, 32768.0, OP.mult)
         elif c == "s" and q == "v":
             copy(IND(B("wV"), B("ou", m0, m1)), B("oz", 0, U * n))
         elif c == "s":
+            assert "SDMA" not in made
             act(IND(B("wS", S0), B("ou", m0, m1)), B("wS", 0, U * n), AF.Silu)
         elif c == "y":
-            cnt = B("id", U * u + 15, U * u + U, 16) if (st, "r", u) in of else bank("pc", 32 * n)
-            ts(B("dd", m0, m1), cnt, 9.5, OP.is_ge, 255.0, OP.mult)
+            ts(B("dd", m0, m1), cnt(), 3.0 if (st, u) in signed else 9.5, OP.is_ge, 255.0, OP.mult)
         elif c == "e":
-            pe(chain(bank("pz", 32 * n), [(B("H"), B("xm%d" % s, m0, m1)), (B("H"), B("mn", U * u + 15, U * (u + n), 16)), (B("BO"), B("dd", m0, m1))]))
+            pe(chain(B("pr0", m0, m1), [(B("H"), B("xm%d" % s, m0, m1)), (B("H"), B("mn", U * u + 15, U * (u + n), 16)), (B("BO"), B("dd", m0, m1))]))
         elif c == "z":
-            ts(B("t1", m0, m1), bank("pz", 32 * n), -0.25, OP.add, MAGIC, OP.add)
+            ts(B("t1", m0, m1), B("pr0", m0, m1), -0.25, OP.add, MAGIC, OP.add)
             ts(B("zc%d" % (s % 2), m0, m1), B("t1", m0, m1), MAGIC, OP.subtract, 255.0, OP.min)
 
-    def run(parts, own):
+    def run(lists, own, st=None, behind={}):
         todo = {q: [] for q in "vst"}
-        for st, ls in parts:
-            for q in ls:
-                for w in ls[q].split():
-                    us = () if w[0].isupper() else tuple(int(k) for k in w[1:])
-                    todo[q].append((st, w if not us else w[0], us))
-                    of.update({(st, w[0], k): us for k in us})
+        for q in lists:
+            for w in lists[q].split():
+                if w[-1] == ":":
+                    st = w[:-1]
+                    continue
+                us = () if w[0].isupper() else tuple(int(k) for k in w[1:])
+                todo[q].append((st, w if not us else w[0], us))
+                sized.update((st, u) for u in us if w[0] == "a")
+                signed.update((st, u) for u in us if w[0] == "n" and q == "s")
+        names = {c for q in todo for st, c, us in todo[q] if not us}
         while any(todo.values()):
             moved = False
             for q in "svt":
                 while todo[q]:
                     st, c, us = todo[q][0]
                     if not us:
-                        if not all(any((x, b, ()) in made for x in (st, "b2", "o2", "b0")) for b in own[c][1]):
+                        if not all(b in made for b in own[c][1]):
                             break
-                        own[c][0]()
+                        own[c][0](q)
+                        made.add(c)
                     else:
-                        before, ring = ready(st, c, us)
-                        w = {"d": "LA" if us[0] < 4 else "LD", "g": "LB" if us[0] > 1 else ""}.get(c)
-                        if (st, w, ()) in todo["v"] or not all((st, b, k) in made for b, k in before):
+                        before, takes = ready(st, c, us)
+                        first = [{"d": "LA" if us[0] < 4 else "LD", "g": "LB" if us[-1] > 1 else "", "o": "VV"}.get(c)] + behind.get((st, c), [])
+                        if any(w in names and w not in made for w in first) or not all((st, b, u) in made for b in before for u in us):
                             break
-                        if ring:
-                            k = turn.get(ring[0], us[0])
-                            if not all(x in made for x in holder.get((ring[0], k), [])):
-                                break
-                            slot[(st, ring[0], us)] = k
-                            holder[(ring[0], k)] = [(st, b, j) for b, j in ring[1]]
-                            if ring[0] in RING:
-                                turn[ring[0]] = (k + 1) % RING[ring[0]]
+                        if not all(x in made for k in takes for x in holder.get(k, [])):
+                            break
+                        for k, after in takes.items():
+                            holder[k] = [(st, b, k[1] if k[0] in ("ga", "id", "mn") else us[0]) for b in after]
+                            if k[0] == "pc":
+                                slot[(st, us[0])] = turn[0]
+                                turn[0] = 1 - turn[0]
                         issue(st, q, c, us)
-                    made.add(todo[q].pop(0))
+                        made.update((st, c, u) for u in us)
+                    todo[q].pop(0)
                     moved = True
             assert moved, todo
+        made.difference_update(own)
 
     def s_rows(s):
         if s < 2:
@@ -424,12 +423,13 @@ def rank_program(g, core, T, topo):
                 pe([(B("pr%d" % h, 0, b - a), B("I32"), B("wS", o + 4 * a + 3, o + 4 * b, 4), True, False) for h, (a, b) in enumerate(HALVES)])
             else:
                 pe([(B("pr%d" % h, 0, b - a), B("I"), B("mn", 1024 * k + a, 1024 * k + b), False, False) for h, (a, b) in enumerate(HALVES)])
-        stubs = {"K%d" % k: (lambda k=k: narrow(k), []) for k in range(3)}
-        stubs.update({"J%d" % k: (lambda k=k: add(k), ["K%d" % k, "J3"] if k < 3 else ["SDMA"]) for k in range(4)})
-        return {**stubs, "LA": (lambda: scaled(s, 0), []), "LB": (lambda: places_of(s, 64, 256), []), "LC": (lambda: marks_of(s, 1), []),
-                "LM": (lambda: turned(s, 1), ["LC"]), "LD": (lambda: scaled(s, 1), ["LM"]), "VV": (lambda: numbers(0, 256), []), "SDMA": (lambda: s_rows(s), []),
-                "PLACES": (lambda: places(s), []),
-                "INV": (lambda: ts(B("invT"), B("pf", 0, 96), 0.0625, OP.mult, -63.75, OP.add), [])}
+        stubs = {"K%d" % k: (lambda q, k=k: narrow(k), ["SDMA"]) for k in range(3)}
+        stubs.update({"J%d" % k: (lambda q, k=k: add(k), ["K%d" % k, "J3"] if k < 3 else ["SDMA"]) for k in range(4)})
+        return {**stubs, "LA": (lambda q: scaled(s, 0), []), "LB": (lambda q: places_of(s, 64, 256), []), "LC": (lambda q: marks_of(s, 1), []),
+                "LM": (lambda q: turned(s, 1), ["LC"]), "LD": (lambda q: scaled(s, 1), ["LM"]), "VV": (lambda q: numbers(0, 256), []),
+                "SDMA": (lambda q: s_rows(s), []), "PLACES": (lambda q: places(s), []),
+                "MASK": (lambda q: take(q, B("M"), B("D"), B("rr", 0, 42)), []),
+                "INV": (lambda q: ts(B("invT"), B("ps", 3 * U, 3 * U + 96), 0.0625, OP.mult, -63.75, OP.add), [])}
 
     def border_sum(h):
         o, (a, b) = DUM + 4 * P, HALVES[h]
@@ -442,34 +442,44 @@ def rank_program(g, core, T, topo):
             act(B("sf", CUT, NB), B("pr1", 0, NB - CUT), AF.Sign, scale=-1.0)
 
     def border_flags(s):
-        for h in range(2):
+        for h, (a, b) in enumerate(HALVES):
             border_sum(h)
-            border_sign(h)
+            tt(B("sf", a, b), B("pr%d" % h, 0, b - a), B("M", a, b), OP.min)
         send("f%d" % s, "sf", "fr", FR * s, -1)
 
     def own_flags(t):
         o = DUM + 4 * BS * t
-        pe(chain(B("pc0", 0, 48), [(B("I32"), B("ts", k, 192, 4)) for k in range(4)]))
+        dma("sync", B("dd", 0, 192), B("wV", o, o + 4 * BS, parts=ROWS))
+        pe(chain(B("pc0", 0, 48), [(B("I32"), B("ts", k, 192, 4)) for k in range(4)], last=False))
+        pe(chain(B("pc0", 0, 48), [(B("I"), B("dd", k, 192, 4)) for k in range(4)], first=False))
+
+    def own_runs():
         move("s", B("be"), B("pc0", 0, 48))
-        for h in range(2):
-            pe(chain(B("ps%d" % h, 0, 384), [(B("I"), B("wV", o + 1536 * h + k, o + 1536 * h + 1536, 4)) for k in range(4)], last=False))
-        pe([(B("ps%d" % (a // 8), 48 * (a % 8), 48 * (a % 8) + 48), Lm(a, "LT"), B("be"), False, a % 8 == 7) for a in range(16)])
+        pe([(B("ps", U * (a // 8) + 48 * (a % 8), U * (a // 8) + 48 * (a % 8) + 48), Lm(a, "LT"), B("be"), True, True) for a in range(16)])
 
     def own_table():
+        own_runs()
         for h in range(2):
-            move("s", B("mn", 384 * h, 384 * h + 384), B("ps%d" % h, 0, 384))
-        pe(chain(B("pf", 0, 48), table("mn", 0, BS), last=False))
+            move("s", B("mn", 384 * h, 384 * h + 384), B("ps", U * h, U * h + 384))
+        pe(chain(B("pc1", 0, 48), table("mn", 0, BS)))
+
+    def flagged(out):
+        ts(B(out), B("pc1", 0, 48), 0.5, OP.is_gt, -1.0, OP.mult)
 
     def flags_in(s):
+        flagged("Fo")
         win = B("fr", FR * s, FR * s + FR)
         o = 48 * s
         act(B("gb", 0, 384), IND(win, B("invT", o, o + 24)), AF.Copy, scale=-1.0)
         ts(B("gb", 384, BS), IND(win, B("invT", o + 24, o + 48)), -1.0, OP.mult)
-        pe(chain(B("pf", 0, 48), table("gb", 0, BS), first=False))
+        scan(B("ga", 0, BS), B("sm", 0, BS), B("gb"), OP.add, OP.min)
+        tt(B("F"), B("Fo"), B("ga", 15, BS, 16), OP.min)
 
-    def stand(s):
-        take("s", B("Y", BS * s, BS * s + 384), B("zc%d" % (s % 2), 0, 1024), B("yp%d" % s, 0, 24))
-        take("v", B("Y", BS * s + 384, BS * s + BS), B("zc%d" % (s % 2), 0, 1024), B("yp%d" % s, 24, 48))
+    def stand(q, s, h):
+        lo = BS * s + 384 * h
+        take(q, B("Y", lo, lo + 384), B("zc%d" % (s % 2), 0, 1024), B("yp%d" % s, 24 * h, 24 * h + 24))
+        if s == 0:
+            dma("scalar" if q == "s" else "sync", HB(T.yv[:, lo:lo + 384]), B("Y", lo, lo + 384))
 
     def old(s):
         dma("sync", B("zc%d" % (s % 2), 256, 1024), HB(T.y0[:, s * BS:s * BS + BS]))
@@ -478,75 +488,72 @@ def rank_program(g, core, T, topo):
         take("s", B(buf, lo, lo + BS), B("oz", Z0 - 256, Z0 + BS), B("yp%d" % s))
         dma("sync", B("rowd", s * BS, s * BS + BS), B(buf, lo, lo + BS, parts=ROWS))
 
-    def border_take(win):
-        take("v", B("sb", 0, CUT), B(win, 0, P), B("sndu", 0, 18))
-        take("s", B("sb", CUT, NB), B(win, 0, P), B("sndu", 18, 42))
+    def border_take(q, win, h):
+        a, b = HALVES[h]
+        take(q, B("sb", a, b), B(win, 0, P), B("sndu", a // 16, b // 16))
 
+    dma("sync", B("sndi"), HB(T.snd[:, :]))
+    dma("sync", B("tlb"), HB(T.tl[:, :]))
+    dma("sync", B("xw", 0, BS), HB(T.x[:, 0:BS]))
     fill(B("gb"), 0.0)
     fill(B("BO"), 1.0)
-    fill(B("I"), 1.0)
-    dma("sync", B("sndi"), HB(T.snd[:, :]))
-    dma("sync", B("xw", 0, BS), HB(T.x[:, 0:BS]))
     dma("sync", B("gb", parts=ROWS), HB(T.sd[:, :]))
     dma("sync", B("xw", BS, P), HB(T.x[:, BS:P]))
-    dma("sync", B("tlb"), HB(T.tl[:, :]))
     dma("sync", B("pk", 0, BS), HB(T.cd[:, 0:BS]))
-    fill(B("oz", Z0), 0.0)
     fill(B("L"), 0.0)
-    dma("sync", B("wV", DUM, DUM + 4 * BS, parts=ROWS), B("oz", Z0, Z0 + 192))
-    dma("sync", B("wV", DUM + 12 * BS, DUM + 4 * P, parts=ROWS), B("oz", Z0, Z0 + 512))
+    fill(B("I"), 1.0)
     gsel(B("BO"), [[-16, 8], [0, 16]], OP.is_ge, 0, 1)
     gsel(B("BO"), [[16, 8], [0, 16]], OP.is_ge, 15, -1)
     giota(B("pi"), [[0, 8]], 0, 1)
-    gsel(B("NU"), [[-1, 128]], OP.is_gt, 0, 1, B("BO"))
     giota(B("N256"), [[16, 48]], 256, 0)
+    giota(B("ar"), [[1, 16]], 0, 0)
+    gsel(B("NU"), [[-1, 128]], OP.is_gt, 0, 1, B("BO"))
+    fill(B("pkw", 1, 257), -256 * DUM)
+    ts(B("sn"), B("sndi"), 15, OP.bitwise_and)
+    copy(B("rs", 0, 42), B("sn"))
+    send("n", "rs", "rr", 0, 1, GB // 16)
     gsel(B("I"), [[-1, 128]], OP.is_equal, 0, 1)
-    giota(B("dk"), [[0, 4], [16, 64]], 0, 0)
     giota(B("wS", ER, ER + NB), [[1, NB]], 64, 0)
-    sfill(B("wS", INV, INV + BS), 64.0 + NB, B("oz", Z0))
-    sfill(B("wS", INV + BS, INV + 2 * BS), 64.0 + NB, B("oz", Z0))
     for a in range(16):
         act(B("L", 128 * a + a, 128 * a + 128, 16), B("BO", a, 128, 16), AF.Copy)
+    sfill(B("wS", INV + BS, INV + 3 * BS), 64.0 + NB, B("L", 0, 2 * BS))
+    copy(B("sndu", 0, 42), B("sndi"))
     ts(B("pj"), B("pi"), 15, OP.bitwise_and)
     copy(B("pf15"), B("pj"))
-    ts(B("NU"), B("NU"), -1.0, OP.mult)
     ts(B("N256"), B("N256"), B("pf15", 0, 1), OP.add)
-    copy(B("sndu", 0, 42), B("sndi"))
-    fill(B("wV", DUM + 4 * BS, DUM + 8 * BS), 0.0)
     ts(B("N769"), B("N256"), 513.0, OP.add)
-    act(B("wS", 0, 2048), B("L"), AF.Copy)
-    pe(chain(B("pf", 0, 48), table("gb", 0, BS)))
-    ts(B("q1", 0, 42), B("sndi"), BS - 0.5, OP.is_ge)
-    ts(B("q2", 0, 42), B("sndi"), 3 * BS - 0.5, OP.is_lt)
-    ts(B("q3", 0, 42), B("N256", 0, 42), float(3 * BS - 256), OP.add)
-    tt(B("q1", 0, 42), B("q1", 0, 42), B("q2", 0, 42), OP.mult)
-    tt(B("q2", 0, 42), B("sndi"), B("q3", 0, 42), OP.subtract)
-    tt(B("q1", 0, 42), B("q1", 0, 42), B("q2", 0, 42), OP.mult)
-    tt(B("q2", 0, 42), B("q1", 0, 42), B("q3", 0, 42), OP.add)
-    ts(B("invo", 0, 42), B("q2", 0, 42), float(-BS), OP.add)
-    ts(B("dk"), B("dk"), B("pf15", 0, 1), OP.add)
-    ts(B("dum"), B("dk"), float(-DUM), OP.add, 256.0, OP.mult)
-    copy(B("pkw", 1, 257), B("dum"))
-    border_take("xw")
-    rx = send("x", "sb", "xw", P)
+    fill(B("oz", Z0), 0.0)
     ts(B("tf", 0, 1), B("tlb"), 2.0, OP.mult, 1.0, OP.add)
     op("vector", lambda e: e.reciprocal(T.sc[:, 0:1], T.tf[:, 0:1]), [B("sc", 0, 1)], [B("tf", 0, 1)])
-    ts(B("Ds"), B("I"), B("sc", 0, 1), OP.mult)
+    pe(chain(B("pc1", 0, 48), table("gb", 0, BS)))
+    flagged("F")
+    positions(0)
+    for h in range(2):
+        border_take("vs"[h], "xw", h)
+    rx = send("x", "sb", "xw", P)
     giota(B("id", 0, 2048), [[-1, 128], [0, 16]], 0, 1)
+    giota(B("dk"), [[0, 4], [16, 64]], 9 * 32768, 0)
     giota(B("wS", S0 + DUM + 4 * P), [[0, 4 * NB]], 0, 0)
+    act(B("wS", 0, 2048), B("L"), AF.Copy)
+    act(IND(B("wS", INV, INV + P), B("sndu", 0, 42)), B("wS", ER, ER + NB), AF.Silu)
+    ts(B("Ds"), B("I"), B("sc", 0, 1), OP.mult)
     fill(B("ts"), 0.0)
     pack(0)
-    act(IND(B("wS", INV, INV + 2 * BS + NB), B("invo", 0, 42)), B("wS", ER, ER + NB), AF.Silu)
-    members(0, lambda: pe(chain(B("pf", 0, 96), [(B("wS", 128 * a, 128 * a + 128), B("wS", INV + a, INV + 2 * BS, 16)) for a in range(16)])))
-    for lo, hi in ((4 * P, 4 * P + 2048), (4 * P + 2048, 4 * W), (8 * BS, 10 * BS), (10 * BS, 12 * BS)):
+    inverse = chain(B("ps", 3 * U, 3 * U + 96), [(B("wS", 128 * a, 128 * a + 128), B("wS", INV + BS + a, INV + 3 * BS, 16)) for a in range(16)])
+    members(0, lambda: pe(inverse[:6]))
+    for lo, hi in ((4 * P, 4 * P + 2048), (4 * P + 2048, 4 * W)):
         sfill(B("wV", DUM + lo, DUM + hi), 0.0, B("L", 0, hi - lo))
-    run([("o0", {"v": "LB LC VV LA LD", "t": "LM"})], out_calls(0))
-    giota(B("wS", 0, U), [[0, U]], 4, 0)
+    run({"v": "LB LC LA LD", "t": "LM"}, out_calls(0))
     ts(B("E"), B("id", 0, 2048), 0.0, OP.is_equal)
+    ts(B("dk"), B("dk"), B("pf15", 0, 1), OP.add, 1.0 / 32768, OP.mult)
+    pe(inverse[6:])
     fill(B("oz", 0, Z0), 1.0)
-    ts(B("dk"), B("dk"), 1.0 / 32768, OP.mult, 9.0, OP.add)
+    ts(B("D"), B("ar"), B("pf15", 0, 1), OP.is_equal)
+    giota(B("wS", 0, U), [[0, U]], 4, 0)
     for k in (3, 2, 1, 0):
         dma("sync", B("wS", S0 + DUM + P * k, S0 + DUM + P * k + P, parts=ROWS), B("ts"), after=[rx])
+    dma("sync", B("wV", DUM, DUM + 16 * BS, parts=ROWS), B("oz", Z0))
+    dma("sync", B("wV", DUM + 16 * BS, DUM + 4 * P, parts=ROWS), B("oz", Z0, Z0 + 320))
     dma("sync", B("pk", BS, 2 * BS), HB(T.cd[:, BS:2 * BS]))
     dma("sync", B("Y", 0, P), HB(T.y0[:, :]))
     dma("sync", B("pk", 0, BS), HB(T.cd[:, 2 * BS:3 * BS]))
@@ -555,14 +562,14 @@ def rank_program(g, core, T, topo):
     gsel(B("I32"), [[-1, 128]], OP.is_equal, 0, 1, B("wS", 0, 128))
     for h in range(2):
         gsel(B("LT", 1024 * h, 1024 * h + 1024), [[-1, 8], [-16, 8], [0, 16]], OP.is_equal, -8 * h, 1, B("oz", 0, 1024))
-    giota(B("sm"), [[0, U]], 191, 0)
-    gsel(B("sm"), [[0, 32], [1, 16]], OP.is_equal, 0, 0)
-    gsel(B("sx"), [[0, 32], [1, 16]], OP.not_equal, 0, 0, B("oz", 0, U))
+    giota(B("sm"), [[0, 2 * U]], 191, 0)
+    gsel(B("sm"), [[0, 64], [1, 16]], OP.is_equal, 0, 0)
     for s in range(2):
         giota(B("fr", FR * s + NB, FR * s + FR), [[0, 16]], 0, 0)
-    giota(B("sdq"), [[0, 272]], 0, 0)
     dma("sync", B("rowd", 3 * BS, P), B("oz", Z0, Z0 + 128))
-    run([("o0", OUT0)], out_calls(0))
+    holder[("ps", 3)] = ["INV"]
+    run(OUT0, out_calls(0), "o0")
+    holder[("ps", 3)] = []
     border_flags(0)
     own_flags(1)
     take("s", B("sb"), B("Y", 0, P), B("sndu", 0, 42))
@@ -571,15 +578,16 @@ def rank_program(g, core, T, topo):
     own_table()
     ts(B("N257"), B("N256"), 1.0, OP.add)
     places(0)
-    ts(B("H"), B("I"), 0.5, OP.mult)
     flags_in(0)
     do_waits("g", need_of("g", [("fr", 0, NB)], []))
     send("y0", "sb", "Y", P)
+    giota(B("sdq"), [[0, 272]], 0, 0)
+    act(B("H"), B("I"), AF.Copy, scale=0.5)
     members(1)
     for q in range(3):
         n = 272 if q < 2 else 224
         dma("sync", B("sdq", 0, n, parts=slice(q, 128, 16)), HB(T.sd[:, 272 * q:272 * q + n]), after=need_of("dma", [("P16", 0, 48)], []))
-    run([("o1", OUT)], out_calls(1))
+    run(OUT, out_calls(1), "o1")
     border_flags(1)
     own_flags(2)
     member_row(0, "id", 0)
@@ -591,48 +599,56 @@ def rank_program(g, core, T, topo):
     member_row(1, "sf", 0)
     members(2)
 
-    calls = out_calls(2)
-    calls["ROW"] = (lambda: (member_row(2, "gb", 0), dma("sync", B("mq"), B("rowd"))), ["PLACES"])
-    run([("b2", BACK2), ("o2", {"s": "g0 g1 g2 g3 g4 ROW"})], calls)
-    stand(2)
-    border_take("Y")
-    ry = send("y1", "sb", "Y", P + NB)
-    dma("sync", HB(T.yv[:, 2 * BS:3 * BS]), B("Y", 2 * BS, 3 * BS), after=[ry])
-    old(0)
-    run([("o2", OUT2A), ("b1", {"v": "g1"}), ("o2", {"v": "o2345"}), ("b1", dict(BACK, v=BACK["v"][3:])), ("o2", {"s": "s2 s3 s4"})], calls)
-    stand(1)
-    border_take("Y")
-    ry = send("y2", "sb", "Y", P + 2 * NB)
-    acc = B("pf", 0, 272)
+    every = lambda st, c: [(st, c, u) for u in range(8)]
+    sent = {}
 
-    def all_rows():
-        dma("g", B("fr", 0, 1088), B("wS", S0 + DUM, S0 + DUM + 4 * P, parts=ROWS))
+    def standings_out(s):
+        sent[s] = send("y%d" % (3 - s), "sb", "Y", P + (3 - s) * NB)
+        if s == 2:
+            dma("sync", HB(T.yv[:, 2 * BS:3 * BS]), B("Y", 2 * BS, 3 * BS), after=[sent[s]])
+            old(0)
+    acc = []
+
+    def all_rows(q):
         dma("sync", B("zc1", 0, 1088), B("wV", DUM, DUM + 4 * P, parts=ROWS))
-        dma("sync", HB(T.yv[:, BS:2 * BS]), B("Y", BS, 2 * BS), after=[ry])
+        dma("sync", HB(T.yv[:, BS:2 * BS]), B("Y", BS, 2 * BS), after=[sent[1]])
 
-    def own_sum():
-        pe(chain(acc, [(B("I"), B(w, k, 1088, 4)) for w in ("fr", "zc1") for k in range(4)] + [(B("I"), B("sdq")), (B("I"), B("mq"))]))
+    def own_first(q):
+        acc.append(B("pc%d" % turn[0], 0, 272))
+        holder[("pc", turn[0])] = ["END"]
+        pe(chain(acc[0], [(B("I"), B("sdq")), (B("I"), B("mq"))] + [(B("I"), B("fr", k, 1088, 4)) for k in range(4)], last=False))
 
-    def last():
-        tt(IND(B("xw", 0, P), B("sndu", 0, 42)), B("gb", 0, NB), B("sb"), OP.add)
-        dma("sync", HB(T.yf[:, :]), B("xw", 0, P, parts=ROWS))
+    def own_sum(q):
+        pe(chain(acc[0], [(B("I"), B("zc1", k, 1088, 4)) for k in range(4)], first=False))
 
-    def own_end():
-        ts(B("yfo"), acc, 0.5, OP.is_gt)
+    def own_end(q):
+        ts(B("yfo"), acc[0], 0.5, OP.is_gt)
         tt(B("yfo"), B("yfo"), B("mq"), OP.add)
         dma("sync", B("xw", 0, P, parts=ROWS), B("yfo"))
 
-    def arrived():
+    def arrived(q):
         ts(B("sf", 0, NB), B("sb"), 0.5, OP.is_lt, -1.0, OP.mult)
         scan(B("gb", 0, NB), B("fr", 2 * FR, 2 * FR + NB), B("sf", 0, NB), OP.min, OP.mult)
-    calls.update({"B1": (lambda: (border_sum(0), border_sum(1)), ["TQ"]), "B2": (lambda: border_sign(0), ["B1"]),
-                  "B3": (lambda: (border_sign(1), send("f2", "sf", "fr", 2 * FR, -1)), ["B1", "B2"]), "W": (lambda: None, ["B3"]),
-                  "TQ": (all_rows, []), "OWN": (own_sum, ["TQ"]), "END": (own_end, ["OWN"]),
-                  "RG": (lambda: take("s", B("sb"), B("xw", 0, P), B("sndu", 0, 42)), ["END"]), "NEW": (arrived, ["RG"]), "FIN": (last, [])})
-    run([("o2", OUT2B), ("b0", BACK0)], calls)
-    for h in range(2):
-        take("s", B("Y", 384 * h, 384 * h + 384), B("zc0", 0, 1024), B("yp0", 24 * h, 24 * h + 24))
-        dma("scalar", HB(T.yv[:, 384 * h:384 * h + 384]), B("Y", 384 * h, 384 * h + 384))
+
+    def last(q):
+        tt(IND(B("xw", 0, P), B("sndu", 0, 42)), B("gb", 0, NB), B("sb"), OP.add)
+        dma("sync", HB(T.yf[:, :]), B("xw", 0, P, parts=ROWS))
+    calls = out_calls(2)
+    for s in range(3):
+        for h in range(2):
+            calls["N%d%d" % (s, h)] = (lambda q, s=s, h=h: stand(q, s, h), every("b%d" % s, "z") + ["PLACES"])
+            calls["T%d%d" % (s, h)] = (lambda q, h=h: border_take(q, "Y", h), ["N%d0" % s, "N%d1" % s])
+        calls["Y%d" % s] = (lambda q, s=s: standings_out(s), ["T%d0" % s, "T%d1" % s])
+    calls.update({"ROW": (lambda q: (member_row(2, "gb", 0), dma("sync", B("mq"), B("rowd"))), ["PLACES"]),
+                  "SDMA": (lambda q: dma("g", B("fr", 0, 1088), B("wS", S0 + DUM, S0 + DUM + 4 * P, parts=ROWS)), []),
+                  "J3": (calls["J3"][0], ["SDMA"] + every("b1", "z")), "OWN0": (own_first, ["SDMA", "ROW"] + every("o2", "o") + every("b1", "y")),
+                  "TQ": (all_rows, every("o2", "s") + ["Y1"]), "B1": (lambda q: (border_sum(0), border_sum(1)), ["TQ", "J0", "J1", "J2"]),
+                  "B2": (lambda q: border_sign(0), ["B1"]), "B3": (lambda q: (border_sign(1), send("f2", "sf", "fr", 2 * FR, -1)), ["B2"]),
+                  "OWN": (own_sum, ["OWN0", "TQ"]), "END": (own_end, ["OWN"]), "RG": (lambda q: take("s", B("sb"), B("xw", 0, P), B("sndu", 0, 42)), ["END"]),
+                  "NEW": (arrived, ["RG"]), "FIN": (last, ["NEW"])})
+    for k in range(3):
+        calls["K%d" % k][1].extend(every("b1", "e"))
+    run(BACK, calls, None, {("b1", "g"): ["Y2"], ("b0", "g"): ["Y1"], ("b0", "m"): ["J0", "J1", "J2"], ("b0", "e"): ["B3"]})
     totals.update(count)
     for s in sorted(totals):
         if known["g"].get(s, 0) < totals[s]:

@@ -9,31 +9,35 @@ DUM = 1024
 FW = DUM + 4 * W
 S0 = 1024
 MAGIC = 12582912.0
-FR = NB + 16
+FR = NB + 32
 Z0 = 2 * U
 INV, ER = 2048, 6400
 CUT = 3 * GB
 HALVES = ((0, CUT), (CUT, NB))
+K = 65536.0
+HI = 32768
+ABSENT = 511 * HI
 
 
 def _sb(n, d):
     return ("sbuf", [128, n], d)
 
 
-_BF = {"xw": W, "Y": P + 3 * NB, "wV": FW, "L": 2048, "LT": 2048, "I": 128, "H": 128, "Ds": 128, "BO": 128, "NU": 128, "ga": 8 * U, "mn": 8 * U,
-       "id": 8 * U, "sm": 2 * U, "oz": Z0 + BS, "tlb": 1, "fr": 3 * FR, "sf": BS, "sb": NB, "gb": BS, "sdq": 272,
+_BF = {"xw": W, "Y": P + 2 * NB, "wV": FW, "L": 2048, "LT": 2048, "I": 128, "IK": 128, "H": 128, "Ds": 128, "DsC": 128, "BO": 128, "NU": 128, "ds": 192, "dT": 256, "s4": 4 * (NB - CUT),
+       "ga": 8 * U, "mn": 8 * U, "id": 8 * U, "sm": 2 * U, "oz": Z0 + BS, "tlb": 1, "fr": 3 * FR, "sf": BS, "sb": NB, "gb": BS, "sdq": 272,
        "mq": 272, "yfo": 272, "F": 48, "cs": 48, "dd": 256, "be": 48, "Fo": 48, "M": NB, "D": 16}
-_F16 = {"E": 2048}
-_F32 = {"wS": S0 + FW, "I32": 128, "ts": 272, "NF": 48, "A": 48, "q1": 48, "q2": 48, "q3": 48, "N769": 48,
-        "N257": 48, "N256": 48, "pf15": 8, "tf": 8, "sc": 8, "dk": 256, "vv": 256, "t1": 256, "t2": 256}
-_I32 = {"pk": 2 * BS, "pkw": 1544, "tb": 256, "sndi": 42, "pi": 8, "pj": 8, "sn": 42, "ar": 16}
-_U16 = {"invT": 96, "sndu": 48, "P16": 48, "ou": 256, "rs": 48, "rr": 48}
+_BF["CK"] = 192
+ASIDE, DSG, SAMEQ, WVZ = 6, False, True, "g"
+_BF["s4"] = 16
+_F16 = {"E": U, "N1": 48, "iv": 2 * BS, "dk": 256, "A": 48}
+_F32 = {"wS": S0 + FW, "I32": 128, "ts": 272, "invF": 96, "q1": 48, "q2": 48, "N769": 48, "N257": 48, "pf": 8, "tf": 8, "sc": 8, "t1": 256, "t2": 256}
+_I32 = {"pk": 2 * BS, "pkw": 3 * BS + 8, "tb": 256, "sndi": 42, "pi": 8, "pj": 8, "sn": 42, "ar": 16}
+_U16 = {"invT": 48, "sndu": 48, "P16": 48, "ou": 256, "rs": 48, "rr": 48, "cb1": 256}
 for _s in range(3):
-    _BF.update({"zc%d" % (_s % 2): 1088, "xm%d" % _s: 256})
-    _F16.update({"nx%d" % _s: 256})
+    _BF.update({"zc%d" % (_s % 2): 1088})
+    _F16.update({"nx%d" % _s: 256, "xm%d" % _s: 256})
     _F32.update({"P32_%d" % _s: 48})
     _U16.update({"cu%d" % _s: 256, "yp%d" % _s: 48})
-_U16.update({"cb0": 256, "cb1": 256})
 SCRATCH = {}
 for _t, _d in ((_BF, "bfloat16"), (_F16, "float16"), (_F32, "float32"), (_I32, "int32"), (_U16, "uint16")):
     SCRATCH.update({_n: _sb(_c, _d) for _n, _c in _t.items()})
@@ -42,34 +46,41 @@ PSUMS = {"ps": 4 * U, "pc0": U, "pc1": U, "pr0": U, "pr1": U}
 for _n in PSUMS:
     SCRATCH[_n] = ("psum", [128, PSUMS[_n]], "float32")
 NDMA = 44
-EXCH = ["n", "x", "f0", "f1", "f2", "y0", "y1", "y2"]
-ONE = []
+EXCH = ["n", "m", "x", "f0", "f1", "f2", "y0", "y1", "y2"]
 SEMAPHORES = ["sv", "sa", "st", "sg"] + ["d%d" % k for k in range(NDMA)] + ["r_" + e for e in EXCH] + ["l_" + e for e in EXCH]
 
-OUT = {"v": "LB LA LC LD g3 n01 VV n23 n45 o01 n67 o2345 s3 o67 s5 s67",
-       "s": "g0 g1 g2 g4 g5 g6 g7 s0 s1 s2 s4 SDMA K0 K1 K2",
-       "t": "d0 LM d1 d2 d3 d4 d5 c01 d6 d7 c2345 c67 J3 J0 J1 J2"}
-OUT0 = {"v": "g1 g2 INV n01 VV n23 o01 n45 n67 o2345 s3 o67 s5 s67", "s": "g0 g3 g4 g5 g6 g7 MASK s0 s1 s2 s4 SDMA K0 K1 K2",
-        "t": "d0 d1 d2 d3 c01 d4 d5 d6 d7 c2345 c67 J3 J0 J1 J2"}
-BACK = {"v": "b2: LB LA LC g3 LD n01 n23 m01 n45 m23 PLACES m45 m67 y012345 y67 z012345 VV z67 N21 T20 Y2 o2: n01 n23 o01 n45 n67 b1: g1 g2 o2: o2345 "
-             "b1: n01 n23 m23 n45 m01 n67 m45 y012345 m67 y67 z012345 z67 N11 T10 Y1 o2: o67 s5 s67 TQ B2 "
-             "b0: g1 g3 n01 END n23 n45 m01 m23 m45 m67 NEW y012345 FIN y67 z012345 z67 N01",
-        "s": "b2: g0 g1 g2 g4 g5 g6 g7 o2: g0 b2: a67 n67 o2: g1 g2 g3 N20 T21 g4 g5 g6 g7 ROW s0 s1 b1: g0 g3 g4 g5 g6 g7 o2: s2 s3 s4 SDMA N10 T11 K0 K1 K2 "
-             "b0: g0 B3 g2 g4 g5 g6 g7 RG a67 n67 N00",
-        "t": "b2: d0 LM d1 d2 d3 d4 d5 d6 d7 c012345 c67 e012345 e67 o2: d0 d1 d2 d3 c01 d4 d5 d6 d7 c2345 "
-             "b1: d0 d1 d2 d3 d4 d5 d6 d7 c012345 c67 e012345 e67 o2: c67 J3 J0 J1 J2 OWN0 B1 b0: d0 d1 OWN d2 d3 d4 d5 d6 d7 c012345 e012345 c67 e67"}
+def PD(a, b):
+    return " ".join("p%d d%d" % (u, u) for u in range(a, b)) + " "
 
 
-def exchange_plan(topo, cores, r, sg, one=False):
+OV = "n01 n23 o01 g6 q01 n45 u01 n67 o2345 q2345 u2345 o67 s3 q67 s5 u67 s67 F0 F1"
+J = "JA0 JA1 JB0 JW0 JB1 JW1 "
+OUT = {"v": "LN LA LB LC g2 LD " + OV,
+       "s": "g0 g1 g3 g4 g5 g7 s0 s1 s2 s4 SDMA K0 K1",
+       "t": "p0 d0 LM " + PD(1, 4) + "c01 " + PD(4, 8) + "c2345 c67 PK " + J}
+OUT0 = {"v": OV, "s": "g0 g1 g2 g3 g4 g5 g7 s0 s1 s2 s4 SDMA K0 K1",
+        "t": "p0 p1 p2 p3 d0 d1 d2 d3 c01 " + PD(4, 8) + "c2345 c67 PK IV " + J}
+BT = PD(4, 8) + "c012345 c67 e012345 e67 "
+BV = "n01 m01 n23 m23 %s n45 m45 n67 m67 y012345 %s y67 z01234567 w01234567 "
+BACK = {"v": "b2: LN LA LB LC g2 LD PLACES " + BV % ("", "") + "N21 T20 Y2 o2: n01 n23 o01 q01 u01 n45 n67 "
+             "b1: g1 g3 o2: o2345 q2345 u2345 b1: " + BV % ("", "") + "N11 T10 Y1 o2: o67 s5 q67 u67 s67 TQ F0 b0: g1 g3 " + BV % ("END", "NEW") + "FIN",
+        "s": "b2: g0 g1 g3 g4 g5 g6 g7 o2: g0 ROW g1 g2 g3 g4 N20 T21 g5 g6 g7 s0 "
+             "b1: g0 g2 g4 g5 g6 g7 o2: s1 s23 N10 T11 s4 SDMA K0 K1 "
+             "b0: g0 g2 g4 F1 g5 g6 g7 N02",
+        "t": "b2: p0 d0 LM " + PD(1, 4) + BT + "o2: " + PD(0, 4) + "c01 " + PD(4, 8) + "c2345 b1: p0 p1 p2 p3 d0 d1 d2 d3 " + BT +
+             "o2: c67 b0: p0 p1 p2 p3 " + J + "d0 d1 OWN0 d2 d3 p4 p5 OWN d4 d5 " + PD(6, 8) + "c012345 c67 e012345 e67"}
+
+
+def exchange_plan(topo, cores, r, sg, short=False):
     src = cores[r]
     dst = [None] + [cores[(r + sg * d) % NR] for d in range(1, NR)]
     off = [d for d in range(1, NR) if topo.chip(dst[d]) != topo.chip(src)]
     eng = topo.engines(src, dst[off[0]])
     q = len(eng) // 4
     calls = []
-    for k, ds in enumerate((range(1, NR),) if one else (range(1, 4), range(4, NR))):
+    for k, ds in enumerate(([d for d in range(1, NR) if d not in off[2:]], off[2:]) if short else (range(1, 4), range(4, NR))):
         mine = [d for d in ds if d in off]
-        sizes = {6: [q // 2] * 4 + [q, q], 4: [q, q, q, q], 2: [2 * q, 2 * q], 3: [q, q, 2 * q] if k == 0 else [2 * q, q, q]}[len(mine)]
+        sizes = {4: [q, q, q, q], 2: [2 * q, 2 * q], 3: [q, q, 2 * q] if k == 0 else [2 * q, q, q]}[len(mine)]
         call, at = [], 0
         for d, n in zip(mine, sizes):
             call.append((d, eng[at:at + n]))
@@ -115,18 +126,18 @@ def rank_program(g, core, T, topo):
             for rec in recs.get(name, []):
                 if rec["hi"] <= lo or rec["lo"] >= hi:
                     continue
-                if rec["q"] == q and q == "tensor":
+                if rec["q"] == q and (q == "tensor" or w and not SAMEQ and q in ("vector", "scalar")):
                     continue
                 if w or rec["w"] or (psum and rec["q"] != q):
                     need.append(rec["tok"])
         return need
 
     def do_waits(q, need):
-        K = known[q]
+        kn = known[q]
         best = {}
         for tok in need:
             s = tok["sem"]
-            if K.get(s, 0) < tok["val"] and (s not in best or best[s]["val"] < tok["val"]):
+            if kn.get(s, 0) < tok["val"] and (s not in best or best[s]["val"] < tok["val"]):
                 best[s] = tok
         for s in sorted(best):
             if any(o != s and best[o]["clk"].get(s, 0) >= best[s]["val"] for o in best):
@@ -134,7 +145,7 @@ def rank_program(g, core, T, topo):
         for s in sorted(best):
             eng[q].wait_ge(T.sem[s], best[s]["val"])
             for a, b in best[s]["clk"].items():
-                K[a] = max(K.get(a, 0), b)
+                kn[a] = max(kn.get(a, 0), b)
 
     def record(q, tok, reads, writes):
         for name, lo, hi in writes:
@@ -163,11 +174,12 @@ def rank_program(g, core, T, topo):
         clk[s] = totals[s] = 16
         record("dma", {"sem": s, "val": 16, "clk": clk}, in_["r"], out["r"])
 
-    def send(name, src, land, at, sg=1, GB=GB):
+    def send(name, src, land, at, sg=1, GB=GB, part=None):
         NB = 7 * GB
         ls, rs = "l_" + name, "r_" + name
         done, pend, clk = 0, [], {}
-        for call in exchange_plan(topo, cores, rank, sg, name in ONE):
+        plan = lambda q: exchange_plan(topo, cores, q, sg) if part is None else exchange_plan(topo, cores, q, sg, True)[part:part + 1]
+        for call in plan(rank):
             tr, reads = [], []
             for d, es in call:
                 to = cores[(rank + sg * d) % NR]
@@ -183,10 +195,11 @@ def rank_program(g, core, T, topo):
             clk = dict(known["g"])
         clk[ls] = totals[ls] = done
         record("g", {"sem": ls, "val": done, "clk": clk}, pend, [])
-        n = sum(len(es) for q in range(NR) if q != rank for call in exchange_plan(topo, cores, q, sg, name in ONE) for d, es in call if (q + sg * d) % NR == rank)
+        n = sum(len(es) for q in range(NR) if q != rank for call in plan(q) for d, es in call if (q + sg * d) % NR == rank)
         totals[rs] = n
         rt = {"sem": rs, "val": n, "clk": {rs: n}}
-        recs[land] = [x for x in recs.get(land, []) if not (x["lo"] >= at and x["hi"] <= at + NB)] + [{"lo": at, "hi": at + NB, "w": True, "tok": rt, "q": "ext"}]
+        keep = [x for x in recs.get(land, []) if part or not (x["lo"] >= at and x["hi"] <= at + NB)]
+        recs[land] = keep + [{"lo": at, "hi": at + NB, "w": True, "tok": rt, "q": "ext"}]
         return rt
 
     def copy(out, in_): op("vector", lambda e: e.tensor_copy(out["ap"], in_["ap"]), [out], [in_])
@@ -202,8 +215,8 @@ def rank_program(g, core, T, topo):
         else:
             op("vector", lambda e: e.tensor_scalar(out["ap"], a["ap"], v1, s2, o1, o2), [out], ins)
 
-    def scan(out, d0, d1, o0, o1):
-        op("vector", lambda e: e.tensor_tensor_scan(out["ap"], d0["ap"], d1["ap"], 0.0, o0, o1), [out], [d0, d1])
+    def scan(out, d0, d1, o0, o1, first=0.0):
+        op("vector", lambda e: e.tensor_tensor_scan(out["ap"], d0["ap"], d1["ap"], first, o0, o1), [out], [d0, d1])
 
     def act(out, in_, f, **kw): op("scalar", lambda e: e.activation(out["ap"], in_["ap"], f, **kw), [out], [in_])
 
@@ -248,94 +261,98 @@ def rank_program(g, core, T, topo):
     def sfill(o, v, src):
         act(o, src, AF.Copy, scale=0.0, bias=v)
 
+    def marks_high(s):
+        pe([(B("ps", 2 * U + a, 2 * U + b), B("IK"), B("xw", s * BS + a, s * BS + b), True, True) for a, b in ((0, U), (U, BS))])
+
     def pack(s):
         o = B("pk", s % 2 * BS, s % 2 * BS + BS)
-        ts(o, o, 256.0, OP.mult)
-        tt(o, o, B("xw", s * BS, s * BS + BS), OP.add)
+        tt(o, o, B("ps", 2 * U, 2 * U + BS), OP.add)
+
+    def numbers(lo, hi):
+        ts(B("tb", lo, hi), B("pkw", 1 + lo, 1 + hi), HI - 1, OP.bitwise_and)
 
     def places_of(s, lo, hi):
-        ts(B("cu%d" % s, lo, hi), B("pkw", 1 + lo, 1 + hi), 1.0 / 1024, OP.mult, -0.499, OP.add)
+        ts(B("cu%d" % s, lo, hi), B("tb", lo, hi), 0.25, OP.mult, -0.375, OP.add)
 
     def marks_of(s, h):
-        lo, hi = 128 * h, 128 * h + 128
-        ts(B("tb", lo, hi), B("pkw", 1 + lo, 1 + hi), 255, OP.bitwise_and)
-        copy(B("xm%d" % s, lo, hi), B("tb", lo, hi))
+        ts(B("xm%d" % s, 128 * h, 128 * h + 128), B("pkw", 1 + 128 * h, 129 + 128 * h), 1.0 / HI, OP.mult, 1023.88, OP.add)
 
     def turned(s, h):
-        pe([(B("pr%d" % h, 0, 128), B("xm%d" % s, 128 * h, 128 * h + 128), B("Ds"), True, True)])
+        pe(chain(B("pr%d" % h, 0, 128), [(B("oz", 0, 128), B("DsC")), (B("xm%d" % s, 128 * h, 128 * h + 128), B("Ds"))]))
 
     def scaled(s, h):
         ts(B("nx%d" % s, 128 * h, 128 * h + 128), B("pr%d" % h, 0, 128), -1.0, OP.mult)
 
     def positions(s):
-        scan(B("cs"), B("oz", Z0, Z0 + 48), B("F"), OP.add, OP.subtract)
-        pe(chain(B("pc0", 0, 48), [(B("BO"), B("cs")), (B("NU"), B("F"))]))
-        ts(B("NF"), B("F"), 1.0, OP.add)
-        tt(B("A"), B("NF"), B("N769"), OP.mult)
-        tt(B("P32_%d" % s), B("pc0", 0, 48), B("A"), OP.max)
-        copy(B("P16"), B("P32_%d" % s))
+        F = B("ga", 15, BS, 16) if s else B("F")
+        scan(B("cs"), B("oz", Z0, Z0 + 48), F, OP.add, OP.subtract)
+        tt(B("A"), F, B("N769"), OP.mult)
+        pe(chain(B("pc0", 0, 48), [(B("I"), B("N1")), (B("NU"), F), (B("BO"), B("cs")), (B("I"), B("A"))]))
+        copy(B("P16"), B("pc0", 0, 48))
 
-    def members(s, beside=lambda: None):
+    def members(s):
         if s:
             positions(s)
         copy(IND(B("pkw"), B("P16")), B("pk", s % 2 * BS, s % 2 * BS + BS))
-        places_of(s, 0, 64)
+        numbers(0, 64)
         marks_of(s, 0)
-        beside()
+        places_of(s, 0, 64)
         turned(s, 0)
+        copy(B("P32_%d" % s), B("pc0", 0, 48))
 
-    def numbers(lo, hi):
-        ts(B("tb", lo, hi), B("pkw", 1 + lo, 1 + hi), 8, OP.arith_shift_right)
-        ts(B("vv", lo, hi), B("tb", lo, hi), 1.0 / 32768, OP.mult, 9.0 + DUM / 32768, OP.add)
-
-    def back_list(s):
-        ts(B("t1"), B("pkw", 1, 257), 1024.0 * P, OP.is_ge, 1024.0 * NB * (2 - s), OP.mult)
-        tt(B("t2"), B("t1"), B("pkw", 1, 257), OP.add)
-        ts(B("cb%d" % s), B("t2"), 1.0 / 1024, OP.mult, -0.499, OP.add)
-        absent()
+    def back_list():
+        ts(B("t1"), B("tb"), 4.0 * P, OP.is_ge, -4.0 * W, OP.mult)
+        tt(B("t2"), B("t1"), B("tb"), OP.add)
+        ts(B("cb1"), B("t2"), 0.25, OP.mult, NB - 0.375, OP.add)
 
     def absent():
-        giota(B("pkw", 1, 257), [[0, 256]], -256 * DUM, 0)
+        giota(B("pkw", 1, 257), [[0, 256]], ABSENT, 0)
 
     def places(s):
         p = B("P32_%d" % s)
-        ts(B("q1"), p, 256.5, OP.is_lt)
-        tt(B("q2"), p, B("N257"), OP.subtract)
-        tt(B("q3"), B("q2"), B("q1"), OP.mult)
-        tt(B("q2"), B("q3"), B("N256"), OP.add)
-        copy(B("yp%d" % s), B("q2"))
+        ts(B("q1"), p, -256.0, OP.add, 4096.0, OP.mult)
+        tt(B("q2"), B("q1"), p, OP.max)
+        tt(B("q1"), B("q2"), B("N257"), OP.min)
+        ts(B("yp%d" % s), B("q1"), -1.0, OP.add)
 
-    turn, holder, slot, made, sized, signed = [0], {}, {}, set(), set(), set()
+    turn, holder, slot, made, sized, signed, still = [0], {}, {}, set(), set(), set(), set()
 
     def aside(st, u):
-        return st == "o2" and u >= 6
+        return st == "o2" and u >= ASIDE
 
     def ready(st, c, us):
         back, first = st[0] == "b", "a" if (st, us[0]) in sized else "n"
-        near = lambda: {} if aside(st, us[0]) else {("id", u): ["c"] for u in us}
         if c == "g":
             return "", {("ga", u): ["d", "m"][:1 + back] for u in us}
+        if c == "p":
+            return "", {("ps", us[0] % 4): [first]}
         if c == "d":
-            return "g", {("ps", us[0] % 4): [first]}
+            return "gp", {}
         if c == first:
-            return "d", near()
+            return "d", {} if aside(st, us[0]) else {("id", u): ["c"] for u in us}
         if c == "m":
             return "g", {("mn", u): ["e"] for u in us}
-        if c == "h" or c == "c" and (st, "h", us[0]) not in made:
+        if c == "c":
             return "n", {("pc", turn[0]): ["y" if back else "o"]}
-        return {"n": "a", "c": "h", "o": "c", "y": "c", "s": "o", "e": "ym", "z": "e"}[c], {}
+        count = "r" if (st, us[0]) in still else "c"
+        return {"n": "a", "h": "c", "r": "h", "o": count, "q": "o", "u": "o" if count == "r" else "q", "y": count, "s": "u", "e": "ym", "z": "e", "w": "z"}[c], {}
 
     def issue(st, q, c, us):
         s, back, u, n = int(st[1]), st[0] == "b", us[0], len(us)
         m0, m1 = 32 * u, 32 * (u + n)
         units = lambda buf, k=u: B(buf, U * k, U * (k + n))
-        near = units("LT", u - 6) if aside(st, u) else units("id")
-        cnt = lambda: B("pc%d" % slot[(st, u)], 0, 32 * n)
+        near = units("LT", u - 4) if aside(st, u) else units("id")
+        at, mem = slot.get((st, u), 0), slice(0, min(32 * n, 128))
+        bank, held = "pc%d" % at, B("dT", 128 * at, 128 * at + 128, 1, mem)
+        cnt = lambda: B(bank, 128, 128 + 32 * n)
         if c == "g":
-            win = B("Y", 0, P + NB * (3 - s)) if back else B("xw")
-            take(q, units("ga"), win, B(("cb%d" if back and s < 2 else "cu%d") % s, m0, m1))
+            win = B("xw") if not back else B("Y", 0, W) if s == 1 else B("Y", NB, NB + W)
+            take(q, units("ga"), win, B("cb1" if st == "b1" else "cu%d" % s, m0, m1))
+        elif c == "p":
+            rows = slice(32 * (u % 4), 32 * (u % 4) + 32)
+            pe([(units("ps", u % 4), B("nx%d" % s, 128 * (u // 4), 128 * (u // 4) + 128, parts=rows), B("E", parts=rows), True, False)])
         elif c == "d":
-            pe(chain(units("ps", u % 4), [(B("nx%d" % s, 128 * (u // 4), 128 * (u // 4) + 128), units("E", u % 4)), (B("Ds"), units("ga"))]))
+            pe([(units("ps", u % 4), B("Ds"), units("ga"), False, True)])
         elif c == "a":
             act(near, units("ps", u % 4), AF.Abs)
         elif c == "n" and q == "s":
@@ -344,27 +361,38 @@ def rank_program(g, core, T, topo):
             ts(near, near, 0.5, OP.is_lt)
         elif c == "n":
             ts(near, units("ps", u % 4), MAGIC, OP.add, MAGIC, OP.is_equal)
+        elif c == "c" and (st, u) in still:
+            buf, lo, hi = near["r"][0]
+            pe([(B(bank, a, 128, 16, mem), B(buf, lo + a, hi, 16), B("BO", 0, 128, 16), True, True) for a in range(16)])
+        elif c == "c":
+            pe(chain(cnt(), ([] if back else [(B("I"), B("CK", 0, 32 * n))]) + table(*near["r"][0][:2], U * n)))
+        elif c == "h" and q == "v":
+            ts(held, B(bank, 0, 128, 1, mem), 9.5, OP.is_ge)
+        elif c == "h":
+            act(held, B(bank, 0, 128, 1, mem), AF.Relu, bias=-9.0)
+        elif c == "r":
+            pe(chain(cnt(), ([] if back else [(B("I"), B("dk", m0, m1))]) + [(held, B("IK", 0, 32 * n, 1, mem))]))
         elif c == "m":
             scan(units("mn"), B("sm", 0, U * n), units("ga"), OP.max, OP.min)
-        elif c in "hc":
-            mm = chain(cnt(), table(*near["r"][0][:2], U * n))
-            pe(mm[:8] if c == "h" else mm[8:] if (st, "h", u) in made else mm)
         elif c == "o":
-            tt(B("t1", m0, m1), cnt(), B("vv", m0, m1), OP.min)
-            tt(B("t2", m0, m1), B("t1", m0, m1), B("dk", m0, m1), OP.max)
-            ts(B("ou", m0, m1), B("t2", m0, m1), -9.0, OP.add, 32768.0, OP.mult)
+            tt(B("t1", m0, m1), cnt(), B("tb", m0, m1), OP.min)
+        elif c == "q":
+            tt(B("t1", m0, m1), B("t1", m0, m1), B("dk", m0, m1), OP.max)
+        elif c == "u":
+            ts(B("ou", m0, m1), B("t1", m0, m1), float(DUM), OP.add)
         elif c == "s" and q == "v":
             copy(IND(B("wV"), B("ou", m0, m1)), B("oz", 0, U * n))
         elif c == "s":
             assert "SDMA" not in made
             act(IND(B("wS", S0), B("ou", m0, m1)), B("wS", 0, U * n), AF.Silu)
         elif c == "y":
-            ts(B("dd", m0, m1), cnt(), 3.0 if (st, u) in signed else 9.5, OP.is_ge, 255.0, OP.mult)
+            ts(B("dd", m0, m1), cnt(), 0.5 if (st, u) in still else K * (3.0 if (st, u) in signed else 9.5), OP.is_gt, 255.0, OP.mult)
         elif c == "e":
             pe(chain(B("pr0", m0, m1), [(B("H"), B("xm%d" % s, m0, m1)), (B("H"), B("mn", U * u + 15, U * (u + n), 16)), (B("BO"), B("dd", m0, m1))]))
         elif c == "z":
-            ts(B("t1", m0, m1), B("pr0", m0, m1), -0.25, OP.add, MAGIC, OP.add)
-            ts(B("zc%d" % (s % 2), m0, m1), B("t1", m0, m1), MAGIC, OP.subtract, 255.0, OP.min)
+            ts(B("t2", m0, m1), B("pr0", m0, m1), -512.25, OP.add, MAGIC, OP.add)
+        elif c == "w":
+            ts(B("zc%d" % (s % 2), m0, m1), B("t2", m0, m1), MAGIC, OP.subtract, 255.0, OP.min)
 
     def run(lists, own, st=None, behind={}):
         todo = {q: [] for q in "vst"}
@@ -377,6 +405,7 @@ def rank_program(g, core, T, topo):
                 todo[q].append((st, w if not us else w[0], us))
                 sized.update((st, u) for u in us if w[0] == "a")
                 signed.update((st, u) for u in us if w[0] == "n" and q == "s")
+                still.update((st, u) for u in us if w[0] == "h")
         names = {c for q in todo for st, c, us in todo[q] if not us}
         while any(todo.values()):
             moved = False
@@ -390,7 +419,7 @@ def rank_program(g, core, T, topo):
                         made.add(c)
                     else:
                         before, takes = ready(st, c, us)
-                        first = [{"d": "LA" if us[0] < 4 else "LD", "g": "LB" if us[-1] > 1 else "", "o": "VV"}.get(c)] + behind.get((st, c), [])
+                        first = [{"p": "LA" if us[0] < 4 else "LD", "g": "LB" if us[-1] > 1 else ""}.get(c)] + behind.get((st, c), [])
                         if any(w in names and w not in made for w in first) or not all((st, b, u) in made for b in before for u in us):
                             break
                         if not all(x in made for k in takes for x in holder.get(k, [])):
@@ -408,49 +437,64 @@ def rank_program(g, core, T, topo):
         made.difference_update(own)
 
     def s_rows(s):
-        if s < 2:
-            o = S0 + DUM + 4 * BS * (s + 1)
+        o = S0 + DUM + 4 * BS * (s + 1)
+        if DSG:
+            dma("g", B("ds"), B("wS", o, o + 4 * BS, parts=ROWS))
+        else:
             dma("sync", B("ts", 0, 192), B("wS", o, o + 4 * BS, parts=ROWS))
 
-    def out_calls(s):
+    def out_calls(s, lists={}):
         o = S0 + DUM + 4 * P
+        parts, buf = [0, 0], "mn" if s < 2 else "xw"
+        sums_of = [[w for w in lists.get("t", "").split() if w[0] == "J" and w[2] == str(h)] for h in range(2)]
 
-        def narrow(k):
-            move("s", B("mn", 1024 * k, 1024 * k + NB), B("wS", o + k, S0 + FW, 4))
-
-        def add(k):
-            if k == 3:
-                pe([(B("pr%d" % h, 0, b - a), B("I32"), B("wS", o + 4 * a + 3, o + 4 * b, 4), True, False) for h, (a, b) in enumerate(HALVES)])
+        def narrow(q, h):
+            a, b = HALVES[h]
+            if "JA%d" % h in sums_of[h]:
+                for k in range(3):
+                    move(q, B(buf, 1024 * k + a, 1024 * k + b), B("wS", o + 4 * a + k, o + 4 * b, 4))
             else:
-                pe([(B("pr%d" % h, 0, b - a), B("I"), B("mn", 1024 * k + a, 1024 * k + b), False, False) for h, (a, b) in enumerate(HALVES)])
-        stubs = {"K%d" % k: (lambda q, k=k: narrow(k), ["SDMA"]) for k in range(3)}
-        stubs.update({"J%d" % k: (lambda q, k=k: add(k), ["K%d" % k, "J3"] if k < 3 else ["SDMA"]) for k in range(4)})
-        return {**stubs, "LA": (lambda q: scaled(s, 0), []), "LB": (lambda q: places_of(s, 64, 256), []), "LC": (lambda q: marks_of(s, 1), []),
-                "LM": (lambda q: turned(s, 1), ["LC"]), "LD": (lambda q: scaled(s, 1), ["LM"]), "VV": (lambda q: numbers(0, 256), []),
+                move(q, B(buf, 4 * a, 4 * b), B("wS", o + 4 * a, o + 4 * b))
+
+        def stubs_of(h):
+            a, b = HALVES[h]
+            scan(B("id", 4 * a, 4 * b), B("s4", 0, 4 * (b - a)), B("wV", DUM + 4 * (P + a), DUM + 4 * (P + b)), OP.mult, OP.max)
+
+        def add(h, src, ks, at=0, by="I"):
+            a, b = HALVES[h]
+            parts[h] += 1
+            cols = lambda k: B(src, 1024 * k + a, 1024 * k + b) if len(ks) == 3 else B(src, at + 4 * a + k, at + 4 * b, 4)
+            pe(chain(B("pr%d" % h, 0, b - a), [(B(by), cols(k)) for k in ks], parts[h] == 1, parts[h] == len(sums_of[h])))
+
+        def flags_out(q, h):
+            a, b = HALVES[h]
+            out, sums = B("sf", a, b), B("pr%d" % h, 0, b - a)
+            if s < 2:
+                tt(out, sums, B("M", a, b), OP.min)
+            elif q == "v":
+                ts(out, sums, 0.5, OP.is_gt)
+            else:
+                act(out, sums, AF.Sign)
+            if h:
+                send("f%d" % s, "sf", "fr", FR * s, -1)
+        stubs = {}
+        for h in range(2):
+            stubs.update({"K%d" % h: (lambda q, h=h: narrow(q, h), ["SDMA"]), "JB%d" % h: (lambda q, h=h: add(h, buf, range(3 if "JA%d" % h in sums_of[h] else 4)), ["K%d" % h]),
+                          "JA%d" % h: (lambda q, h=h: add(h, "wS", [3], o, "I32"), ["SDMA"]),
+                          "JW%d" % h: (lambda q, h=h: add(h, "wV", range(4), DUM + 4 * P), [("o%d" % s, "s", u) for u in range(8)]),
+                          "R%d" % h: (lambda q, h=h: stubs_of(h), [("o%d" % s, "s", u) for u in range(8)] + [("b1", "c", u) for u in range(8 * (s // 2))]),
+                          "JV%d" % h: (lambda q, h=h: add(h, "id", [3]), ["R%d" % h]),
+                          "F%d" % h: (lambda q, h=h: flags_out(q, h), sums_of[h] + ["F0"][:h])})
+        return {**stubs, "PK": (lambda q: marks_high(s + 1), [("o%d" % s, "n", u) for u in range(8)]),
+                "IV": (lambda q: pe(chain(B("ps", 0, 96), table("iv", 0, 2 * BS))), [("o%d" % s, "n", u) for u in range(8)]), "LA": (lambda q: scaled(s, 0), []), "LN": (lambda q: numbers(64, 256), []), "LB": (lambda q: places_of(s, 64, 256), ["LN"]), "LC": (lambda q: marks_of(s, 1), []),
+                "LM": (lambda q: turned(s, 1), ["LC"]), "LD": (lambda q: scaled(s, 1), ["LM"]),
                 "SDMA": (lambda q: s_rows(s), []), "PLACES": (lambda q: places(s), []),
-                "MASK": (lambda q: take(q, B("M"), B("D"), B("rr", 0, 42)), []),
-                "INV": (lambda q: ts(B("invT"), B("ps", 3 * U, 3 * U + 96), 0.0625, OP.mult, -63.75, OP.add), [])}
-
-    def border_sum(h):
-        o, (a, b) = DUM + 4 * P, HALVES[h]
-        pe(chain(B("pr%d" % h, 0, b - a), [(B("I"), B("wV", o + 4 * a + k, o + 4 * b, 4)) for k in range(4)], first=False))
-
-    def border_sign(h):
-        if h == 0:
-            ts(B("sf", 0, CUT), B("pr0", 0, CUT), 0.5, OP.is_gt, -1.0, OP.mult)
-        else:
-            act(B("sf", CUT, NB), B("pr1", 0, NB - CUT), AF.Sign, scale=-1.0)
-
-    def border_flags(s):
-        for h, (a, b) in enumerate(HALVES):
-            border_sum(h)
-            tt(B("sf", a, b), B("pr%d" % h, 0, b - a), B("M", a, b), OP.min)
-        send("f%d" % s, "sf", "fr", FR * s, -1)
+                "MASK": (lambda q: take(q, B("M"), B("D"), B("rr", 0, 42)), [])}
 
     def own_flags(t):
         o = DUM + 4 * BS * t
         dma("sync", B("dd", 0, 192), B("wV", o, o + 4 * BS, parts=ROWS))
-        pe(chain(B("pc0", 0, 48), [(B("I32"), B("ts", k, 192, 4)) for k in range(4)], last=False))
+        pe(chain(B("pc0", 0, 48), [(B("I"), B("ds", k, 192, 4)) if DSG else (B("I32"), B("ts", k, 192, 4)) for k in range(4)], last=False))
         pe(chain(B("pc0", 0, 48), [(B("I"), B("dd", k, 192, 4)) for k in range(4)], first=False))
 
     def own_runs():
@@ -460,26 +504,25 @@ def rank_program(g, core, T, topo):
     def own_table():
         own_runs()
         for h in range(2):
-            move("s", B("mn", 384 * h, 384 * h + 384), B("ps", U * h, U * h + 384))
+            move("sv"[h], B("mn", 384 * h, 384 * h + 384), B("ps", U * h, U * h + 384))
         pe(chain(B("pc1", 0, 48), table("mn", 0, BS)))
 
-    def flagged(out):
-        ts(B(out), B("pc1", 0, 48), 0.5, OP.is_gt, -1.0, OP.mult)
+    def unflagged(out):
+        ts(B(out), B("pc1", 0, 48), 0.5, OP.is_lt)
 
     def flags_in(s):
-        flagged("Fo")
+        tt(B("q2"), B("pc1", 0, 48), B("invF", 48 * s, 48 * s + 48), OP.max)
+        ts(B("invT"), B("q2"), B("pf", 2, 3), OP.min)
         win = B("fr", FR * s, FR * s + FR)
-        o = 48 * s
-        act(B("gb", 0, 384), IND(win, B("invT", o, o + 24)), AF.Copy, scale=-1.0)
-        ts(B("gb", 384, BS), IND(win, B("invT", o + 24, o + 48)), -1.0, OP.mult)
+        act(B("gb", 0, 384), IND(win, B("invT", 0, 24)), AF.Copy, scale=-1.0, bias=1.0)
+        ts(B("gb", 384, BS), IND(win, B("invT", 24, 48)), -1.0, OP.mult, 1.0, OP.add)
         scan(B("ga", 0, BS), B("sm", 0, BS), B("gb"), OP.add, OP.min)
-        tt(B("F"), B("Fo"), B("ga", 15, BS, 16), OP.min)
 
     def stand(q, s, h):
-        lo = BS * s + 384 * h
-        take(q, B("Y", lo, lo + 384), B("zc%d" % (s % 2), 0, 1024), B("yp%d" % s, 24 * h, 24 * h + 24))
+        lo, n = (BS * s + 384 * h, 384) if h < 2 else (BS * s, BS)
+        take(q, B("Y", NB + lo, NB + lo + n), B("zc%d" % (s % 2), 0, 1024), B("yp%d" % s, 24 * (h % 2), 24 * (h % 2) + n // 16))
         if s == 0:
-            dma("scalar" if q == "s" else "sync", HB(T.yv[:, lo:lo + 384]), B("Y", lo, lo + 384))
+            dma("scalar" if q == "s" and h < 2 else "sync", HB(T.yv[:, lo:lo + n]), B("Y", NB + lo, NB + lo + n))
 
     def old(s):
         dma("sync", B("zc%d" % (s % 2), 256, 1024), HB(T.y0[:, s * BS:s * BS + BS]))
@@ -490,109 +533,116 @@ def rank_program(g, core, T, topo):
 
     def border_take(q, win, h):
         a, b = HALVES[h]
-        take(q, B("sb", a, b), B(win, 0, P), B("sndu", a // 16, b // 16))
+        take(q, B("sb", a, b), B("xw", 0, P) if win == "xw" else B("Y", NB, W), B("sndu", a // 16, b // 16))
 
     dma("sync", B("sndi"), HB(T.snd[:, :]))
-    dma("sync", B("tlb"), HB(T.tl[:, :]))
-    dma("sync", B("xw", 0, BS), HB(T.x[:, 0:BS]))
-    fill(B("gb"), 0.0)
-    fill(B("BO"), 1.0)
-    dma("sync", B("gb", parts=ROWS), HB(T.sd[:, :]))
-    dma("sync", B("xw", BS, P), HB(T.x[:, BS:P]))
+    dma("sync", B("xw", 0, P), HB(T.x[:, :]))
     dma("sync", B("pk", 0, BS), HB(T.cd[:, 0:BS]))
-    fill(B("L"), 0.0)
-    fill(B("I"), 1.0)
-    gsel(B("BO"), [[-16, 8], [0, 16]], OP.is_ge, 0, 1)
-    gsel(B("BO"), [[16, 8], [0, 16]], OP.is_ge, 15, -1)
+    dma("scalar", B("tlb"), HB(T.tl[:, :]))
+    fill(B("gb"), 0.0)
+    dma("scalar", B("gb", parts=ROWS), HB(T.sd[:, :]))
+    giota(B("id", 0, 128), [[-32, 8], [0, 16]], -15, 2)
+    giota(B("id", 128, 256), [[1, 128]], 0, -1)
     giota(B("pi"), [[0, 8]], 0, 1)
-    giota(B("N256"), [[16, 48]], 256, 0)
+    giota(B("N257"), [[16, 48]], 257, 0)
     giota(B("ar"), [[1, 16]], 0, 0)
-    gsel(B("NU"), [[-1, 128]], OP.is_gt, 0, 1, B("BO"))
-    fill(B("pkw", 1, 257), -256 * DUM)
+    fill(B("L"), 0.0)
+    ts(B("BO"), B("id", 0, 128), 32 * MAGIC, OP.add, 32 * MAGIC, OP.is_equal)
     ts(B("sn"), B("sndi"), 15, OP.bitwise_and)
+    ts(B("I"), B("id", 128, 256), 0.0, OP.is_equal)
     copy(B("rs", 0, 42), B("sn"))
     send("n", "rs", "rr", 0, 1, GB // 16)
-    gsel(B("I"), [[-1, 128]], OP.is_equal, 0, 1)
-    giota(B("wS", ER, ER + NB), [[1, NB]], 64, 0)
     for a in range(16):
-        act(B("L", 128 * a + a, 128 * a + 128, 16), B("BO", a, 128, 16), AF.Copy)
-    sfill(B("wS", INV + BS, INV + 3 * BS), 64.0 + NB, B("L", 0, 2 * BS))
+        act(B("L", 128 * a + a, 128 * a + 128, 16), B("BO", a, 128, 16), AF.Copy, scale=K)
+    ts(B("pj", 0, 1), B("pi", 0, 1), 15, OP.bitwise_and)
+    ts(B("pj", 1, 2), B("pi", 0, 1), 31, OP.bitwise_and)
+    ts(B("H"), B("id", 128, 256), 0.0, OP.is_lt)
     copy(B("sndu", 0, 42), B("sndi"))
-    ts(B("pj"), B("pi"), 15, OP.bitwise_and)
-    copy(B("pf15"), B("pj"))
-    ts(B("N256"), B("N256"), B("pf15", 0, 1), OP.add)
-    ts(B("N769"), B("N256"), 513.0, OP.add)
-    fill(B("oz", Z0), 0.0)
+    copy(B("pf", 0, 2), B("pj", 0, 2))
+    tt(B("NU"), B("H"), B("BO"), OP.mult)
     ts(B("tf", 0, 1), B("tlb"), 2.0, OP.mult, 1.0, OP.add)
+    ts(B("N257"), B("N257"), B("pf", 0, 1), OP.add)
+    fill(B("oz", Z0), 0.0)
     op("vector", lambda e: e.reciprocal(T.sc[:, 0:1], T.tf[:, 0:1]), [B("sc", 0, 1)], [B("tf", 0, 1)])
+    fill(B("oz", 0, Z0), 1.0)
+    ts(B("IK"), B("I"), float(HI), OP.mult)
+    ts(B("N769"), B("N257"), 512.0, OP.add)
+    ts(B("N1"), B("N257"), -256.0, OP.add)
+    ts(B("D"), B("ar"), B("pf", 0, 1), OP.is_equal)
+    ts(B("Ds"), B("I"), B("sc", 0, 1), OP.mult)
+    scan(B("wS", ER, ER + NB), B("oz", 0, NB), B("oz", Z0, Z0 + NB), OP.add, OP.add, 63.0)
+    sfill(B("wS", INV + BS, INV + 3 * BS), 64.0 + NB, B("L", 0, 2 * BS))
     pe(chain(B("pc1", 0, 48), table("gb", 0, BS)))
-    flagged("F")
-    positions(0)
+    marks_high(0)
     for h in range(2):
         border_take("vs"[h], "xw", h)
     rx = send("x", "sb", "xw", P)
-    giota(B("id", 0, 2048), [[-1, 128], [0, 16]], 0, 1)
-    giota(B("dk"), [[0, 4], [16, 64]], 9 * 32768, 0)
+    giota(B("id", 0, U), [[1, 32], [0, 16]], 0, 0)
+    giota(B("t1"), [[0, 4], [16, 64]], -DUM, 0)
     giota(B("wS", S0 + DUM + 4 * P), [[0, 4 * NB]], 0, 0)
-    act(B("wS", 0, 2048), B("L"), AF.Copy)
     act(IND(B("wS", INV, INV + P), B("sndu", 0, 42)), B("wS", ER, ER + NB), AF.Silu)
-    ts(B("Ds"), B("I"), B("sc", 0, 1), OP.mult)
-    fill(B("ts"), 0.0)
+    take("s", B("M"), B("D"), B("rr", 0, 42))
+    sfill(B("wS", 0, 2 * U), 4.0, B("L", 0, 2 * U))
+    unflagged("F")
+    fill(B("pkw", 1, 257), ABSENT)
+    positions(0)
     pack(0)
-    inverse = chain(B("ps", 3 * U, 3 * U + 96), [(B("wS", 128 * a, 128 * a + 128), B("wS", INV + BS + a, INV + 3 * BS, 16)) for a in range(16)])
-    members(0, lambda: pe(inverse[:6]))
-    for lo, hi in ((4 * P, 4 * P + 2048), (4 * P + 2048, 4 * W)):
-        sfill(B("wV", DUM + lo, DUM + hi), 0.0, B("L", 0, hi - lo))
-    run({"v": "LB LC LA LD", "t": "LM"}, out_calls(0))
-    ts(B("E"), B("id", 0, 2048), 0.0, OP.is_equal)
-    ts(B("dk"), B("dk"), B("pf15", 0, 1), OP.add, 1.0 / 32768, OP.mult)
-    pe(inverse[6:])
-    fill(B("oz", 0, Z0), 1.0)
-    ts(B("D"), B("ar"), B("pf15", 0, 1), OP.is_equal)
-    giota(B("wS", 0, U), [[0, U]], 4, 0)
+    ts(B("DsC"), B("Ds"), -1024.0, OP.mult)
+    members(0)
+    run({"v": "LN LC LB LA LD", "t": "LM"}, out_calls(0))
+    ts(B("E"), B("id", 0, U), B("pf", 1, 2), OP.is_equal)
+    fill(B("ts"), 0.0)
+    copy(B("iv"), B("wS", INV + BS, INV + 3 * BS))
+    ts(B("dk"), B("t1"), B("pf", 0, 1), OP.add)
+    fill(B("CK"), -9.5 * K)
+    ts(B("pf", 2, 3), B("pf", 0, 1), NB + 16.0, OP.add)
+    if WVZ == "v":
+        fill(B("wV", DUM + 4 * P), 0.0)
     for k in (3, 2, 1, 0):
         dma("sync", B("wS", S0 + DUM + P * k, S0 + DUM + P * k + P, parts=ROWS), B("ts"), after=[rx])
     dma("sync", B("wV", DUM, DUM + 16 * BS, parts=ROWS), B("oz", Z0))
     dma("sync", B("wV", DUM + 16 * BS, DUM + 4 * P, parts=ROWS), B("oz", Z0, Z0 + 320))
     dma("sync", B("pk", BS, 2 * BS), HB(T.cd[:, BS:2 * BS]))
-    dma("sync", B("Y", 0, P), HB(T.y0[:, :]))
+    dma("sync", B("Y", NB, W), HB(T.y0[:, :]))
     dma("sync", B("pk", 0, BS), HB(T.cd[:, 2 * BS:3 * BS]))
     for s in (2, 1):
         old(s)
+    if WVZ == "g":
+        giota(B("wV", DUM + 4 * P), [[0, 4 * NB]], 0, 0)
     gsel(B("I32"), [[-1, 128]], OP.is_equal, 0, 1, B("wS", 0, 128))
+    if "R0" in OUT["v"] + BACK["v"]:
+        giota(B("s4"), [[0, NB - CUT], [1, 4]], 0, 0)
     for h in range(2):
         gsel(B("LT", 1024 * h, 1024 * h + 1024), [[-1, 8], [-16, 8], [0, 16]], OP.is_equal, -8 * h, 1, B("oz", 0, 1024))
-    giota(B("sm"), [[0, 2 * U]], 191, 0)
-    gsel(B("sm"), [[0, 64], [1, 16]], OP.is_equal, 0, 0)
     for s in range(2):
-        giota(B("fr", FR * s + NB, FR * s + FR), [[0, 16]], 0, 0)
+        giota(B("fr", FR * s + NB, FR * s + NB + 16), [[0, 16]], 0, 0)
+        gsel(B("fr", FR * s + NB + 16, FR * s + FR), [[0, 16]], OP.is_equal, 0, 0, B("D"))
     dma("sync", B("rowd", 3 * BS, P), B("oz", Z0, Z0 + 128))
-    holder[("ps", 3)] = ["INV"]
-    run(OUT0, out_calls(0), "o0")
-    holder[("ps", 3)] = []
-    border_flags(0)
+    run(OUT0, out_calls(0, OUT0), "o0")
+    ts(B("invF"), B("ps", 0, 96), 0.0625 / K, OP.mult, -64.0, OP.add)
     own_flags(1)
-    take("s", B("sb"), B("Y", 0, P), B("sndu", 0, 42))
+    take("s", B("sb"), B("Y", NB, W), B("sndu", 0, 42))
+    fill(B("sm"), 0.0)
     pack(1)
-    back_list(0)
+    fill(B("sm", 0, 2 * U, 16), 191.0)
+    absent()
     own_table()
-    ts(B("N257"), B("N256"), 1.0, OP.add)
     places(0)
     flags_in(0)
     do_waits("g", need_of("g", [("fr", 0, NB)], []))
-    send("y0", "sb", "Y", P)
+    send("y0", "sb", "Y", W)
     giota(B("sdq"), [[0, 272]], 0, 0)
     act(B("H"), B("I"), AF.Copy, scale=0.5)
     members(1)
     for q in range(3):
         n = 272 if q < 2 else 224
         dma("sync", B("sdq", 0, n, parts=slice(q, 128, 16)), HB(T.sd[:, 272 * q:272 * q + n]), after=need_of("dma", [("P16", 0, 48)], []))
-    run(OUT, out_calls(1), "o1")
-    border_flags(1)
+    run(OUT, out_calls(1, OUT), "o1")
     own_flags(2)
     member_row(0, "id", 0)
     pack(2)
-    back_list(1)
+    absent()
+    back_list()
     own_table()
     places(1)
     flags_in(1)
@@ -603,15 +653,15 @@ def rank_program(g, core, T, topo):
     sent = {}
 
     def standings_out(s):
-        sent[s] = send("y%d" % (3 - s), "sb", "Y", P + (3 - s) * NB)
+        sent[s] = send("y%d" % (3 - s), "sb", "Y", (2 - s) * W)
         if s == 2:
-            dma("sync", HB(T.yv[:, 2 * BS:3 * BS]), B("Y", 2 * BS, 3 * BS), after=[sent[s]])
+            dma("sync", HB(T.yv[:, 2 * BS:3 * BS]), B("Y", NB + 2 * BS, NB + 3 * BS), after=[sent[s]])
             old(0)
     acc = []
 
     def all_rows(q):
         dma("sync", B("zc1", 0, 1088), B("wV", DUM, DUM + 4 * P, parts=ROWS))
-        dma("sync", HB(T.yv[:, BS:2 * BS]), B("Y", BS, 2 * BS), after=[sent[1]])
+        dma("sync", HB(T.yv[:, BS:2 * BS]), B("Y", NB + BS, NB + 2 * BS), after=[sent[1]])
 
     def own_first(q):
         acc.append(B("pc%d" % turn[0], 0, 272))
@@ -626,29 +676,25 @@ def rank_program(g, core, T, topo):
         tt(B("yfo"), B("yfo"), B("mq"), OP.add)
         dma("sync", B("xw", 0, P, parts=ROWS), B("yfo"))
 
-    def arrived(q):
-        ts(B("sf", 0, NB), B("sb"), 0.5, OP.is_lt, -1.0, OP.mult)
-        scan(B("gb", 0, NB), B("fr", 2 * FR, 2 * FR + NB), B("sf", 0, NB), OP.min, OP.mult)
-
     def last(q):
-        tt(IND(B("xw", 0, P), B("sndu", 0, 42)), B("gb", 0, NB), B("sb"), OP.add)
+        copy(IND(B("xw", 0, P), B("sndu", 0, 42)), B("gb", 0, NB))
         dma("sync", HB(T.yf[:, :]), B("xw", 0, P, parts=ROWS))
-    calls = out_calls(2)
+    calls = out_calls(2, BACK)
     for s in range(3):
         for h in range(2):
-            calls["N%d%d" % (s, h)] = (lambda q, s=s, h=h: stand(q, s, h), every("b%d" % s, "z") + ["PLACES"])
+            calls["N%d%d" % (s, h)] = (lambda q, s=s, h=h: stand(q, s, h), every("b%d" % s, "w") + ["PLACES"])
             calls["T%d%d" % (s, h)] = (lambda q, h=h: border_take(q, "Y", h), ["N%d0" % s, "N%d1" % s])
+        calls["N%d2" % s] = (lambda q, s=s: stand(q, s, 2), every("b%d" % s, "w"))
         calls["Y%d" % s] = (lambda q, s=s: standings_out(s), ["T%d0" % s, "T%d1" % s])
     calls.update({"ROW": (lambda q: (member_row(2, "gb", 0), dma("sync", B("mq"), B("rowd"))), ["PLACES"]),
-                  "SDMA": (lambda q: dma("g", B("fr", 0, 1088), B("wS", S0 + DUM, S0 + DUM + 4 * P, parts=ROWS)), []),
-                  "J3": (calls["J3"][0], ["SDMA"] + every("b1", "z")), "OWN0": (own_first, ["SDMA", "ROW"] + every("o2", "o") + every("b1", "y")),
-                  "TQ": (all_rows, every("o2", "s") + ["Y1"]), "B1": (lambda q: (border_sum(0), border_sum(1)), ["TQ", "J0", "J1", "J2"]),
-                  "B2": (lambda q: border_sign(0), ["B1"]), "B3": (lambda q: (border_sign(1), send("f2", "sf", "fr", 2 * FR, -1)), ["B2"]),
-                  "OWN": (own_sum, ["OWN0", "TQ"]), "END": (own_end, ["OWN"]), "RG": (lambda q: take("s", B("sb"), B("xw", 0, P), B("sndu", 0, 42)), ["END"]),
-                  "NEW": (arrived, ["RG"]), "FIN": (last, ["NEW"])})
-    for k in range(3):
-        calls["K%d" % k][1].extend(every("b1", "e"))
-    run(BACK, calls, None, {("b1", "g"): ["Y2"], ("b0", "g"): ["Y1"], ("b0", "m"): ["J0", "J1", "J2"], ("b0", "e"): ["B3"]})
+                  "SDMA": (lambda q: dma("g", B("fr", 0, 1088), B("wS", S0 + DUM, S0 + DUM + 4 * P, parts=ROWS)), ["Y1"]),
+                  "OWN0": (own_first, ["SDMA", "ROW"] + every("o2", "o") + every("b1", "y")), "TQ": (all_rows, every("o2", "s") + ["Y1"]),
+                  "OWN": (own_sum, ["OWN0", "TQ"]), "END": (own_end, ["OWN", "JB0", "JB1"]),
+                  "NEW": (lambda q: tt(B("gb", 0, NB), IND(B("xw", 0, P), B("sndu", 0, 42)), B("fr", 2 * FR, 2 * FR + NB), OP.max), ["END", "F1"]),
+                  "FIN": (last, ["NEW"] + ["N02"] * ("N02" in BACK["s"]))})
+    for w in ("JA0", "JB0", "JV0", "JW0"):
+        calls[w][1].extend(every("b1", "z"))
+    run(BACK, calls, None, {("b1", "g"): ["Y2"], ("b0", "g"): ["Y1"], ("b0", "e"): ["F0"], ("b0", "n"): ["JV0", "JV1"], ("b0", "a"): ["JV0", "JV1"]})
     totals.update(count)
     for s in sorted(totals):
         if known["g"].get(s, 0) < totals[s]:

from concourse.bass import DstId, RemoteDMATransfer
from concourse.mybir import AluOpType, ActivationFunctionType

P, BS, GB, NR = 4352, 768, 96, 8
NB = 7 * GB
W = P + NB
U = 512
DUM = 1024
FW = DUM + 4 * W
S0 = 1024
MAGIC = 12582912.0
FR = NB + 32
Z0 = 2 * U
INV, ER = 2048, 6400
CUT = 3 * GB
HALVES = ((0, CUT), (CUT, NB))
K = 65536.0
HI = 32768
ABSENT = 511 * HI


def _sb(n, d):
    return ("sbuf", [128, n], d)


_BF = {"xw": W, "Y": P + 2 * NB, "wV": FW, "L": 2048, "LT": 2048, "I": 128, "IK": 128, "H": 128, "Ds": 128, "DsC": 128, "BO": 128, "NU": 128, "ds": 192, "dT": 256, "s4": 4 * (NB - CUT),
       "ga": 8 * U, "mn": 8 * U, "id": 8 * U, "sm": 2 * U, "oz": Z0 + BS, "tlb": 1, "fr": 3 * FR, "sf": BS, "sb": NB, "gb": BS, "sdq": 272,
       "mq": 272, "yfo": 272, "F": 48, "cs": 48, "dd": 256, "be": 48, "Fo": 48, "M": NB, "D": 16}
_BF["CK"] = 192
ASIDE, DSG, SAMEQ, WVZ = 6, False, True, "g"
_BF["s4"] = 16
_F16 = {"E": U, "N1": 48, "iv": 2 * BS, "dk": 256, "A": 48}
_F32 = {"wS": S0 + FW, "I32": 128, "ts": 272, "invF": 96, "q1": 48, "q2": 48, "N769": 48, "N257": 48, "pf": 8, "tf": 8, "sc": 8, "t1": 256, "t2": 256}
_I32 = {"pk": 2 * BS, "pkw": 3 * BS + 8, "tb": 256, "sndi": 42, "pi": 8, "pj": 8, "sn": 42, "ar": 16}
_U16 = {"invT": 48, "sndu": 48, "P16": 48, "ou": 256, "rs": 48, "rr": 48, "cb1": 256}
for _s in range(3):
    _BF.update({"zc%d" % (_s % 2): 1088})
    _F16.update({"nx%d" % _s: 256, "xm%d" % _s: 256})
    _F32.update({"P32_%d" % _s: 48})
    _U16.update({"cu%d" % _s: 256, "yp%d" % _s: 48})
SCRATCH = {}
for _t, _d in ((_BF, "bfloat16"), (_F16, "float16"), (_F32, "float32"), (_I32, "int32"), (_U16, "uint16")):
    SCRATCH.update({_n: _sb(_c, _d) for _n, _c in _t.items()})
SCRATCH["rowd"] = ("dram", [8, P], "bfloat16")
PSUMS = {"ps": 4 * U, "pc0": U, "pc1": U, "pr0": U, "pr1": U}
for _n in PSUMS:
    SCRATCH[_n] = ("psum", [128, PSUMS[_n]], "float32")
NDMA = 44
EXCH = ["n", "m", "x", "f0", "f1", "f2", "y0", "y1", "y2"]
SEMAPHORES = ["sv", "sa", "st", "sg"] + ["d%d" % k for k in range(NDMA)] + ["r_" + e for e in EXCH] + ["l_" + e for e in EXCH]

def PD(a, b):
    return " ".join("p%d d%d" % (u, u) for u in range(a, b)) + " "


OV = "n01 n23 o01 g6 q01 n45 u01 n67 o2345 q2345 u2345 o67 s3 q67 s5 u67 s67 F0 F1"
J = "JA0 JA1 JB0 JW0 JB1 JW1 "
OUT = {"v": "LN LA LB LC g2 LD " + OV,
       "s": "g0 g1 g3 g4 g5 g7 s0 s1 s2 s4 SDMA K0 K1",
       "t": "p0 d0 LM " + PD(1, 4) + "c01 " + PD(4, 8) + "c2345 c67 PK " + J}
OUT0 = {"v": OV, "s": "g0 g1 g2 g3 g4 g5 g7 s0 s1 s2 s4 SDMA K0 K1",
        "t": "p0 p1 p2 p3 d0 d1 d2 d3 c01 " + PD(4, 8) + "c2345 c67 PK IV " + J}
BT = PD(4, 8) + "c012345 c67 e012345 e67 "
BV = "n01 m01 n23 m23 %s n45 m45 n67 m67 y012345 %s y67 z01234567 w01234567 "
BACK = {"v": "b2: LN LA LB LC g2 LD PLACES " + BV % ("", "") + "N21 T20 Y2 o2: n01 n23 o01 q01 u01 n45 n67 "
             "b1: g1 g3 o2: o2345 q2345 u2345 b1: " + BV % ("", "") + "N11 T10 Y1 o2: o67 s5 q67 u67 s67 TQ F0 b0: g1 g3 " + BV % ("END", "NEW") + "FIN",
        "s": "b2: g0 g1 g3 g4 g5 g6 g7 o2: g0 ROW g1 g2 g3 g4 N20 T21 g5 g6 g7 s0 "
             "b1: g0 g2 g4 g5 g6 g7 o2: s1 s23 N10 T11 s4 SDMA K0 K1 "
             "b0: g0 g2 g4 F1 g5 g6 g7 N02",
        "t": "b2: p0 d0 LM " + PD(1, 4) + BT + "o2: " + PD(0, 4) + "c01 " + PD(4, 8) + "c2345 b1: p0 p1 p2 p3 d0 d1 d2 d3 " + BT +
             "o2: c67 b0: p0 p1 p2 p3 " + J + "d0 d1 OWN0 d2 d3 p4 p5 OWN d4 d5 " + PD(6, 8) + "c012345 c67 e012345 e67"}


def exchange_plan(topo, cores, r, sg, short=False):
    src = cores[r]
    dst = [None] + [cores[(r + sg * d) % NR] for d in range(1, NR)]
    off = [d for d in range(1, NR) if topo.chip(dst[d]) != topo.chip(src)]
    eng = topo.engines(src, dst[off[0]])
    q = len(eng) // 4
    calls = []
    for k, ds in enumerate(([d for d in range(1, NR) if d not in off[2:]], off[2:]) if short else (range(1, 4), range(4, NR))):
        mine = [d for d in ds if d in off]
        sizes = {4: [q, q, q, q], 2: [2 * q, 2 * q], 3: [q, q, 2 * q] if k == 0 else [2 * q, q, q]}[len(mine)]
        call, at = [], 0
        for d, n in zip(mine, sizes):
            call.append((d, eng[at:at + n]))
            at += n
        for d in ds:
            if d not in off:
                call.append((d, [e for e in topo.engines(src, dst[d]) if e not in eng][:8]))
        calls.append(call)
    return calls


def rank_program(g, core, T, topo):
    rank = T.rank_of(core)
    if rank is None:
        return
    OP, AF = AluOpType, ActivationFunctionType
    cores = list(T.cores)
    eng = {"g": g, "vector": g.vector, "scalar": g.scalar, "tensor": g.tensor, "sync": g.sync}
    csem = {"vector": "sv", "scalar": "sa", "tensor": "st", "g": "sg"}
    count, totals, recs, ndma = {}, {}, {}, [0]
    known = {q: {} for q in eng}
    ROWS = slice(0, 128, 16)

    def B(name, lo=None, hi=None, st=1, parts=None):
        lo = 0 if lo is None else lo
        hi = SCRATCH[name][1][1] if hi is None else hi
        ap = T[name][:, lo:hi:st] if parts is None else T[name][parts, lo:hi:st]
        if name in PSUMS:
            lo, hi = lo // U * U, -(-hi // U) * U
        return {"ap": ap, "r": [(name, lo, hi)], "x": []}

    def IND(win, off):
        return {"ap": win["ap"].indirect(off["ap"]), "r": win["r"], "x": off["r"]}

    def HB(ap):
        return {"ap": ap, "r": [], "x": []}

    def need_of(q, reads, writes):
        need = []
        for acc, w in [(a, False) for a in reads] + [(a, True) for a in writes]:
            name, lo, hi = acc
            psum = name in PSUMS
            for rec in recs.get(name, []):
                if rec["hi"] <= lo or rec["lo"] >= hi:
                    continue
                if rec["q"] == q and (q == "tensor" or w and not SAMEQ and q in ("vector", "scalar")):
                    continue
                if w or rec["w"] or (psum and rec["q"] != q):
                    need.append(rec["tok"])
        return need

    def do_waits(q, need):
        kn = known[q]
        best = {}
        for tok in need:
            s = tok["sem"]
            if kn.get(s, 0) < tok["val"] and (s not in best or best[s]["val"] < tok["val"]):
                best[s] = tok
        for s in sorted(best):
            if any(o != s and best[o]["clk"].get(s, 0) >= best[s]["val"] for o in best):
                del best[s]
        for s in sorted(best):
            eng[q].wait_ge(T.sem[s], best[s]["val"])
            for a, b in best[s]["clk"].items():
                kn[a] = max(kn.get(a, 0), b)

    def record(q, tok, reads, writes):
        for name, lo, hi in writes:
            keep = [x for x in recs.get(name, []) if not (x["lo"] >= lo and x["hi"] <= hi)]
            recs[name] = keep + [{"lo": lo, "hi": hi, "w": True, "tok": tok, "q": q}]
        for name, lo, hi in reads:
            recs.setdefault(name, []).append({"lo": lo, "hi": hi, "w": False, "tok": tok, "q": q})

    def op(q, fn, outs, ins):
        reads = [a for o in ins for a in o["r"] + o["x"]] + [a for o in outs for a in o["x"]]
        writes = [a for o in outs for a in o["r"]]
        do_waits(q, need_of(q, reads, writes))
        s = csem[q]
        count[s] = count.get(s, 0) + 1
        fn(eng[q]).then_inc(T.sem[s], 1)
        clk = dict(known[q])
        clk[s] = count[s]
        record(q, {"sem": s, "val": count[s], "clk": clk}, reads, writes)

    def dma(q, out, in_, after=()):
        do_waits(q, need_of("dma", in_["r"], out["r"]) + list(after))
        s = "d%d" % ndma[0]
        ndma[0] += 1
        eng[q].dma_start(out["ap"], in_["ap"]).then_inc(T.sem[s], 16)
        clk = dict(known[q])
        clk[s] = totals[s] = 16
        record("dma", {"sem": s, "val": 16, "clk": clk}, in_["r"], out["r"])

    def send(name, src, land, at, sg=1, GB=GB, part=None):
        NB = 7 * GB
        ls, rs = "l_" + name, "r_" + name
        done, pend, clk = 0, [], {}
        plan = lambda q: exchange_plan(topo, cores, q, sg) if part is None else exchange_plan(topo, cores, q, sg, True)[part:part + 1]
        for call in plan(rank):
            tr, reads = [], []
            for d, es in call:
                to = cores[(rank + sg * d) % NR]
                rid, pid = topo.addr(to)[:2]
                lo = (d - 1) * GB
                reads.append((src, lo, lo + GB))
                tr.append(RemoteDMATransfer(dst_ids=[DstId(rid=rid, pnc=pid)], dma_engine_mask=sum(1 << e for e in es), remote_sem=T.sem[rs],
                                            src=T[src][:, lo:lo + GB], dst=T[land][:, at + lo:at + lo + GB]))
                done += len(es)
            do_waits("g", need_of("g", reads, []))
            g.remote_dma_fused(tr, local_sem=T.sem[ls])
            pend += reads
            clk = dict(known["g"])
        clk[ls] = totals[ls] = done
        record("g", {"sem": ls, "val": done, "clk": clk}, pend, [])
        n = sum(len(es) for q in range(NR) if q != rank for call in plan(q) for d, es in call if (q + sg * d) % NR == rank)
        totals[rs] = n
        rt = {"sem": rs, "val": n, "clk": {rs: n}}
        keep = [x for x in recs.get(land, []) if part or not (x["lo"] >= at and x["hi"] <= at + NB)]
        recs[land] = keep + [{"lo": at, "hi": at + NB, "w": True, "tok": rt, "q": "ext"}]
        return rt

    def copy(out, in_): op("vector", lambda e: e.tensor_copy(out["ap"], in_["ap"]), [out], [in_])
    def tt(out, a, b, o): op("vector", lambda e: e.tensor_tensor(out["ap"], a["ap"], b["ap"], o), [out], [a, b])
    def fill(out, v): op("vector", lambda e: e.memset(out["ap"], v), [out], [])

    def ts(out, a, s1, o1, s2=None, o2=None):
        col = isinstance(s1, dict)
        v1 = s1["ap"] if col else s1
        ins = [a, s1] if col else [a]
        if o2 is None:
            op("vector", lambda e: e.tensor_scalar(out["ap"], a["ap"], v1, None, o1), [out], ins)
        else:
            op("vector", lambda e: e.tensor_scalar(out["ap"], a["ap"], v1, s2, o1, o2), [out], ins)

    def scan(out, d0, d1, o0, o1, first=0.0):
        op("vector", lambda e: e.tensor_tensor_scan(out["ap"], d0["ap"], d1["ap"], first, o0, o1), [out], [d0, d1])

    def act(out, in_, f, **kw): op("scalar", lambda e: e.activation(out["ap"], in_["ap"], f, **kw), [out], [in_])

    def move(q, out, in_):
        if q == "v":
            copy(out, in_)
        else:
            act(out, in_, AF.Copy)

    def take(q, out, win, off):
        move(q, out, IND(win, off))

    def pe(mms):
        def run_all(e):
            for o, l, r, a, b in mms:
                k = e.matmul(o["ap"], l["ap"], r["ap"], a, b)
            return k
        outs, ins = {}, {}
        for o, l, r, a, b in mms:
            outs[o["r"][0]] = o
            ins[l["r"][0]] = l
            ins[r["r"][0]] = r
        op("tensor", run_all, list(outs.values()), list(ins.values()))

    def chain(out, pairs, first=True, last=True):
        n = len(pairs)
        return [(out, l, r, first and i == 0, last and i == n - 1) for i, (l, r) in enumerate(pairs)]

    def Lm(a, nm="L"):
        return B(nm, 128 * a, 128 * a + 128)

    def table(src, lo, n, nm="L"):
        return [(Lm(a, nm), B(src, lo + a, lo + n, 16)) for a in range(16)]

    def gsel(o, pat, cmp, base, cm, i=None):
        i = o if i is None else i
        op("g", lambda e: e.affine_select(o["ap"], i["ap"], pat, cmp, 0.0, base, cm), [o], [i])

    def giota(o, pat, base, cm):
        op("g", lambda e: e.iota(o["ap"], pat, base, cm, allow_small_or_imprecise_dtypes=True), [o], [])

    def sfill(o, v, src):
        act(o, src, AF.Copy, scale=0.0, bias=v)

    def marks_high(s):
        pe([(B("ps", 2 * U + a, 2 * U + b), B("IK"), B("xw", s * BS + a, s * BS + b), True, True) for a, b in ((0, U), (U, BS))])

    def pack(s):
        o = B("pk", s % 2 * BS, s % 2 * BS + BS)
        tt(o, o, B("ps", 2 * U, 2 * U + BS), OP.add)

    def numbers(lo, hi):
        ts(B("tb", lo, hi), B("pkw", 1 + lo, 1 + hi), HI - 1, OP.bitwise_and)

    def places_of(s, lo, hi):
        ts(B("cu%d" % s, lo, hi), B("tb", lo, hi), 0.25, OP.mult, -0.375, OP.add)

    def marks_of(s, h):
        ts(B("xm%d" % s, 128 * h, 128 * h + 128), B("pkw", 1 + 128 * h, 129 + 128 * h), 1.0 / HI, OP.mult, 1023.88, OP.add)

    def turned(s, h):
        pe(chain(B("pr%d" % h, 0, 128), [(B("oz", 0, 128), B("DsC")), (B("xm%d" % s, 128 * h, 128 * h + 128), B("Ds"))]))

    def scaled(s, h):
        ts(B("nx%d" % s, 128 * h, 128 * h + 128), B("pr%d" % h, 0, 128), -1.0, OP.mult)

    def positions(s):
        F = B("ga", 15, BS, 16) if s else B("F")
        scan(B("cs"), B("oz", Z0, Z0 + 48), F, OP.add, OP.subtract)
        tt(B("A"), F, B("N769"), OP.mult)
        pe(chain(B("pc0", 0, 48), [(B("I"), B("N1")), (B("NU"), F), (B("BO"), B("cs")), (B("I"), B("A"))]))
        copy(B("P16"), B("pc0", 0, 48))

    def members(s):
        if s:
            positions(s)
        copy(IND(B("pkw"), B("P16")), B("pk", s % 2 * BS, s % 2 * BS + BS))
        numbers(0, 64)
        marks_of(s, 0)
        places_of(s, 0, 64)
        turned(s, 0)
        copy(B("P32_%d" % s), B("pc0", 0, 48))

    def back_list():
        ts(B("t1"), B("tb"), 4.0 * P, OP.is_ge, -4.0 * W, OP.mult)
        tt(B("t2"), B("t1"), B("tb"), OP.add)
        ts(B("cb1"), B("t2"), 0.25, OP.mult, NB - 0.375, OP.add)

    def absent():
        giota(B("pkw", 1, 257), [[0, 256]], ABSENT, 0)

    def places(s):
        p = B("P32_%d" % s)
        ts(B("q1"), p, -256.0, OP.add, 4096.0, OP.mult)
        tt(B("q2"), B("q1"), p, OP.max)
        tt(B("q1"), B("q2"), B("N257"), OP.min)
        ts(B("yp%d" % s), B("q1"), -1.0, OP.add)

    turn, holder, slot, made, sized, signed, still = [0], {}, {}, set(), set(), set(), set()

    def aside(st, u):
        return st == "o2" and u >= ASIDE

    def ready(st, c, us):
        back, first = st[0] == "b", "a" if (st, us[0]) in sized else "n"
        if c == "g":
            return "", {("ga", u): ["d", "m"][:1 + back] for u in us}
        if c == "p":
            return "", {("ps", us[0] % 4): [first]}
        if c == "d":
            return "gp", {}
        if c == first:
            return "d", {} if aside(st, us[0]) else {("id", u): ["c"] for u in us}
        if c == "m":
            return "g", {("mn", u): ["e"] for u in us}
        if c == "c":
            return "n", {("pc", turn[0]): ["y" if back else "o"]}
        count = "r" if (st, us[0]) in still else "c"
        return {"n": "a", "h": "c", "r": "h", "o": count, "q": "o", "u": "o" if count == "r" else "q", "y": count, "s": "u", "e": "ym", "z": "e", "w": "z"}[c], {}

    def issue(st, q, c, us):
        s, back, u, n = int(st[1]), st[0] == "b", us[0], len(us)
        m0, m1 = 32 * u, 32 * (u + n)
        units = lambda buf, k=u: B(buf, U * k, U * (k + n))
        near = units("LT", u - 4) if aside(st, u) else units("id")
        at, mem = slot.get((st, u), 0), slice(0, min(32 * n, 128))
        bank, held = "pc%d" % at, B("dT", 128 * at, 128 * at + 128, 1, mem)
        cnt = lambda: B(bank, 128, 128 + 32 * n)
        if c == "g":
            win = B("xw") if not back else B("Y", 0, W) if s == 1 else B("Y", NB, NB + W)
            take(q, units("ga"), win, B("cb1" if st == "b1" else "cu%d" % s, m0, m1))
        elif c == "p":
            rows = slice(32 * (u % 4), 32 * (u % 4) + 32)
            pe([(units("ps", u % 4), B("nx%d" % s, 128 * (u // 4), 128 * (u // 4) + 128, parts=rows), B("E", parts=rows), True, False)])
        elif c == "d":
            pe([(units("ps", u % 4), B("Ds"), units("ga"), False, True)])
        elif c == "a":
            act(near, units("ps", u % 4), AF.Abs)
        elif c == "n" and q == "s":
            act(near, near, AF.Sign, scale=-1.0, bias=0.499)
        elif c == "n" and (st, u) in sized:
            ts(near, near, 0.5, OP.is_lt)
        elif c == "n":
            ts(near, units("ps", u % 4), MAGIC, OP.add, MAGIC, OP.is_equal)
        elif c == "c" and (st, u) in still:
            buf, lo, hi = near["r"][0]
            pe([(B(bank, a, 128, 16, mem), B(buf, lo + a, hi, 16), B("BO", 0, 128, 16), True, True) for a in range(16)])
        elif c == "c":
            pe(chain(cnt(), ([] if back else [(B("I"), B("CK", 0, 32 * n))]) + table(*near["r"][0][:2], U * n)))
        elif c == "h" and q == "v":
            ts(held, B(bank, 0, 128, 1, mem), 9.5, OP.is_ge)
        elif c == "h":
            act(held, B(bank, 0, 128, 1, mem), AF.Relu, bias=-9.0)
        elif c == "r":
            pe(chain(cnt(), ([] if back else [(B("I"), B("dk", m0, m1))]) + [(held, B("IK", 0, 32 * n, 1, mem))]))
        elif c == "m":
            scan(units("mn"), B("sm", 0, U * n), units("ga"), OP.max, OP.min)
        elif c == "o":
            tt(B("t1", m0, m1), cnt(), B("tb", m0, m1), OP.min)
        elif c == "q":
            tt(B("t1", m0, m1), B("t1", m0, m1), B("dk", m0, m1), OP.max)
        elif c == "u":
            ts(B("ou", m0, m1), B("t1", m0, m1), float(DUM), OP.add)
        elif c == "s" and q == "v":
            copy(IND(B("wV"), B("ou", m0, m1)), B("oz", 0, U * n))
        elif c == "s":
            assert "SDMA" not in made
            act(IND(B("wS", S0), B("ou", m0, m1)), B("wS", 0, U * n), AF.Silu)
        elif c == "y":
            ts(B("dd", m0, m1), cnt(), 0.5 if (st, u) in still else K * (3.0 if (st, u) in signed else 9.5), OP.is_gt, 255.0, OP.mult)
        elif c == "e":
            pe(chain(B("pr0", m0, m1), [(B("H"), B("xm%d" % s, m0, m1)), (B("H"), B("mn", U * u + 15, U * (u + n), 16)), (B("BO"), B("dd", m0, m1))]))
        elif c == "z":
            ts(B("t2", m0, m1), B("pr0", m0, m1), -512.25, OP.add, MAGIC, OP.add)
        elif c == "w":
            ts(B("zc%d" % (s % 2), m0, m1), B("t2", m0, m1), MAGIC, OP.subtract, 255.0, OP.min)

    def run(lists, own, st=None, behind={}):
        todo = {q: [] for q in "vst"}
        for q in lists:
            for w in lists[q].split():
                if w[-1] == ":":
                    st = w[:-1]
                    continue
                us = () if w[0].isupper() else tuple(int(k) for k in w[1:])
                todo[q].append((st, w if not us else w[0], us))
                sized.update((st, u) for u in us if w[0] == "a")
                signed.update((st, u) for u in us if w[0] == "n" and q == "s")
                still.update((st, u) for u in us if w[0] == "h")
        names = {c for q in todo for st, c, us in todo[q] if not us}
        while any(todo.values()):
            moved = False
            for q in "svt":
                while todo[q]:
                    st, c, us = todo[q][0]
                    if not us:
                        if not all(b in made for b in own[c][1]):
                            break
                        own[c][0](q)
                        made.add(c)
                    else:
                        before, takes = ready(st, c, us)
                        first = [{"p": "LA" if us[0] < 4 else "LD", "g": "LB" if us[-1] > 1 else ""}.get(c)] + behind.get((st, c), [])
                        if any(w in names and w not in made for w in first) or not all((st, b, u) in made for b in before for u in us):
                            break
                        if not all(x in made for k in takes for x in holder.get(k, [])):
                            break
                        for k, after in takes.items():
                            holder[k] = [(st, b, k[1] if k[0] in ("ga", "id", "mn") else us[0]) for b in after]
                            if k[0] == "pc":
                                slot[(st, us[0])] = turn[0]
                                turn[0] = 1 - turn[0]
                        issue(st, q, c, us)
                        made.update((st, c, u) for u in us)
                    todo[q].pop(0)
                    moved = True
            assert moved, todo
        made.difference_update(own)

    def s_rows(s):
        o = S0 + DUM + 4 * BS * (s + 1)
        if DSG:
            dma("g", B("ds"), B("wS", o, o + 4 * BS, parts=ROWS))
        else:
            dma("sync", B("ts", 0, 192), B("wS", o, o + 4 * BS, parts=ROWS))

    def out_calls(s, lists={}):
        o = S0 + DUM + 4 * P
        parts, buf = [0, 0], "mn" if s < 2 else "xw"
        sums_of = [[w for w in lists.get("t", "").split() if w[0] == "J" and w[2] == str(h)] for h in range(2)]

        def narrow(q, h):
            a, b = HALVES[h]
            if "JA%d" % h in sums_of[h]:
                for k in range(3):
                    move(q, B(buf, 1024 * k + a, 1024 * k + b), B("wS", o + 4 * a + k, o + 4 * b, 4))
            else:
                move(q, B(buf, 4 * a, 4 * b), B("wS", o + 4 * a, o + 4 * b))

        def stubs_of(h):
            a, b = HALVES[h]
            scan(B("id", 4 * a, 4 * b), B("s4", 0, 4 * (b - a)), B("wV", DUM + 4 * (P + a), DUM + 4 * (P + b)), OP.mult, OP.max)

        def add(h, src, ks, at=0, by="I"):
            a, b = HALVES[h]
            parts[h] += 1
            cols = lambda k: B(src, 1024 * k + a, 1024 * k + b) if len(ks) == 3 else B(src, at + 4 * a + k, at + 4 * b, 4)
            pe(chain(B("pr%d" % h, 0, b - a), [(B(by), cols(k)) for k in ks], parts[h] == 1, parts[h] == len(sums_of[h])))

        def flags_out(q, h):
            a, b = HALVES[h]
            out, sums = B("sf", a, b), B("pr%d" % h, 0, b - a)
            if s < 2:
                tt(out, sums, B("M", a, b), OP.min)
            elif q == "v":
                ts(out, sums, 0.5, OP.is_gt)
            else:
                act(out, sums, AF.Sign)
            if h:
                send("f%d" % s, "sf", "fr", FR * s, -1)
        stubs = {}
        for h in range(2):
            stubs.update({"K%d" % h: (lambda q, h=h: narrow(q, h), ["SDMA"]), "JB%d" % h: (lambda q, h=h: add(h, buf, range(3 if "JA%d" % h in sums_of[h] else 4)), ["K%d" % h]),
                          "JA%d" % h: (lambda q, h=h: add(h, "wS", [3], o, "I32"), ["SDMA"]),
                          "JW%d" % h: (lambda q, h=h: add(h, "wV", range(4), DUM + 4 * P), [("o%d" % s, "s", u) for u in range(8)]),
                          "R%d" % h: (lambda q, h=h: stubs_of(h), [("o%d" % s, "s", u) for u in range(8)] + [("b1", "c", u) for u in range(8 * (s // 2))]),
                          "JV%d" % h: (lambda q, h=h: add(h, "id", [3]), ["R%d" % h]),
                          "F%d" % h: (lambda q, h=h: flags_out(q, h), sums_of[h] + ["F0"][:h])})
        return {**stubs, "PK": (lambda q: marks_high(s + 1), [("o%d" % s, "n", u) for u in range(8)]),
                "IV": (lambda q: pe(chain(B("ps", 0, 96), table("iv", 0, 2 * BS))), [("o%d" % s, "n", u) for u in range(8)]), "LA": (lambda q: scaled(s, 0), []), "LN": (lambda q: numbers(64, 256), []), "LB": (lambda q: places_of(s, 64, 256), ["LN"]), "LC": (lambda q: marks_of(s, 1), []),
                "LM": (lambda q: turned(s, 1), ["LC"]), "LD": (lambda q: scaled(s, 1), ["LM"]),
                "SDMA": (lambda q: s_rows(s), []), "PLACES": (lambda q: places(s), []),
                "MASK": (lambda q: take(q, B("M"), B("D"), B("rr", 0, 42)), [])}

    def own_flags(t):
        o = DUM + 4 * BS * t
        dma("sync", B("dd", 0, 192), B("wV", o, o + 4 * BS, parts=ROWS))
        pe(chain(B("pc0", 0, 48), [(B("I"), B("ds", k, 192, 4)) if DSG else (B("I32"), B("ts", k, 192, 4)) for k in range(4)], last=False))
        pe(chain(B("pc0", 0, 48), [(B("I"), B("dd", k, 192, 4)) for k in range(4)], first=False))

    def own_runs():
        move("s", B("be"), B("pc0", 0, 48))
        pe([(B("ps", U * (a // 8) + 48 * (a % 8), U * (a // 8) + 48 * (a % 8) + 48), Lm(a, "LT"), B("be"), True, True) for a in range(16)])

    def own_table():
        own_runs()
        for h in range(2):
            move("sv"[h], B("mn", 384 * h, 384 * h + 384), B("ps", U * h, U * h + 384))
        pe(chain(B("pc1", 0, 48), table("mn", 0, BS)))

    def unflagged(out):
        ts(B(out), B("pc1", 0, 48), 0.5, OP.is_lt)

    def flags_in(s):
        tt(B("q2"), B("pc1", 0, 48), B("invF", 48 * s, 48 * s + 48), OP.max)
        ts(B("invT"), B("q2"), B("pf", 2, 3), OP.min)
        win = B("fr", FR * s, FR * s + FR)
        act(B("gb", 0, 384), IND(win, B("invT", 0, 24)), AF.Copy, scale=-1.0, bias=1.0)
        ts(B("gb", 384, BS), IND(win, B("invT", 24, 48)), -1.0, OP.mult, 1.0, OP.add)
        scan(B("ga", 0, BS), B("sm", 0, BS), B("gb"), OP.add, OP.min)

    def stand(q, s, h):
        lo, n = (BS * s + 384 * h, 384) if h < 2 else (BS * s, BS)
        take(q, B("Y", NB + lo, NB + lo + n), B("zc%d" % (s % 2), 0, 1024), B("yp%d" % s, 24 * (h % 2), 24 * (h % 2) + n // 16))
        if s == 0:
            dma("scalar" if q == "s" and h < 2 else "sync", HB(T.yv[:, lo:lo + n]), B("Y", NB + lo, NB + lo + n))

    def old(s):
        dma("sync", B("zc%d" % (s % 2), 256, 1024), HB(T.y0[:, s * BS:s * BS + BS]))

    def member_row(s, buf, lo):
        take("s", B(buf, lo, lo + BS), B("oz", Z0 - 256, Z0 + BS), B("yp%d" % s))
        dma("sync", B("rowd", s * BS, s * BS + BS), B(buf, lo, lo + BS, parts=ROWS))

    def border_take(q, win, h):
        a, b = HALVES[h]
        take(q, B("sb", a, b), B("xw", 0, P) if win == "xw" else B("Y", NB, W), B("sndu", a // 16, b // 16))

    dma("sync", B("sndi"), HB(T.snd[:, :]))
    dma("sync", B("xw", 0, P), HB(T.x[:, :]))
    dma("sync", B("pk", 0, BS), HB(T.cd[:, 0:BS]))
    dma("scalar", B("tlb"), HB(T.tl[:, :]))
    fill(B("gb"), 0.0)
    dma("scalar", B("gb", parts=ROWS), HB(T.sd[:, :]))
    giota(B("id", 0, 128), [[-32, 8], [0, 16]], -15, 2)
    giota(B("id", 128, 256), [[1, 128]], 0, -1)
    giota(B("pi"), [[0, 8]], 0, 1)
    giota(B("N257"), [[16, 48]], 257, 0)
    giota(B("ar"), [[1, 16]], 0, 0)
    fill(B("L"), 0.0)
    ts(B("BO"), B("id", 0, 128), 32 * MAGIC, OP.add, 32 * MAGIC, OP.is_equal)
    ts(B("sn"), B("sndi"), 15, OP.bitwise_and)
    ts(B("I"), B("id", 128, 256), 0.0, OP.is_equal)
    copy(B("rs", 0, 42), B("sn"))
    send("n", "rs", "rr", 0, 1, GB // 16)
    for a in range(16):
        act(B("L", 128 * a + a, 128 * a + 128, 16), B("BO", a, 128, 16), AF.Copy, scale=K)
    ts(B("pj", 0, 1), B("pi", 0, 1), 15, OP.bitwise_and)
    ts(B("pj", 1, 2), B("pi", 0, 1), 31, OP.bitwise_and)
    ts(B("H"), B("id", 128, 256), 0.0, OP.is_lt)
    copy(B("sndu", 0, 42), B("sndi"))
    copy(B("pf", 0, 2), B("pj", 0, 2))
    tt(B("NU"), B("H"), B("BO"), OP.mult)
    ts(B("tf", 0, 1), B("tlb"), 2.0, OP.mult, 1.0, OP.add)
    ts(B("N257"), B("N257"), B("pf", 0, 1), OP.add)
    fill(B("oz", Z0), 0.0)
    op("vector", lambda e: e.reciprocal(T.sc[:, 0:1], T.tf[:, 0:1]), [B("sc", 0, 1)], [B("tf", 0, 1)])
    fill(B("oz", 0, Z0), 1.0)
    ts(B("IK"), B("I"), float(HI), OP.mult)
    ts(B("N769"), B("N257"), 512.0, OP.add)
    ts(B("N1"), B("N257"), -256.0, OP.add)
    ts(B("D"), B("ar"), B("pf", 0, 1), OP.is_equal)
    ts(B("Ds"), B("I"), B("sc", 0, 1), OP.mult)
    scan(B("wS", ER, ER + NB), B("oz", 0, NB), B("oz", Z0, Z0 + NB), OP.add, OP.add, 63.0)
    sfill(B("wS", INV + BS, INV + 3 * BS), 64.0 + NB, B("L", 0, 2 * BS))
    pe(chain(B("pc1", 0, 48), table("gb", 0, BS)))
    marks_high(0)
    for h in range(2):
        border_take("vs"[h], "xw", h)
    rx = send("x", "sb", "xw", P)
    giota(B("id", 0, U), [[1, 32], [0, 16]], 0, 0)
    giota(B("t1"), [[0, 4], [16, 64]], -DUM, 0)
    giota(B("wS", S0 + DUM + 4 * P), [[0, 4 * NB]], 0, 0)
    act(IND(B("wS", INV, INV + P), B("sndu", 0, 42)), B("wS", ER, ER + NB), AF.Silu)
    take("s", B("M"), B("D"), B("rr", 0, 42))
    sfill(B("wS", 0, 2 * U), 4.0, B("L", 0, 2 * U))
    unflagged("F")
    fill(B("pkw", 1, 257), ABSENT)
    positions(0)
    pack(0)
    ts(B("DsC"), B("Ds"), -1024.0, OP.mult)
    members(0)
    run({"v": "LN LC LB LA LD", "t": "LM"}, out_calls(0))
    ts(B("E"), B("id", 0, U), B("pf", 1, 2), OP.is_equal)
    fill(B("ts"), 0.0)
    copy(B("iv"), B("wS", INV + BS, INV + 3 * BS))
    ts(B("dk"), B("t1"), B("pf", 0, 1), OP.add)
    fill(B("CK"), -9.5 * K)
    ts(B("pf", 2, 3), B("pf", 0, 1), NB + 16.0, OP.add)
    if WVZ == "v":
        fill(B("wV", DUM + 4 * P), 0.0)
    for k in (3, 2, 1, 0):
        dma("sync", B("wS", S0 + DUM + P * k, S0 + DUM + P * k + P, parts=ROWS), B("ts"), after=[rx])
    dma("sync", B("wV", DUM, DUM + 16 * BS, parts=ROWS), B("oz", Z0))
    dma("sync", B("wV", DUM + 16 * BS, DUM + 4 * P, parts=ROWS), B("oz", Z0, Z0 + 320))
    dma("sync", B("pk", BS, 2 * BS), HB(T.cd[:, BS:2 * BS]))
    dma("sync", B("Y", NB, W), HB(T.y0[:, :]))
    dma("sync", B("pk", 0, BS), HB(T.cd[:, 2 * BS:3 * BS]))
    for s in (2, 1):
        old(s)
    if WVZ == "g":
        giota(B("wV", DUM + 4 * P), [[0, 4 * NB]], 0, 0)
    gsel(B("I32"), [[-1, 128]], OP.is_equal, 0, 1, B("wS", 0, 128))
    if "R0" in OUT["v"] + BACK["v"]:
        giota(B("s4"), [[0, NB - CUT], [1, 4]], 0, 0)
    for h in range(2):
        gsel(B("LT", 1024 * h, 1024 * h + 1024), [[-1, 8], [-16, 8], [0, 16]], OP.is_equal, -8 * h, 1, B("oz", 0, 1024))
    for s in range(2):
        giota(B("fr", FR * s + NB, FR * s + NB + 16), [[0, 16]], 0, 0)
        gsel(B("fr", FR * s + NB + 16, FR * s + FR), [[0, 16]], OP.is_equal, 0, 0, B("D"))
    dma("sync", B("rowd", 3 * BS, P), B("oz", Z0, Z0 + 128))
    run(OUT0, out_calls(0, OUT0), "o0")
    ts(B("invF"), B("ps", 0, 96), 0.0625 / K, OP.mult, -64.0, OP.add)
    own_flags(1)
    take("s", B("sb"), B("Y", NB, W), B("sndu", 0, 42))
    fill(B("sm"), 0.0)
    pack(1)
    fill(B("sm", 0, 2 * U, 16), 191.0)
    absent()
    own_table()
    places(0)
    flags_in(0)
    do_waits("g", need_of("g", [("fr", 0, NB)], []))
    send("y0", "sb", "Y", W)
    giota(B("sdq"), [[0, 272]], 0, 0)
    act(B("H"), B("I"), AF.Copy, scale=0.5)
    members(1)
    for q in range(3):
        n = 272 if q < 2 else 224
        dma("sync", B("sdq", 0, n, parts=slice(q, 128, 16)), HB(T.sd[:, 272 * q:272 * q + n]), after=need_of("dma", [("P16", 0, 48)], []))
    run(OUT, out_calls(1, OUT), "o1")
    own_flags(2)
    member_row(0, "id", 0)
    pack(2)
    absent()
    back_list()
    own_table()
    places(1)
    flags_in(1)
    member_row(1, "sf", 0)
    members(2)

    every = lambda st, c: [(st, c, u) for u in range(8)]
    sent = {}

    def standings_out(s):
        sent[s] = send("y%d" % (3 - s), "sb", "Y", (2 - s) * W)
        if s == 2:
            dma("sync", HB(T.yv[:, 2 * BS:3 * BS]), B("Y", NB + 2 * BS, NB + 3 * BS), after=[sent[s]])
            old(0)
    acc = []

    def all_rows(q):
        dma("sync", B("zc1", 0, 1088), B("wV", DUM, DUM + 4 * P, parts=ROWS))
        dma("sync", HB(T.yv[:, BS:2 * BS]), B("Y", NB + BS, NB + 2 * BS), after=[sent[1]])

    def own_first(q):
        acc.append(B("pc%d" % turn[0], 0, 272))
        holder[("pc", turn[0])] = ["END"]
        pe(chain(acc[0], [(B("I"), B("sdq")), (B("I"), B("mq"))] + [(B("I"), B("fr", k, 1088, 4)) for k in range(4)], last=False))

    def own_sum(q):
        pe(chain(acc[0], [(B("I"), B("zc1", k, 1088, 4)) for k in range(4)], first=False))

    def own_end(q):
        ts(B("yfo"), acc[0], 0.5, OP.is_gt)
        tt(B("yfo"), B("yfo"), B("mq"), OP.add)
        dma("sync", B("xw", 0, P, parts=ROWS), B("yfo"))

    def last(q):
        copy(IND(B("xw", 0, P), B("sndu", 0, 42)), B("gb", 0, NB))
        dma("sync", HB(T.yf[:, :]), B("xw", 0, P, parts=ROWS))
    calls = out_calls(2, BACK)
    for s in range(3):
        for h in range(2):
            calls["N%d%d" % (s, h)] = (lambda q, s=s, h=h: stand(q, s, h), every("b%d" % s, "w") + ["PLACES"])
            calls["T%d%d" % (s, h)] = (lambda q, h=h: border_take(q, "Y", h), ["N%d0" % s, "N%d1" % s])
        calls["N%d2" % s] = (lambda q, s=s: stand(q, s, 2), every("b%d" % s, "w"))
        calls["Y%d" % s] = (lambda q, s=s: standings_out(s), ["T%d0" % s, "T%d1" % s])
    calls.update({"ROW": (lambda q: (member_row(2, "gb", 0), dma("sync", B("mq"), B("rowd"))), ["PLACES"]),
                  "SDMA": (lambda q: dma("g", B("fr", 0, 1088), B("wS", S0 + DUM, S0 + DUM + 4 * P, parts=ROWS)), ["Y1"]),
                  "OWN0": (own_first, ["SDMA", "ROW"] + every("o2", "o") + every("b1", "y")), "TQ": (all_rows, every("o2", "s") + ["Y1"]),
                  "OWN": (own_sum, ["OWN0", "TQ"]), "END": (own_end, ["OWN", "JB0", "JB1"]),
                  "NEW": (lambda q: tt(B("gb", 0, NB), IND(B("xw", 0, P), B("sndu", 0, 42)), B("fr", 2 * FR, 2 * FR + NB), OP.max), ["END", "F1"]),
                  "FIN": (last, ["NEW"] + ["N02"] * ("N02" in BACK["s"]))})
    for w in ("JA0", "JB0", "JV0", "JW0"):
        calls[w][1].extend(every("b1", "z"))
    run(BACK, calls, None, {("b1", "g"): ["Y2"], ("b0", "g"): ["Y1"], ("b0", "e"): ["F0"], ("b0", "n"): ["JV0", "JV1"], ("b0", "a"): ["JV0", "JV1"]})
    totals.update(count)
    for s in sorted(totals):
        if known["g"].get(s, 0) < totals[s]:
            g.wait_ge(T.sem[s], totals[s])
